import numpy as np, ml_dtypes
CORES = [23,119,17,113]
N = 4
BF = ml_dtypes.bfloat16
V, L, K, RO, KM = 4096, 256, 16, 4, 3967
B = L // N
WT = np.array([1, 7, 2, 6, 3, 5, 4, 4, 5, 3, 6, 2, 7, 1, 8, 1], np.int64)
def mix(v):
    return np.add.reduce(v * WT[:, None], axis=-2)
def spots(u, kap, a):
    return ((u * u >> 5)[..., None, :] + kap[..., None] * u[..., None, :] + a[..., None, None]) & (V - 1)
def first(x, z, kap, a=0):
    h = spots(mix(z), kap, np.asarray(a, np.int64)); e = np.add.reduce(np.abs(x[:, h] - z[:, None, :]), axis=0); m = np.argmin(e, axis=0)[None]
    return np.take_along_axis(h, m, 0)[0], np.take_along_axis(e, m, 0)[0]
def back(x, t, s):
    node = t[np.maximum(np.argsort(t)[s] - 1 - (1 + (mix(x[:, s]) & 15)) * np.arange(K)[:, None], 0)]
    e = np.add.reduce(np.abs(x[:, node] - x[:, None, s]), axis=0)
    return np.take_along_axis(node, np.argmin(e, axis=0)[None], 0)[0]
def far(rng):
    q = int(rng.integers(80, 113)); a = q // 2 + rng.integers(-7, 8, (8, L)); z = np.concatenate([a, q - a]); z[0] -= rng.integers(0, 4, L)
    return rng.integers(0, 8, (16, V)), z
def apart(rng, kap):
    z = rng.integers(2, 62, (16, L)); z[0] ^= 1 - (mix(z) & 1)
    h = spots(mix(z), kap, np.zeros((), np.int64)); used = np.zeros(V, bool); s = np.zeros(L, np.int64)
    for l in range(L):
        c = h[:, l]; s[l] = c[int(np.argmin(used[c]))]; used[s[l]] = True
    us, i = np.unique(s, return_index=True); k = len(us); rest = rng.permutation(np.flatnonzero(~used)); n = rest[:k]; rest = rest[k:]
    x = rng.integers(0, 64, (16, V)); x[:, us] = z[:, i] + rng.integers(-1, 2, (16, k)); x[:, n] = z[:, i] + 4 * rng.integers(0, 2, (16, k)) - 2
    o = rng.permutation(k); j = int(rng.integers(0, len(rest) // 2)); two = np.stack([n[o], us[o]], axis=1).reshape(-1)
    return x, z, np.concatenate([rest[:j], two, rest[j:]])
def parts(rng):
    x = rng.integers(0, 64, (N, 8, 16, V)); z = rng.integers(0, 64, (N, 8, 16, L)); ts = np.argsort(rng.random((N, 8, V)), axis=-1)
    return x, z, ts, rng.integers(0, KM + 1, (N, 8, 16)), rng.integers(20, 261, (N, 8))
def pack(x, z, ts, kap, th):
    return {"xr": np.ascontiguousarray(x.reshape(N, 128, V)).astype(np.float32).astype(BF), "ts": np.ascontiguousarray(ts).astype(np.int32), "zq": np.ascontiguousarray(z.reshape(N, 128, L)).astype(np.float32).astype(BF),
            "kap": np.ascontiguousarray(kap.reshape(N, 128, 1)).astype(np.int32), "th": np.ascontiguousarray(th.reshape(N, 8, 1)).astype(np.int32)}
def plant(rng, x, z, kap):
    h = spots(mix(z), kap, np.zeros((N, 8), np.int64)); m = rng.integers(0, 16, (N, 8, 1, L)); h = np.take_along_axis(h, m, 2)[:, :, 0]
    for r in range(N):
        for g in range(8):
            w = np.flatnonzero(rng.random(L) < rng.choice(np.array([0.2, 0.4, 0.6]))); c = int(rng.integers(2, 14))
            x[r, g][:, h[r, g, w]] = np.clip(z[r, g][:, w] + rng.integers(-c, c + 1, (16, len(w))), 0, 63)
def setup_inputs(rng):
    x, z, ts, kap, th = parts(rng)
    src = np.where(rng.random((N, 8, L)) < 0.12, rng.integers(0, L, (N, 8, L)), np.arange(L))
    z = np.take_along_axis(z, src[:, :, None, :], 3)
    plant(rng, x, z, kap)
    return pack(x, z, ts, kap, th)
def setup_inputs_corners(rng):
    x, z, ts, kap, th = parts(rng)
    for r in range(N):
        for g in range(8):
            y = (g + r) & 7
            if y == 0 and r & 1:
                x[r, g], z[r, g] = far(rng); X, Z = x[r, g], z[r, g]; s, e = first(X, Z, kap[r, g])
                v = np.abs(Z - X[:, back(X, ts[r, g], s)])[:, r * B:r * B + B]; e2 = first(X, v, kap[r, g], L)[1]
                th[r, g] = max(0, min(int(e2[int(rng.integers(0, B))]) - L, int(np.min(e)) - 1))
            elif y < 2:
                x[r, g, 0] &= 62; z[r, g, 0] |= 1; th[r, g] = 0
                if y == 1:
                    l = (0, L - 1)[int(rng.integers(0, 2))]; h = spots(mix(z[r, g]), kap[r, g], np.zeros((), np.int64))
                    x[r, g][:, h[int(rng.integers(0, 16)), l]] = z[r, g][:, l]
            elif y == 2: x[r, g], z[r, g], ts[r, g] = apart(rng, kap[r, g]); th[r, g] = 1008
            elif y == 3 and r & 1:
                x[r, g], z[r, g] = far(rng); c = np.bincount(first(x[r, g], z[r, g], kap[r, g])[1], minlength=1010)
                o = np.arange(513 + (r & 2), 1008, 4); th[r, g] = o[int(np.argmax(np.minimum(c[o], c[o + 1])))]
            elif y == 3: th[r, g] = np.sort(first(x[r, g], z[r, g], kap[r, g])[1])[L // 2]
            elif y < 6:
                us = rng.permutation(np.unique(first(x[r, g], z[r, g], kap[r, g])[0])); rest = rng.permutation(np.setdiff1d(np.arange(V), us))
                ts[r, g] = np.concatenate([us, rest] if y == 4 else [rest, us]); th[r, g] = 1008 if y == 4 else 600
            elif y == 6:
                x[r, g, 0] = 0; t = 15 * rng.integers(0, 2, V); x[r, g, 0] = ((t - mix(x[r, g])) & 15) + 16 * rng.integers(0, 4, V)
            else:
                pat = rng.integers(0, 64, (16, 3)); x[r, g] = pat[:, rng.integers(0, 3, V)]; z[r, g] = 63 * rng.integers(0, 2, (1, L)); z[r, g][:, L - 1] = 0; z[r, g][:, 0] = 63
    return pack(x, z, ts, kap, th)
def setup_inputs_crowd(rng):
    x, z, ts, kap, th = parts(rng); zero = np.zeros((), np.int64)
    for r in range(N):
        for g in range(8):
            X, Z = x[r, g], z[r, g]
            if g < 3:
                b = rng.integers(0, 16, 16); v = np.repeat(b[:, None], L, axis=1)
                for i, j in ((0, 13), (1, 12), (2, 11), (3, 10), (4, 9), (5, 8), (6, 7)):
                    fl = rng.random(L) < 0.5; v[i] = np.where(fl, b[j], b[i]); v[j] = np.where(fl, b[i], b[j])
                h = spots(mix(v), kap[r, g], zero)[:, 0]; X[:, h] = rng.integers(40, 64, (16, 16))
                X[:, h[int(rng.integers(0, 16))]] = np.clip(b + rng.integers(-2, 3, 16), 0, 63)
                odd = Z[:, 0].copy(); Z[:] = v; th[r, g] = (1008, 700, 350)[(g + r) % 3]
                if g == 1: Z[:, L - 1] = odd
                if g == 2: Z[:, 0] = odd
            elif g < 5:
                b = rng.integers(16, 44, 16); zi = b[:, None] + rng.integers(-2, 3, (16, 8)); hs = spots(mix(zi), kap[r, g], zero)[int(rng.integers(0, 16))]
                v = zi + rng.integers(-3, 4, (16, 8)); v[0] = v[0] + ((15 - mix(v)) & 15); X[:, hs] = v
                us = rng.permutation(np.unique(hs)); rest = rng.permutation(np.setdiff1d(np.arange(V), us)); a = rest[0]; X[:, a] = b
                at = 2 * np.arange(1, len(us) + 1); free = np.ones(V, bool); free[at] = False; free[0] = False
                ts[r, g, 0] = a; ts[r, g, at] = us; ts[r, g, free] = rest[1:]
                odd = Z[:, 0].copy(); Z[:] = zi[:, np.arange(L) & 7]; th[r, g] = (1008, 200)[(g + r) & 1]
                if g == 4: Z[:, 0] = odd
            elif g < 7:
                X[0] &= 62; Z[0] |= 1; th[r, g] = 0; odd = Z[:, L - 1].copy(); Z[:] = Z[:, :1].copy()
                if g == 6:
                    Z[:, L - 1] = odd; X[:, spots(mix(Z), kap[r, g], zero)[int(rng.integers(0, 16)), L - 1]] = odd
            else: Z[:] = Z[:, rng.integers(0, 4, L)].copy(); th[r, g] = 500
    return pack(x, z, ts, kap, th)
def setup_inputs_ends(rng):
    x, z, ts, kap, th = parts(rng); sh = np.array([1.0, 0.0, 0.5, 0.5, 0.9, 0.1, 0.5, 0.5]).reshape(1, 8, 1, 1)
    x = 63 * np.where(rng.random((N, 8, 1, V)) < sh, rng.integers(0, 2, (N, 8, 1, V)), rng.integers(0, 2, (N, 8, 16, V)))
    z = 63 * np.where(rng.random((N, 8, 1, L)) < sh, rng.integers(0, 2, (N, 8, 1, L)), rng.integers(0, 2, (N, 8, 16, L)))
    z[..., 0] = 63; z[..., 1] = 0; z[..., L - 2] = 0; z[..., L - 1] = 63
    kap = KM * rng.integers(0, 2, (N, 8, 16)); kap[..., 13] = 0; kap[..., 14] = KM; kap[..., 15] = 3841
    th = 1008 * rng.integers(0, 2, (N, 8)); th[:, 6] = 0; th[:, 7] = 1008
    c = (4095 * 4095 >> 5) & (V - 1); cs = np.array([c, (c + KM * 4095) & (V - 1), V - 1])
    for r in range(N):
        for g in range(8):
            y = (g + r) & 3; X = x[r, g]; X[:, cs] = (0, 63, 0, 0)[y]
            if y == 1: kap[r, g, 0] = 3841
            if y == 0: ts[r, g] = np.arange(V); X[:, V - 1] = 63
            elif y == 2: ts[r, g] = np.arange(V)[::-1]; X[:, 0] = 63
            else:
                i = int(np.flatnonzero(ts[r, g] == V - 1)[0]); j = V - 1 if y == 1 else 0; t = int(ts[r, g, j]); ts[r, g, j] = V - 1; ts[r, g, i] = t; X[:, V - 1] = 63
            if y < 2: X[:, ts[r, g, V - 2 - 16 * np.arange(K)]] = 63 * y
    X = x[N - 1, 1]; X[:] = np.where(rng.random((1, V)) < 0.1, 63 * rng.integers(0, 2, (16, V)), 0); X[0] = 0; X[:, cs] = 0
    z[N - 1, 1, 0] = 63; th[N - 1, 1] = 0
    return pack(x, z, ts, kap, th)
def setup_inputs_spread(rng):
    x, z, ts, kap, th = parts(rng)
    def odd(n):
        v = np.minimum((np.exp2(6 * rng.random((N, 8, 1, n))) * rng.random((N, 8, 16, n))).astype(np.int64), 63)
        return np.where(rng.random((N, 8, 1, n)) < 0.4, 63 - v, v)
    kap = np.minimum(np.exp2(12 * rng.random((N, 8, 16))).astype(np.int64) - 1, KM); th = np.minimum(np.exp2(10 * rng.random((N, 8))).astype(np.int64) - 1, 1008)
    return pack(odd(V), odd(L), ts, kap, th)
def setup_inputs_ties(rng):
    x, z, ts, kap, th = parts(rng); pat = rng.integers(0, 64, (N, 8, 16, 8))
    x = np.take_along_axis(pat, rng.integers(0, 8, (N, 8, 1, V)), 3); z = np.take_along_axis(pat, rng.integers(0, 8, (N, 8, 1, L)), 3)
    z = np.clip(z + rng.integers(-1, 2, z.shape) * (rng.random((N, 8, 1, L)) < 0.5), 0, 63); th = rng.integers(0, 40, (N, 8)); th[:, 3] = 0
    for r in range(N):
        for g in range(6):
            o = np.arange(V); ts[r, g] = o if g < 2 else o[::-1] if g < 4 else np.roll(o, int(rng.integers(1, V)))
    return pack(x, z, ts, kap, th)
def check_inputs(d):
    bad = []
    for k, lo, hi in (("xr", 0, 63), ("ts", 0, V - 1), ("zq", 0, 63), ("kap", 0, KM), ("th", 0, 1008)):
        a = np.asarray(d[k]).astype(np.float64)
        if not (np.min(a) >= lo and np.max(a) <= hi): bad.append("range of " + k)
        if np.any(a != np.floor(a)): bad.append("whole numbers of " + k)
    if np.any(np.sort(np.asarray(d["ts"]), axis=-1) != np.arange(V)): bad.append("permutation of ts")
    return bad
def reference(xr, ts, zq, kap, th):
    pick = np.take_along_axis
    X = xr.astype(np.float32).astype(np.int32).reshape(N, 8, 16, V); z = zq.astype(np.float32).astype(np.int32).reshape(N, 8, 16, L)
    T = ts.astype(np.int64); ka = kap.astype(np.int64).reshape(N, 8, 16); lim = th.astype(np.int64).reshape(N, 8); A = np.zeros((N, 8), np.int64)
    for rnd in range(RO):
        h = spots(mix(z), ka, A)
        xh = pick(X, h.reshape(N, 8, 1, 16 * L), 3).reshape(N, 8, 16, 16, L)
        e = np.add.reduce(np.abs(xh - z[:, :, :, None, :]), axis=2); m = np.argmin(e, axis=2)[:, :, None]
        s = pick(h, m, 2)[:, :, 0]; es = pick(e, m, 2)[:, :, 0]; xs = pick(X, s[:, :, None, :], 3)
        p = pick(np.argsort(T, axis=-1), s, 2); d = 1 + (mix(xs) & 15)
        at = np.maximum(p[:, :, None, :] - 1 - d[:, :, None, :] * np.arange(K)[:, None], 0)
        node = pick(T, at.reshape(N, 8, K * L), 2)
        xm = pick(X, node[:, :, None, :], 3).reshape(N, 8, 16, K, L)
        e = np.add.reduce(np.abs(xm - xs[:, :, :, None, :]), axis=2); k = np.argmin(e, axis=2)[:, :, None]
        n = pick(node.reshape(N, 8, K, L), k, 2)[:, :, 0]; xn = pick(X, n[:, :, None, :], 3)
        hit = es <= (lim + A)[:, :, None]
        vn = np.clip(xn + np.clip(z - xs, -2, 2), 0, 63); vs = (xs + z) >> 1
        z = np.where(hit[:, :, None, :], (z + xn) >> 1, np.abs(z - xn))
        for r in range(N):
            for g in range(8):
                lanes = np.flatnonzero(hit[r, g])
                un, i = np.unique(n[r, g, lanes], return_index=True); X[r, g][:, un] = vn[r, g][:, lanes[i]]
                us, i = np.unique(s[r, g, lanes], return_index=True); X[r, g][:, us] = vs[r, g][:, lanes[i]]
                gone = np.zeros(V, bool); gone[us] = True; old = T[r, g]
                T[r, g] = np.concatenate([old[~gone[old]], s[r, g, np.sort(lanes[i])]])
        A = L - np.add.reduce(hit.astype(np.int64), axis=2)
        z = np.ascontiguousarray(z.reshape(N, 8, 16, N, B).transpose(3, 1, 2, 0, 4)).reshape(N, 8, 16, L)
    return {"yx": X.reshape(N, 128, V).astype(np.float32).astype(BF), "yt": T.astype(np.float32), "yz": z.reshape(N, 128, L).astype(np.float32).astype(BF)}

@@ -1,0 +1,725 @@
+from concourse.bass import DstId, RemoteDMATransfer
+from concourse.mybir import AluOpType as OP, AxisListType, ActivationFunctionType as AF
+
+V, L, RO = 4096, 256, 4
+VV = V + RO * L
+MAGIC = 12582912.0
+RATIO = 1.875
+CFG = {"war": True, "na1": [range(8), [0, 2], [0, 2], [0, 2]], "na2": [[0]] * 4, "onA": ["xs", "g4", "g5", "g6"],
+       "tries": 7000, "pull": 3, "noise": 4000.0, "heat": 0.001,
+       "plans": [(1.04, 1.56, 3.8, 0.52, 70.0, 45.0, 2000.0, 4200.0, 0.4), (0.9, 1.2, 2.4, 0.45, 70.0, 45.0, 2000.0, 4200.0, 0.25),
+                 (1.15, 1.9, 5.0, 0.58, 130.0, 90.0, 2500.0, 5000.0, 0.25), (1.04, 1.56, 3.8, 1.04, 70.0, 45.0, 2000.0, 4200.0, 0.1)]}
+
+F32, BF, I32, U16 = "float32", "bfloat16", "int32", "uint16"
+BIG = {
+    "X": (V + L, BF), "XTa": (V + 2 * L, F32), "XTb": (V + 2 * L, F32), "POS": (V + L, F32), "FL": (V + L + 16, F32),
+    "DD": (VV, F32), "CUM": (VV, BF), "MK": (V + 16 + L, F32), "MS": (V, BF), "DF": (V, BF), "AB": (V, BF),
+    "Es": (2176, BF), "En": (2176, BF), "GA": (1024, BF), "ZR": (512, BF), "XR": (512, BF),
+    "Z0": (L, BF), "Z1": (L, BF), "Z2": (L, BF), "Z3": (L, BF), "Z4": (L, BF),
+    "S0": (L, BF), "S1": (L, BF), "S2": (L, BF), "S3": (L, BF),
+}
+SMALL = {
+    "tsb": (L, I32), "tsi": (2 * L, I32), "tsu": (L, U16), "tsd": (2 * L, BF), "pay": (2 * L, F32), "src": (L, U16),
+    "C256": (L, BF), "PA": (L, BF), "PB": (L, BF), "pI": (2, I32), "pF": (4, F32), "kI": (2, I32), "tI": (2, I32),
+    "OH": (16, F32), "ZB": (144, BF), "Z16": (144, BF), "ZU": (144, BF), "ZP": (144, BF), "BO": (128, BF), "BP": (128, BF),
+    "ID": (128, BF), "IN": (128, BF), "IH": (128, BF), "I16": (128, BF), "I32": (128, F32), "BO32": (128, F32), "TRI": (128, BF),
+    "G8": (128, F32), "row": (192, F32), "col": (32, F32), "kR": (16, F32), "kRi": (48, I32), "thF": (2, F32),
+    "kD": (48, F32), "KT": (16, BF), "PI": (L, F32), "P0": (L, F32), "PU": (RO * L, F32),
+    "t1": (L, BF), "t2": (L, BF), "t3": (L, BF), "t4": (L, BF), "t5": (128, BF), "lW": (16, F32), "wW": (16, F32),
+    "DM": (48 * RO, F32), "DN": (48, F32), "uF": (16, F32), "uI": (32, I32), "bF": (16, F32), "hI": (2 * L, I32),
+    "off": (L, U16), "of2": (L, U16), "K1": (128, F32), "K2": (128, F32), "K3": (96, F32), "KI": (32, I32), "KJ": (32, I32),
+    "mU": (16, U16), "hit": (16, BF), "hU": (16, U16), "g1": (L, BF), "g2": (L, BF), "g3": (L, BF), "g4": (2 * L, BF), "g4f": (L, F32),
+    "w1": (64, F32), "sI": (32, I32), "sU": (16, U16), "vU": (16, U16), "vF": (16, F32), "pm": (16, F32), "pU": (16, U16),
+    "dI": (32, I32), "nd": (16, F32), "wh": (64, F32), "kUs": (L, U16), "kUn": (L, U16), "TBs": (L, BF), "TBn": (L, BF),
+    "wins": (16, F32), "winn": (16, F32), "KDs": (48, F32), "KDn": (32, F32), "o1s": (48, F32), "o2s": (48, F32),
+    "o1n": (32, F32), "o2n": (32, F32), "oUs": (64, U16), "oUn": (32, U16), "qU": (16, U16), "w2": (112, F32), "aF": (32, F32),
+    "aU": (16, U16), "nF": (16, F32), "zw": (2 * L, BF), "cc": (L, BF), "vs": (L, BF), "v2": (L, BF), "xsf": (L, F32),
+    "rr": (L, BF), "vn": (L, BF), "fr": (2 * L, BF), "val": (L, F32),
+    "DC": (VV // 16, F32), "DB": (VV // 16, BF), "DS": (VV // 16, BF), "DO": (VV // 16, BF),
+    "MC": (L, F32), "MB": (L, BF), "MX": (L, BF), "MO": (L, BF), "MR": (16, BF), "zero": (VV // 16, F32), "zerb": (L, BF),
+    "ya": (544, F32), "yr": (544, BF), "yo": (272, F32),
+}
+PS = ["PK0", "PK1", "PH0", "PH1", "PN0", "PN1", "PS0", "PS1"]
+POOL = {F32: "sf", BF: "sb", I32: "si", U16: "su"}
+PLACE, FILL = {}, {d: 0 for d in POOL}
+for _k, (_n, _d) in SMALL.items():
+    PLACE[_k] = (POOL[_d], FILL[_d])
+    FILL[_d] += (_n + 15) // 16 * 16
+SCRATCH = {k: ("sbuf", [128, n], d) for k, (n, d) in BIG.items()}
+SCRATCH.update({POOL[d]: ("sbuf", [128, n], d) for d, n in FILL.items()})
+SCRATCH.update({k: ("psum", [128, 512], F32) for k in PS})
+DTYPE = {k: v[2] for k, v in SCRATCH.items()}
+NDMA = 44
+SEMAPHORES = ["eV", "eA", "eP", "eG"] + ["d%d" % i for i in range(NDMA)] + ["arr%d" % i for i in range(RO)] + ["snt%d" % i for i in range(RO)]
+ORDER = {}
+
+
+def A(name, c0=0, c1=None, st=1, p0=0, p1=128, ps=1):
+    if c1 is None:
+        c1 = BIG[name][0] if name in BIG else SMALL[name][0] if name in SMALL else 512
+    if name in PLACE:
+        name, c0, c1 = PLACE[name][0], c0 + PLACE[name][1], c1 + PLACE[name][1]
+    return ("ap", name, c0, c1, st, p0, p1, ps)
+
+
+def IND(win, off):
+    return ("ind", win, off)
+
+
+def width(a):
+    return 16 * (a[2][3] - a[2][2]) if a[0] == "ind" else (a[3] - a[2] + a[4] - 1) // a[4]
+
+
+def short(*xs):
+    return 0.5 if all(DTYPE[a[1]] in (BF, U16) for a in xs if a[0] == "ap") else 1.0
+
+
+def arrange(queue, work, pre):
+    n = len(queue)
+    above = [0] * n
+    for i in range(n):
+        far = 0
+        for p, _ in pre[i]:
+            far |= above[p]
+        keep = [(p, d) for p, d in pre[i] if not far >> p & 1 or work[p][6]]
+        for p, _ in pre[i]:
+            above[i] |= above[p] | 1 << p
+        pre[i] = keep
+    plans = []
+    for cy, gg, ss, pe, x, own, dm, rem, weight in CFG["plans"]:
+        cost = [1.0 + w[0] + cy * (max(64, w[1]) * (w[1] > 0) + w[2] + gg * w[3] + ss * w[4]) + pe * w[5] for w in work]
+        lat = [(0.0, dm + w[7] / 200.0, rem - 1000.0)[w[6]] for w in work]
+        plans.append((cost, lat, [[(p, lat[p] + (0.0, own, x)[d]) for p, d in pre[i]] for i in range(n)], weight))
+    cost, lat, edges, _ = plans[0]
+    post = [[] for _ in range(n)]
+    for i in range(n):
+        for p, d in edges[i]:
+            post[p].append((i, d))
+
+    def place(order, ed, first):
+        t, busy = [0.0] * n, {}
+        for i in order:
+            s = first[i]
+            for p, d in ed[i]:
+                s = max(s, t[p] + cost[p] + d)
+            lst = busy.setdefault(queue[i], [])
+            lo, hi = 0, len(lst)
+            while lo < hi:
+                mid = (lo + hi) // 2
+                if lst[mid][1] <= s:
+                    lo = mid + 1
+                else:
+                    hi = mid
+            while lo < len(lst) and s + cost[i] > lst[lo][0]:
+                s = max(s, lst[lo][1])
+                lo += 1
+            lst.insert(lo, (s, s + cost[i]))
+            t[i] = s
+        return t
+
+    def topo_order(key, ed):
+        done, out = [False] * n, []
+        for i in sorted(range(n), key=lambda j: key[j]):
+            stack = [i]
+            while stack:
+                j = stack[-1]
+                todo = [p for p, _ in ed[j] if not done[p]]
+                if todo and not done[j]:
+                    stack += sorted(todo, key=lambda p: -key[p])
+                    continue
+                stack.pop()
+                if not done[j]:
+                    done[j] = True
+                    out.append(j)
+        return out
+
+    def length(order, plan):
+        c, la, ed, _ = plan
+        e, free, end = [0.0] * n, {}, 0.0
+        for i in order:
+            s = free.get(queue[i], 0.0)
+            for p, d in ed[i]:
+                if e[p] + d > s:
+                    s = e[p] + d
+            e[i] = free[queue[i]] = s + c[i]
+            if e[i] + la[i] > end:
+                end = e[i] + la[i]
+        return end
+
+    rest = [cost[i] + lat[i] for i in range(n)]
+    for i in reversed(range(n)):
+        for p, d in edges[i]:
+            rest[p] = max(rest[p], cost[p] + d + rest[i])
+    best, cur, norm, seed, zero = None, None, None, 12345, [0.0] * n
+    key = [-r for r in rest]
+    for it in range(CFG["tries"]):
+        t = place(topo_order(key, edges), edges, zero)
+        order = sorted(range(n), key=lambda i: (t[i], i))
+        first = length(order, plans[0])
+        if norm is None or first * plans[0][3] / norm[0] < cur[2] * 1.03:
+            ends = [first] + [length(order, p) for p in plans[1:]]
+            norm = norm or ends
+            score = sum(e * p[3] / m for e, p, m in zip(ends, plans, norm))
+            if best is None or score < best[0]:
+                best = (score, order, ends)
+            if cur is None or score < cur[0] + CFG["heat"] * (1.0 - it / CFG["tries"]):
+                cur = (score, t, first * plans[0][3] / norm[0])
+        noise = [0.0] * n
+        if it % 4 < CFG["pull"]:
+            t, draw = cur[1], []
+            for i in range(6):
+                seed = (seed * 1103515245 + 12345) % 2147483648
+                draw.append(seed / 2147483648.0)
+            key = list(t)
+            for k in (0, 3):
+                a = int(draw[k] * n)
+                for i in range(n):
+                    if (i == a or above[a] >> i & 1) and t[i] > t[a] - draw[k + 1] * 2 * CFG["noise"]:
+                        key[i] -= draw[k + 2] ** 2 * CFG["noise"]
+            continue
+        if it % 2:
+            t, draw = cur[1], []
+            for i in range(19):
+                seed = (seed * 1103515245 + 12345) % 2147483648
+                draw.append(seed / 2147483648.0)
+            for k in range(1 + int(draw[18] * 6)):
+                a = int(draw[3 * k] * n)
+                for i in range(a, min(n, a + 1 + int(draw[3 * k + 1] ** 2 * 60))):
+                    noise[i] += (draw[3 * k + 2] - 0.5) * CFG["noise"]
+        u = place(topo_order([-(t[i] + cost[i]) + noise[i] for i in range(n)], post), post, lat)
+        key = [-(u[i] + cost[i]) for i in range(n)]
+    ORDER["end"] = best[2]
+    return best[1]
+
+
+def rank_program(g, core, T, topo):
+    rank = T.rank_of(core)
+    if rank is None:
+        return
+    N = len(T.cores)
+    B = L // N
+    Q = {"V": g.vector, "A": g.scalar, "P": g.tensor, "G": g, "S": g.sync}
+    ops = []
+
+    def real(a):
+        if not isinstance(a, tuple):
+            return a
+        if a[0] == "ind":
+            return real(a[1]).indirect(real(a[2]))
+        if a[0] == "raw":
+            return a[1]
+        _, n, c0, c1, st, p0, p1, ps = a
+        rows = slice(p0, p1) if ps == 1 else slice(p0, p1, ps)
+        cols = slice(c0, c1) if st == 1 else slice(c0, c1, st)
+        return T[n][rows, cols]
+
+    def spans(xs):
+        r = []
+        for a in xs:
+            if isinstance(a, tuple) and a[0] == "ap":
+                r.append((a[1], 0, 512, 1, 0, 1) if a[1] in PS else (a[1], a[2], a[3], a[4], a[5], a[7]))
+        return r
+
+    def meet(x, y):
+        if x[1] >= y[2] or y[1] >= x[2]:
+            return False
+        if x[3] == y[3] and (x[1] - y[1]) % x[3]:
+            return False
+        return not (x[5] == y[5] and (x[4] - y[4]) % x[5])
+
+    def add(q, fn, out, ins, work, sem=None, cnt=1, after=None):
+        w, r = [], []
+        for o in out:
+            if o[0] == "ind":
+                w.append(o[1]); r.append(o[2])
+            else:
+                w.append(o)
+        for i in ins:
+            if isinstance(i, tuple) and i[0] == "ind":
+                r += [i[1], i[2]]
+            else:
+                r.append(i)
+        ops.append({"q": q, "fn": fn, "w": spans(w), "r": spans(r), "sem": sem, "cnt": cnt, "work": work, "after": after, "i": len(ops)})
+
+    def vwork(o, a, k, fix=50):
+        if o[0] == "ind":
+            return (fix, 0, 0, 0, width(o), 0, 0, 0)
+        if a[0] == "ind":
+            return (fix, 0, 0, width(o), 0, 0, 0, 0)
+        return (0, width(o) * k, 0, 0, 0, 0, 0, 0)
+
+    def cp(o, i):
+        add("V", lambda: g.vector.tensor_copy(real(o), real(i)), [o], [i], vwork(o, i, short(o, i)))
+
+    def tt(o, a, b, op):
+        add("V", lambda: g.vector.tensor_tensor(real(o), real(a), real(b), op), [o], [a, b], vwork(o, a, 1 if a[1] in PS or b[1] in PS else 2))
+
+    def ts(o, a, s1, op0, s2=None, op1=None):
+        if op1 is None:
+            add("V", lambda: g.vector.tensor_scalar(real(o), real(a), real(s1), None, op0), [o], [a, s1], vwork(o, a, short(o, a)))
+        else:
+            add("V", lambda: g.vector.tensor_scalar(real(o), real(a), real(s1), real(s2), op0, op1), [o], [a, s1, s2], vwork(o, a, short(o, a)))
+
+    def rnd(o, a):
+        ts(o, a, MAGIC, OP.add, MAGIC, OP.subtract)
+
+    def ms(o, c):
+        add("V", lambda: g.vector.memset(real(o), c), [o], [], vwork(o, o, short(o)))
+
+    def red(o, a, op=OP.add):
+        add("V", lambda: g.vector.tensor_reduce(real(o), real(a), AxisListType.X, op), [o], [a], vwork(a, a, 1))
+
+    def scan(o, a, b, ini, op0, op1):
+        add("V", lambda: g.vector.tensor_tensor_scan(real(o), real(a), real(b), real(ini), op0, op1), [o], [a, b, ini], vwork(o, a, short(o, a, b)))
+
+    def act(o, a, f=AF.Copy, bias=None, scale=None):
+        kw = {}
+        if bias is not None:
+            kw["bias"] = bias
+        if scale is not None:
+            kw["scale"] = scale
+        w = vwork(o, a, 1, 65) if "ind" in (o[0], a[0]) else (0, 0, 64 + width(o), 0, 0, 0, 0, 0)
+        add("A", lambda: g.scalar.activation(real(o), real(a), f, **{k: real(v) for k, v in kw.items()}), [o], [a] + list(kw.values()), w)
+
+    def lin(o, a, scale=None, bias=None):
+        act(o, a, AF.Identity, bias, scale)
+
+    def pick(nm, o, a):
+        (act if nm in CFG["onA"] else cp)(o, a)
+
+    def iota(o, pat, base=0, cm=0, small=True):
+        w = (130, 0, 2 * width(o), 0, 0, 0, 0, 0)
+        if small:
+            add("G", lambda: g.iota(real(o), pat, base, cm, allow_small_or_imprecise_dtypes=True), [o], [], w)
+        else:
+            add("G", lambda: g.iota(real(o), pat, base, cm), [o], [], w)
+
+    def gcopy(o, i):
+        add("G", lambda: g.affine_select(real(o), real(i), [[0, width(o)]], OP.is_ge, 0.0, 0, 0), [o], [i], (170, 0, 2 * width(o), 0, 0, 0, 0, 0))
+
+    def zeros(name, c1):
+        for c in range(0, c1, 1024):
+            iota(A(name, c, min(c + 1024, c1)), [[0, min(c + 1024, c1) - c]])
+
+    def mm(terms, start=True, stop=True):
+        def fn():
+            for k, (o, l, r) in enumerate(terms):
+                ins = g.tensor.matmul(real(o), real(l), real(r), start and k == 0, stop and k == len(terms) - 1)
+            return ins
+        c = sum(max(64, width(r)) * (4 if DTYPE[l[1]] == F32 else 1) for _, l, r in terms)
+        add("P", fn, [t[0] for t in terms], [t[1] for t in terms] + [t[2] for t in terms], (0, 0, 0, 0, 0, c, 0, 0))
+
+    def wrap(out, band, name, c0=0, c1=L):
+        return [(out, A(band, 15 - r, 143 - r), A(name, c0 + r, c1, 16)) for r in range(16)]
+
+    nd = [0]
+
+    def dma(q, o, i, nbytes=0, **kw):
+        sem = "d%d" % nd[0]; nd[0] += 1
+        add(q, lambda: Q[q].dma_start(real(o), real(i), **kw), [o], [i] + ([o] if kw else []),
+            (1000 if q == "G" else 100, 0, 0, 0, 0, 0, 1, nbytes), sem, 16)
+
+    def rows(name, r, c1):
+        return A(name, 0, c1, p0=r, ps=16)
+
+    col = lambda k: A("col", k, k + 1)
+    C_W, C_P, C_WR, C_A, C_TH, C_T0, C_HS, C_MX, C_CC = 0, 1, 2, 3, 4, 5, 6, 7, 8
+    pcol, rcol, gcol, kcol = A("pF", 0, 1), A("pF", 1, 2), A("pF", 2, 3), A("pF", 3, 4)
+    e = lambda k: A("OH", k, k + 1)
+    row = lambda k, a=0, b=16, st=1: A("row", 16 * k + a, 16 * k + b, st)
+    W = lambda nm, k=0: A(nm, 16 * k, 16 * k + 16)
+    H = lambda nm, k=0: A(nm, L * k, L * k + L)
+
+    dma("S", A("tsb"), ("raw", T.ts[:]), 131072)
+    dma("A", A("X", 0, V), ("raw", T.xr[:]), 1 << 20)
+    dma("S", A("Z0"), ("raw", T.zq[:]), 65536)
+    dma("S", A("kI", 0, 1), ("raw", T.kap[:]))
+    dma("S", A("tI", 0, 1, p1=8), ("raw", T.th[:]))
+    iota(A("pI", 0, 1), [[0, 1]], 0, 1, False)
+    iota(A("C256"), [[1, L]])
+    iota(A("PA"), [[0, 16], [1, 16]])
+    iota(A("PB"), [[1, 16], [0, 16]])
+    zeros("MS", V)
+    cp(pcol, A("pI", 0, 1))
+    ts(A("pI", 1, 2), A("pI", 0, 1), 15, OP.bitwise_and)
+    ms(A("ZB"), 0.0)
+    cp(rcol, A("pI", 1, 2))
+    ts(gcol, pcol, rcol, OP.subtract, 1.0 / 16, OP.mult)
+    ts(A("OH"), A("C256", 0, 16), rcol, OP.is_equal)
+    ts(A("t1"), A("PA"), e(0), OP.mult)
+    ts(A("t2"), A("PB"), e(1), OP.mult)
+    ts(A("ZB", 15, 143, 16), A("C256", 0, 8), gcol, OP.is_equal)
+    ts(A("ID"), A("C256", 0, 128), pcol, OP.is_equal)
+    mm([(H("PN0"), A("ID"), A("t1")), (H("PN0"), A("ID"), A("t2"))])
+    act(A("PI"), H("PN0"))
+    cp(A("tsu"), A("tsb"))
+    ts(H("tsi"), A("tsb"), 4032, OP.bitwise_and)
+    ts(H("tsi", 1), A("tsb"), 63, OP.bitwise_and)
+    cp(A("tsd"), A("tsi"))
+    dma("S", rows("MS", 0, V), H("tsd"), 65536)
+    dma("S", rows("MS", 1, V), H("tsd", 1), 65536)
+    lin(A("pay"), A("tsd"), 2.0 ** -18)
+    ts(row(0, 0, 16, 2), A("C256", 0, 8), -1.0, OP.mult, -1.0, OP.add)
+    ts(row(0, 1, 16, 2), A("C256", 0, 8), 6.0, OP.min, 7.0, OP.subtract)
+    ts(A("BO32"), A("PB", 0, 128), gcol, OP.is_equal)
+    cp(kcol, A("kI", 0, 1))
+    tt(row(1), row(0), A("OH"), OP.mult)
+    ts(W("kD", 2), A("OH"), kcol, OP.mult)
+    red(col(C_W), row(1))
+    mm([(W("PH1"), A("BO32"), W("kD", 2))])
+    ts(A("ZU"), A("ZB"), col(C_W), OP.mult, -1.0, OP.mult)
+    ms(col(C_A), 0.0)
+    cp(A("kR"), W("PH1"))
+    lin(A("Z16"), A("ZB"), 16.0)
+    lin(A("IN"), A("ID"), -1.0)
+    lin(A("IH"), A("ID"), 0.5)
+    lin(A("I16"), A("ID"), 16.0)
+    act(A("I32"), A("ID"))
+    act(A("BO"), A("BO32"))
+    iota(A("zero"), [[0, VV // 16]])
+    iota(A("zerb"), [[0, L]])
+    dma("S", rows("DD", 0, VV), A("zero"), 163840)
+    zeros("FL", V + L + 16)
+    for k in range(RO):
+        dma("S", rows("MK", k, V), A("zero", 0, L), 131072)
+    zeros("CUM", VV)
+    ts(A("G8", p1=8), A("PB", 0, 128, p1=8), A("pF", 0, 1, p1=8), OP.is_equal)
+    cp(A("thF", 0, 1, p1=8), A("tI", 0, 1, p1=8))
+    mm([(A("PH1", 0, 1), A("G8", p1=8), A("thF", 0, 1, p1=8))])
+    ts(col(C_TH), A("PH1", 0, 1), 1.0, OP.add, 16.0, OP.mult)
+    lin(col(C_T0), col(C_TH), None, 4096.0)
+    cp(W("kRi"), A("kR"))
+    ts(W("kRi", 1), W("kRi"), 4032, OP.bitwise_and)
+    ts(W("kRi", 2), W("kRi"), 63, OP.bitwise_and)
+    ts(W("kD"), W("kRi", 1), e(0), OP.mult)
+    ts(W("kD", 1), W("kRi", 2), e(1), OP.mult)
+    tt(A("KT"), W("kD"), W("kD", 1), OP.add)
+    iota(row(2), [[0, 16]])
+    for k, w in enumerate((256, 1, 16, -256, -1)):
+        iota(row(2, k, k + 1), [[0, 1]], w)
+    tt(row(3), row(2), A("OH"), OP.mult)
+    red(col(C_P), row(3))
+    lin(A("ZP"), A("ZB"), col(C_P))
+    lin(A("BP"), A("BO"), col(C_P))
+    ms(row(4), RATIO ** -8)
+    ms(row(5), 1.0 / RATIO)
+    ms(row(6), 1e29)
+    scan(row(7), row(4), row(6), RATIO ** 68, OP.mult, OP.min)
+    scan(row(8), row(5), row(6), RATIO ** 8, OP.mult, OP.min)
+    tt(row(9), row(8), A("OH"), OP.mult)
+    tt(row(10), row(7), row(7), OP.mult)
+    red(col(C_WR), row(9))
+    lin(A("wW"), row(10), col(C_WR))
+    lin(A("lW"), A("C256", 0, 16), 16.0, rcol)
+    lin(A("t3"), A("PA"), e(1))
+    lin(A("t4"), A("PB"), e(2))
+    mm([(H("PN0"), A("ID"), A("t3")), (H("PN0"), A("ID"), A("t4"))])
+    act(A("P0"), H("PN0"))
+    ts(row(11, 0, 4), A("C256", 0, 4), 14.0, OP.add, e(0), OP.mult)
+    ts(row(11, 4, 8), A("C256", 0, 4), 40.0, OP.mult, e(5), OP.mult)
+    tt(row(11, 8, 12), row(11, 0, 4), row(11, 4, 8), OP.add)
+    lin(A("col", C_CC, C_CC + 4), row(11, 8, 12), None, 32.0)
+    ts(A("t5"), A("PA", 0, 128), rcol, OP.is_gt)
+    tt(A("TRI"), A("t5"), A("BO"), OP.mult)
+    for k in range(RO):
+        lin(H("PU", k), A("P0"), None, col(C_CC + k))
+    for nm, k, w in [("DM", k, V + (k % 3 == 1) * L * (k // 3)) for k in range(3 * RO)] + [("DN", 0, V), ("DN", 1, V + L), ("DN", 2, V + 16)]:
+        lin(W(nm, k), A("lW"), None, float(w))
+
+    def reorder(dst, srcw):
+        for k in range(8):
+            act(A(dst, 512 * k, 512 * k + 512), IND(srcw, A("src", 32 * k, 32 * k + 32)))
+
+    turn = [0]
+
+    def stage(win, off, ref, by_a, key):
+        for k in range(8):
+            c, o = (512 * k, 512 * k + 512), A(off, 32 * k, 32 * k + 32)
+            if k in by_a:
+                j = turn[0] % 2; turn[0] += 1
+                ga, pb = A("GA", 512 * j, 512 * j + 512), A("PS%d" % j)
+                act(ga, IND(win, o))
+                mm([(pb, A("ID"), ga), (pb, A("IN"), A(ref))])
+                act(A("AB", *c), pb, AF.Abs)
+            else:
+                tt(A("DF", *c), IND(win, o), A(ref), OP.subtract)
+                act(A("AB", *c), A("DF", *c), AF.Abs)
+            if k % 2:
+                q = k // 2
+                out = A("PK%d" % (q // 2), 64 * (q % 2), 64 * (q % 2) + 64)
+                mm([(out, A("ID"), A("PB", 64 * q, 64 * q + 64))] + wrap(out, "Z16", "AB", 1024 * q, 1024 * q + 1024))
+            if k == 3:
+                act(A("K1"), A("PK0", 0, 128))
+        tt(A("K2"), A("PK1", 0, 128), A("K1"), OP.min)
+        tt(A("K3", 0, 64), A("K2", 0, 64), A("K2", 64, 128), OP.min)
+        tt(A("K3", 64, 96), A("K3", 0, 32), A("K3", 32, 64), OP.min)
+        tt(W(key), W("K3", 4), W("K3", 5), OP.min)
+        ts(W(key, 1), W(key), 15, OP.bitwise_and)
+
+    def lowest(x, key, dm, n, bank, bank2, thr):
+        o = 0
+        for h in range(4):
+            terms = []
+            for c in range(4 * h, 4 * h + 4):
+                w = L - 16 * c
+                ts(A("E" + x, o, o + w), A("kU" + x, 16 * c, L), A(key, c, c + 1), OP.is_equal, A("wh", c, c + 1), OP.mult)
+                terms.append((A(bank, 16 * c, L), A("BO"), A("E" + x, o, o + w)))
+                o += w
+            mm(terms, h == 0, h == 3)
+        act(A("TB" + x), H(bank))
+        mm(wrap(W(bank2), "ZB", "TB" + x))
+        tt(A("win" + x), W(bank2), thr, OP.is_lt)
+        for k in range(n):
+            tt(W("o1" + x, k), W("KD" + x, k), A("win" + x), OP.mult)
+        tt(A("o2" + x, 0, 16 * n), A("o1" + x, 0, 16 * n), dm, OP.add)
+        cp(A("oU" + x, 0, 16 * n), A("o2" + x, 0, 16 * n))
+
+    peers = [r for r in range(N) if r != rank]
+
+    def engines_for(sender, dst):
+        sc = T.cores[sender]
+        fr = [r for r in range(N) if topo.chip(T.cores[r]) != topo.chip(sc)]
+        nr = [r for r in range(N) if r != sender and r not in fr]
+        used = topo.engines(sc, T.cores[fr[0]]) if fr else []
+        pool, lst = (used, fr) if dst in fr else ([x for x in topo.engines(sc, T.cores[dst]) if x not in used], nr)
+        n = 1
+        while 2 * n * len(lst) <= len(pool):
+            n *= 2
+        k = lst.index(dst)
+        return pool[k * n:(k + 1) * n]
+
+    def send(rho):
+        s, z = "S%d" % rho, "Z%d" % (rho + 1)
+
+        def fn():
+            trs = []
+            for r in peers:
+                rid, pid, _ = topo.addr(T.cores[r])
+                trs.append(RemoteDMATransfer(dst_ids=[DstId(rid=rid, pnc=pid)], dma_engine_mask=sum(1 << x for x in engines_for(rank, r)),
+                                             remote_sem=T.sem["arr%d" % rho], src=T[s][:, r * B:r * B + B], dst=T[z][:, rank * B:rank * B + B]))
+            g.remote_dma_fused(trs, local_sem=T.sem["snt%d" % rho])
+            return None
+        add("G", fn, [], [A(s)], (1000, 0, 0, 0, 0, 0, 0, 0), "snt%d" % rho, sum(len(engines_for(rank, r)) for r in peers))
+        add("R", None, [A(z, r * B, r * B + B) for r in peers], [], (0, 0, 0, 0, 0, 0, 2, 0), "arr%d" % rho,
+            sum(len(engines_for(r, rank)) for r in peers), ops[-1])
+        gcopy(A(z, rank * B, rank * B + B), A(s, rank * B, rank * B + B))
+
+    xt, xt2, xs = "XTa", "XTb", H("XR")
+    for rho in range(RO):
+        z, last_round = "Z%d" % rho, rho == RO - 1
+        Xw, XTw, PU, new = A("X", 0, V), A(xt, 0, V), H("PU", rho), 525.0 + 41 * rho
+        mm(wrap(W("PH0"), "ZU", z))
+        gcopy(H("ZR"), A(z))
+        gcopy(H("ZR", 1), A(z))
+        cp(A("uF"), W("PH0"))
+        tt(W("uI"), W("PH0"), A("uF"), OP.mult)
+        ts(W("uI", 1), W("uI"), 5, OP.arith_shift_right)
+        ts(A("bF"), W("uI", 1), col(C_A), OP.add)
+        for c in range(16):
+            ts(A("hI", c, L, 16), A("kR"), A("uF", c, c + 1), OP.mult, A("bF", c, c + 1), OP.add)
+        ts(H("hI", 1), H("hI"), V - 1, OP.bitwise_and)
+        cp(A("off"), H("hI", 1))
+        if rho == 0:
+            mm(wrap(H("PN1"), "ZB", "MS", 0, V))
+            cp(A("src"), H("PN1"))
+            dma("S", rows("MS", 1, V), A("zerb"), 65536)
+            for k in range(16):
+                ts(IND(A("POS", 0, V), W("tsu", k)), A("PI"), 1.0, OP.mult, float(k), OP.add)
+            reorder(xt, Xw)
+            dma("G", rows(xt, 0, V), H("pay"), 262144, accum_op=OP.add, max_dma_last_dim=8192)
+            dma("G", rows(xt, 1, V), H("pay", 1), 262144, accum_op=OP.add, max_dma_last_dim=8192)
+        stage(Xw, "off", "ZR", CFG["na1"][rho], "KI")
+        cp(A("mU"), W("KI", 1))
+        pick("g1", A("g1"), IND(A("KT"), A("mU")))
+        mm(wrap(W("PH0"), "ZB", "g1"))
+        tt(W("w1"), W("PH0"), A("uF"), OP.mult)
+        tt(W("sI"), W("w1"), A("bF"), OP.add)
+        ts(W("sI", 1), W("sI"), V - 1, OP.bitwise_and)
+        cp(A("sU"), W("sI", 1))
+        pick("g2", A("g2"), IND(A("POS", 0, V), A("sU")))
+        pick("xs", xs, IND(Xw, A("sU")))
+        mm(wrap(W("PH1"), "ZP", "g2"))
+        mm(wrap(W("PH0"), "ZU", "XR"))
+        gcopy(H("XR", 1), xs)
+        if rho > 0:
+            cp(A("vU"), W("PH1"))
+            pick("g3", A("g3"), IND(A("CUM"), A("vU")))
+        cp(A("vF"), W("PH1"))
+        if rho > 0:
+            mm(wrap(W("PH1"), "ZB", "g3"))
+        cp(W("dI"), W("PH0"))
+        ts(W("dI", 1), W("dI"), 15, OP.bitwise_and)
+        ts(A("nd"), W("dI", 1), -1.0, OP.mult, -1.0, OP.add)
+        if rho > 0:
+            lin(W("w1", 1), A("vF"), None, -1.0)
+            tt(A("pm"), W("w1", 1), W("PH1"), OP.subtract)
+        else:
+            ts(A("pm"), A("vF"), -1.0, OP.add)
+        for c in range(16):
+            ts(A("of2", c, L, 16), A("C256", 0, 16), A("nd", c, c + 1), OP.mult, A("pm", c, c + 1), OP.add)
+        ts(A("hit"), W("KI"), col(C_TH), OP.is_lt)
+        lin(W("w2", 5), A("hit"), float(L))
+        tt(W("w2", 6), W("w2", 5), A("lW"), OP.add)
+        cp(A("hU"), W("w2", 6))
+        tt(W("wh"), A("wW"), A("hit"), OP.mult)
+        lin(W("wh", 1), W("wh"), 40.0)
+        mm([(H("PN0"), A("BP"), A("g2"))])
+        cp(A("kUs"), H("PN0"))
+        tt(W("KDs"), W("sI", 1), W("DM", 3 * rho), OP.subtract)
+        tt(W("KDs", 1), A("vF"), W("DM", 3 * rho + 1), OP.subtract)
+        lin(W("w1", 2), A("pm"), None, 1.0)
+        ts(A("pU"), A("pm"), 1.0, OP.add)
+        tt(W("KDs", 2), W("w1", 2), W("DM", 3 * rho + 2), OP.subtract)
+        mm([(H("PN0"), A("ID"), A(z)), (H("PN0"), A("IN"), xs)])
+        lin(A("v2"), H("PN0"), 0.5, -0.25)
+        ts(A("cc"), H("PN0"), -2.0, OP.max, 2.0, OP.min)
+        rnd(A("vs"), A("v2"))
+        lowest("s", "vF", A("DM", 48 * rho, 48 * rho + 48), 3, "PN1", "PH0", W("wh", 1))
+        ts(W("oUs", 3), W("o2s", 2), 1.0, OP.add)
+        act(IND(A("DD"), W("oUs", 1)), PU, AF.Silu)
+        dma("S", A("DC"), rows("DD", 0, VV), 163840)
+        act(IND(A("FL", 0, V + L), W("oUs", 2)), PU, AF.Silu)
+        pick("g5", H("g4", 1), IND(A("FL"), W("oUs", 3)))
+        tt(IND(A("X"), W("oUs")), xs, A("vs"), OP.add)
+        act(A("DB"), A("DC"), AF.Relu, -91.0 - 2 * rho, 2.0)
+        scan(A("DS"), A("DB"), A("DB"), 0.0, OP.add, OP.max)
+        mm([(A("PH1", 0, 1), A("TRI"), A("DS", VV // 16 - 1, VV // 16))])
+        ts(A("DO"), A("DS"), A("PH1", 0, 1), OP.add)
+        dma("S", rows("CUM", rho, VV), A("DO"), 81920)
+        if not last_round:
+            act(IND(A("POS"), W("oUs")), PU, AF.Silu)
+            act(A("xsf"), IND(XTw, A("pU")))
+            mm([(H("PN1"), A("I32"), A("xsf")), (H("PN1"), A("ID"), A("vs"))])
+            act(A(xt, V, V + L), H("PN1"))
+            mm([(W("PH0"), A("BO"), A("hit"))])
+            red(col(C_HS), W("PH0"))
+            lin(col(C_A), col(C_HS), -1.0, float(L))
+            lin(col(C_TH), col(C_HS), -16.0, col(C_T0))
+        else:
+            act(A(xt, V, V + L), IND(XTw, A("pU")))
+            dma("S", A("ya", 0, 272), rows(xt, 0, V + L), 139264)
+            dma("S", A("ya", 272, 544), rows(xt, 1, V + L), 139264)
+            rnd(A("yr"), A("ya"))
+            o = A("PN1", 0, 272)
+            mm([(o, A("I32"), A("ya", 0, 272)), (o, A("IN"), A("yr", 0, 272)), (o, A("I32"), A("ya", 272, 544)), (o, A("IN"), A("yr", 272, 544))])
+            lin(A("yo"), o, 2.0 ** 18)
+            dma("S", rows(xt2, 0, V + L), A("yo"), 139264)
+        stage(XTw, "of2", "XR", CFG["na2"][rho], "KJ")
+        tt(W("w1", 3), W("KJ", 1), A("nd"), OP.mult)
+        tt(W("aF"), W("w1", 3), A("pm"), OP.add)
+        cp(A("aU"), W("aF"))
+        rnd(A("rr"), IND(XTw, A("aU")))
+        mm([(H("PN0"), A("ID"), A(z)), (H("PN0"), A("IN"), A("rr"))])
+        mm([(H("PN0", 1), A("IH"), A(z)), (H("PN0", 1), A("IH"), A("rr"))])
+        lin(H("zw"), H("PN0"), None, 128.0)
+        lin(H("zw", 1), H("PN0", 1), None, 127.75)
+        act(A("S%d" % rho), IND(A("zw"), A("hU")), AF.Abs, -128.0)
+        send(rho)
+        pick("g4", H("g4"), IND(A("CUM"), W("oUs", 1)))
+        mm(wrap(A("PH1", 0, 32), "ZB", "g4", 0, 2 * L))
+        lin(W("w2"), W("o2s", 1), None, 1.0)
+        tt(W("w2", 1), W("w2"), W("DN", 2), OP.subtract)
+        tt(W("w2", 2), W("w2", 1), W("PH1"), OP.subtract)
+        ts(W("w2", 3), W("PH1", 1), new, OP.is_lt)
+        tt(W("w2", 4), W("w2", 2), W("w2", 3), OP.mult)
+        tt(W("w2"), W("w2", 4), W("DN", 2), OP.add)
+        cp(A("qU"), W("w2"))
+        lin(A("g4f"), H("g4"), None, 32.0)
+        act(IND(A("MK"), A("qU")), A("g4f"), AF.Silu)
+        dma("S", A("MC"), rows("MK", rho, V), 131072)
+        lin(A("MB"), A("MC"), None, -32.0)
+        scan(A("MX"), A("MB"), A("MB"), 0.0, OP.max, OP.max)
+        ts(A("MR"), A("OH"), A("MX", L - 1, L), OP.mult)
+        mm([(W("PH1"), A("TRI"), A("MR"))])
+        red(col(C_MX), W("PH1"), OP.max)
+        ts(A("MO"), A("MX"), col(C_MX), OP.max)
+        dma("S", rows("MS", 0, V), A("MO"), 65536)
+        pick("g6", H("fr", 1), IND(A("FL"), A("aU")))
+        tt(H("fr"), IND(XTw, A("aU")), A("rr"), OP.subtract)
+        mm([(H("PS0"), A("ID"), A("rr")), (H("PS0"), A("ID"), A("cc"))])
+        mm([(H("PS1"), A("BO"), H("fr"))])
+        mm(wrap(A("PH0", 0, 32), "ZB", "fr", 0, 2 * L))
+        ts(W("wh", 3), W("PH0", 1), new, OP.is_lt)
+        tt(W("wh", 2), W("wh", 3), W("wh", 1), OP.mult)
+        ts(A("kUn"), H("PS1"), 2.0 ** 18, OP.mult)
+        lin(A("nF"), W("PH0"), 2.0 ** 18)
+        ts(A("vn"), H("PS0"), 0.0, OP.max, 63.0, OP.min)
+        tt(W("KDn"), A("nF"), W("DN"), OP.subtract)
+        if not last_round:
+            act(W("aF", 1), W("aF"), AF.Relu)
+            tt(W("KDn", 1), W("aF", 1), W("DN", 1), OP.subtract)
+            mm([(H("PS0"), A("ID"), H("fr")), (H("PS0"), A("ID"), A("vn"))])
+            act(A("val"), H("PS0"))
+        lowest("n", "nF", A("DN", 0, 16 if last_round else 32), 1 if last_round else 2, "PS1", "PH0", W("wh", 2))
+        if not last_round:
+            cp(IND(A(xt), W("oUn", 1)), A("val"))
+        cp(IND(A("X"), W("oUn")), A("vn"))
+        for h in range(4):
+            o = A(("PN1", "PN0")[h % 2], 0, 64)
+            mm([(o, A("I16"), A("C256", 64 * h, 64 * h + 64))] + wrap(o, "ZB", "MS", 1024 * h, 1024 * h + 1024))
+            ts(A("src", 64 * h, 64 * h + 64), o, rcol, OP.add)
+        if not last_round:
+            xt, xt2 = xt2, xt
+            reorder(xt, A(xt2, 0, V + L))
+        else:
+            dma("S", ("raw", T.yx[:]), A("X", 0, V), 1 << 20)
+            dma("S", ("raw", T.yz[:]), A("Z4"), 65536)
+            for h in range(4):
+                (cp if h % 2 else act)(A("POS", 1024 * h, 1024 * h + 1024), IND(A(xt2, 0, V + L), A("src", 64 * h, 64 * h + 64)))
+            dma("S", ("raw", T.yt[:]), rows("POS", 0, V), 131072)
+
+    hist = {}
+    for o in ops:
+        o["pre"], seen = [], set()
+        for kind in ("r", "w"):
+            for x in o[kind]:
+                for p, k2, y in hist.get(x[0], []):
+                    same = p["q"] == o["q"] and p["sem"] is None
+                    if not meet(x, y) or (kind == "r" and k2 == "r" and (x[0] not in PS or same)):
+                        continue
+                    free = same and (o["q"] == "P" or (not CFG["war"] and not (kind == "r" and k2 == "w")))
+                    if (p["i"], free) not in seen:
+                        seen.add((p["i"], free)); o["pre"].append((p, 0 if free else 1 if same else 2))
+        if o["after"]:
+            o["pre"].append((o["after"], 0))
+        for kind in ("r", "w"):
+            for x in o[kind]:
+                h = hist.setdefault(x[0], [])
+                if kind == "w" and x[3] == 1 and x[5] == 1 and x[4] == 0:
+                    h[:] = [y for y in h if not (x[1] <= y[2][1] and y[2][2] <= x[2])]
+                if not any(y[0] is o and y[1] == kind and y[2] == x for y in h[-3:]):
+                    h.append((o, kind, x))
+    shape = tuple((o["q"], tuple(p["i"] for p, _ in o["pre"])) for o in ops)
+    if shape not in ORDER:
+        ORDER[shape] = arrange([o["q"] for o in ops], [o["work"] for o in ops], [[(p["i"], d) for p, d in o["pre"]] for o in ops])
+    count, known = {}, {q: {} for q in Q}
+    for o in [ops[i] for i in ORDER[shape]]:
+        q = o["q"]
+        sem = o["sem"] or "e" + q
+        count[sem] = count.get(sem, 0) + o["cnt"]
+        o["tok"] = (sem, count[sem])
+        if q == "R":
+            o["kn"] = {}
+            continue
+        kn, want = known[q], {}
+        need = [p for p, d in o["pre"] if d]
+        for p in need:
+            s, c = p["tok"]
+            if kn.get(s, 0) < c:
+                want[s] = max(want.get(s, 0), c)
+        for p in need:
+            for s, c in p["kn"].items():
+                if want.get(s, 0) and want[s] <= c:
+                    want[s] = 0
+        for s, c in want.items():
+            if c:
+                Q[q].wait_ge(T.sem[s], c)
+        for p in need:
+            for s, c in list(p["kn"].items()) + [p["tok"]]:
+                kn[s] = max(kn.get(s, 0), c)
+        o["kn"] = dict(kn)
+        ins = o["fn"]()
+        if ins is not None:
+            ins.then_inc(T.sem[sem], o["cnt"])
+    for s, c in count.items():
+        g.wait_ge(T.sem[s], c)

@@ -1,43 +1,56 @@
+import math
 from concourse.bass import DstId, RemoteDMATransfer
 from concourse.mybir import AluOpType as OP, AxisListType, ActivationFunctionType as AF
 
 V, L, RO = 4096, 256, 4
 VV = V + RO * L
-MAGIC = 12582912.0
 RATIO = 1.875
-CFG = {"war": True, "na1": [range(8), [0, 2], [0, 2], [0, 2]], "na2": [[0]] * 4, "onA": ["xs", "g4", "g5", "g6"],
-       "tries": 7000, "pull": 3, "noise": 4000.0, "heat": 0.001,
-       "plans": [(1.04, 1.56, 3.8, 0.52, 70.0, 45.0, 2000.0, 4200.0, 0.4), (0.9, 1.2, 2.4, 0.45, 70.0, 45.0, 2000.0, 4200.0, 0.25),
-                 (1.15, 1.9, 5.0, 0.58, 130.0, 90.0, 2500.0, 5000.0, 0.25), (1.04, 1.56, 3.8, 1.04, 70.0, 45.0, 2000.0, 4200.0, 0.1)]}
+MARK = 512
+UP = 192.0
+ST_V = "%sVDFa0 %sVDFa1 %sVABa0 {} %sVABa1 %sVDFa4 {} %sVDFa5 %sVDFa6 %sVDFa7 "
+ST_A = "%sAGAa2 %sAGAa3 {} %sAABa2 %sAABa4 %sAABa3 {} %sAABa5 %sAABa6 %sAABa7 "
+TAIL_V = ("lowsVkUs lowsVE#1:16 " + (ST_V % (("st2",) * 8)).format("lowsVoFs lowsVoUs", "") + "xsVX foldVFS foldVR1 foldVFO foldVR2 "
+          "nVaUa lownVkUn lownVE#1:16 lownVfr lownVvn markVMK")
+TAIL_A = "valsAvs " + (ST_A % (("st2",) * 8)).format("foldAFL", "") + "valsAXT nArra nAzwa nASa markAg4 lownAg6 ddADD poswAPO"
+CFG = {"war": True, "nh": 1, "late": True, "st1": ["AAAAAAbb"] + ["rrAAbbbb"] * 3, "st2": ["rrAAbbbb"] * 4, "early": True, "g1v": True, "tbv": True,
+       "reo": 512, "mk": 128, "onV": ["sq"], "bank": ("PH0", "PS1"),
+       "line": {"V": "-xwVX uVuFa " + (ST_V % (("st1",) * 8)).format("-ddVDS", "-ddVDO") + "sVmUa -xtnVXT " + TAIL_V,
+                "A": "-reoAXT#1:4 " + (ST_A % (("st1",) * 8)).format("-reoAXT#5", "-reoAXT#6") + "-reoAXT#7:8 sAXRa#1:2 sAg3a " + TAIL_A},
+       "first": {"V": "pos0VPO#1:8 st10VDFa6 st10VDFa7 pos0VPO#9:16 " + TAIL_V,
+                 "A": "st10AGAa0 st10AGAa1 st10AABa0 st10AABa6 reo0AXT#1:4 st10AGAa2 st10AABa1 st10AABa7 st10AGAa3 st10AABa2 st10AGAa4 "
+                      "st10AABa3 st10AGAa5 st10AABa4 st10AABa5 reo0AXT#5:8 sAXRa#1:2 sAg3a " + TAIL_A},
+       "seed": 1, "steps": 190000, "reach": 5, "heat": 400.0, "cool": 30.0, "share": 0.6, "margin": 4000.0,
+       "plans": [(0.88, 1.56, 3.8, 0.6, 130.0, 70.0, 1300.0, 3200.0, 1.0)]}
 
 F32, BF, I32, U16 = "float32", "bfloat16", "int32", "uint16"
 BIG = {
-    "X": (V + L, BF), "XTa": (V + 2 * L, F32), "XTb": (V + 2 * L, F32), "POS": (V + L, F32), "FL": (V + L + 16, F32),
-    "DD": (VV, F32), "CUM": (VV, BF), "MK": (V + 16 + L, F32), "MS": (V, BF), "DF": (V, BF), "AB": (V, BF),
-    "Es": (2176, BF), "En": (2176, BF), "GA": (1024, BF), "ZR": (512, BF), "XR": (512, BF),
-    "Z0": (L, BF), "Z1": (L, BF), "Z2": (L, BF), "Z3": (L, BF), "Z4": (L, BF),
+    "X": (V + L, BF), "XTa": (V + 2 * L, F32), "XTb": (V + 2 * L, F32), "POS": (V + L, F32), "FL": (V + L, F32),
+    "DD": (VV, F32), "CUM": (16 + VV, BF), "MK": (V + 16 + L, BF), "MW": (2048, BF), "DF": (V, BF), "AB": (V, BF),
+    "E": (2176, BF), "NUM": (V, F32), "GA": (1024, BF), "XR": (5 * L, BF), "PU": (3 * L, F32), "MV": (RO * L, F32),
+    "Z0": (4 * L, BF), "Z1": (4 * L, BF), "Z2": (4 * L, BF), "Z3": (4 * L, BF), "Z4": (L, BF),
     "S0": (L, BF), "S1": (L, BF), "S2": (L, BF), "S3": (L, BF),
 }
 SMALL = {
-    "tsb": (L, I32), "tsi": (2 * L, I32), "tsu": (L, U16), "tsd": (2 * L, BF), "pay": (2 * L, F32), "src": (L, U16),
-    "C256": (L, BF), "PA": (L, BF), "PB": (L, BF), "pI": (2, I32), "pF": (4, F32), "kI": (2, I32), "tI": (2, I32),
-    "OH": (16, F32), "ZB": (144, BF), "Z16": (144, BF), "ZU": (144, BF), "ZP": (144, BF), "BO": (128, BF), "BP": (128, BF),
-    "ID": (128, BF), "IN": (128, BF), "IH": (128, BF), "I16": (128, BF), "I32": (128, F32), "BO32": (128, F32), "TRI": (128, BF),
-    "G8": (128, F32), "row": (192, F32), "col": (32, F32), "kR": (16, F32), "kRi": (48, I32), "thF": (2, F32),
-    "kD": (48, F32), "KT": (16, BF), "PI": (L, F32), "P0": (L, F32), "PU": (RO * L, F32),
-    "t1": (L, BF), "t2": (L, BF), "t3": (L, BF), "t4": (L, BF), "t5": (128, BF), "lW": (16, F32), "wW": (16, F32),
-    "DM": (48 * RO, F32), "DN": (48, F32), "uF": (16, F32), "uI": (32, I32), "bF": (16, F32), "hI": (2 * L, I32),
-    "off": (L, U16), "of2": (L, U16), "K1": (128, F32), "K2": (128, F32), "K3": (96, F32), "KI": (32, I32), "KJ": (32, I32),
-    "mU": (16, U16), "hit": (16, BF), "hU": (16, U16), "g1": (L, BF), "g2": (L, BF), "g3": (L, BF), "g4": (2 * L, BF), "g4f": (L, F32),
-    "w1": (64, F32), "sI": (32, I32), "sU": (16, U16), "vU": (16, U16), "vF": (16, F32), "pm": (16, F32), "pU": (16, U16),
-    "dI": (32, I32), "nd": (16, F32), "wh": (64, F32), "kUs": (L, U16), "kUn": (L, U16), "TBs": (L, BF), "TBn": (L, BF),
-    "wins": (16, F32), "winn": (16, F32), "KDs": (48, F32), "KDn": (32, F32), "o1s": (48, F32), "o2s": (48, F32),
-    "o1n": (32, F32), "o2n": (32, F32), "oUs": (64, U16), "oUn": (32, U16), "qU": (16, U16), "w2": (112, F32), "aF": (32, F32),
-    "aU": (16, U16), "nF": (16, F32), "zw": (2 * L, BF), "cc": (L, BF), "vs": (L, BF), "v2": (L, BF), "xsf": (L, F32),
-    "rr": (L, BF), "vn": (L, BF), "fr": (2 * L, BF), "val": (L, F32),
-    "DC": (VV // 16, F32), "DB": (VV // 16, BF), "DS": (VV // 16, BF), "DO": (VV // 16, BF),
-    "MC": (L, F32), "MB": (L, BF), "MX": (L, BF), "MO": (L, BF), "MR": (16, BF), "zero": (VV // 16, F32), "zerb": (L, BF),
-    "ya": (544, F32), "yr": (544, BF), "yo": (272, F32),
+    "tsb": (L, I32), "tsf": (L, F32), "tsh": (L, BF), "tsu": (L, U16), "tsd": (2 * L, BF), "src": (L, U16),
+    "C256": (L, BF), "PA": (L, BF), "PB": (L, BF), "PM": (L, BF), "pI": (2, I32), "pF": (4, F32), "kI": (2, I32), "tI": (2, I32),
+    "OH": (16, F32), "ZB": (144, BF), "Z16": (144, BF), "Z32": (144, BF), "ZM16": (144, BF), "ZU": (144, BF), "ZC": (144, BF),
+    "ZN": (144, BF), "ZQ": (144, BF), "ZX": (144, BF), "ZY": (144, BF), "BO": (128, BF), "ID": (128, BF), "IN": (128, BF), "IH": (128, BF),
+    "IBIG": (128, BF), "IDG": (128, BF), "IN64": (128, BF), "I288": (128, BF), "I32": (128, F32), "I64": (128, F32),
+    "BO32": (128, F32), "TRI": (128, BF), "SH": (128, BF), "SD": (128, BF), "one": (272, BF), "m128": (L, BF),
+    "MSK": (L, BF), "MS4": (L, BF), "KEEP": (L, BF),
+    "G8": (128, F32), "row": (176, F32), "col": (32, F32), "ro": (128, F32), "kR": (16, F32), "kB": (16, BF), "thF": (2, F32),
+    "kD": (48, F32), "KT": (16, BF), "PI": (L, F32), "PK": (L, F32), "t1": (L, BF), "t2": (L, BF), "t5": (128, BF),
+    "wW": (16, F32), "DM": (128, F32), "uF": (16, F32), "sq": (16, F32), "uI": (16, I32), "bF": (16, F32), "hI": (2 * L, I32),
+    "off": (L, U16), "of2": (L, U16), "K1": (64, F32), "K3": (48, F32), "k1": (32, I32), "k2": (32, I32),
+    "mU": (16, U16), "hit": (16, BF), "hU": (16, U16), "g1": (L, BF), "g1f": (L, F32), "g1s": (L, F32), "g3": (L, BF), "g4": (L, BF),
+    "g6": (L, BF), "w1": (64, F32), "sI": (32, I32), "sU": (16, U16), "vU": (16, U16), "pm": (16, F32),
+    "dI": (32, I32), "nd": (16, F32), "wh": (16, F32), "kUs": (L, U16), "kUn": (L, U16), "TBs": (L, BF), "TBn": (L, BF), "TS": (L, BF),
+    "los": (16, BF), "lon": (16, BF), "Ks": (48, F32), "Kn": (32, F32), "oFs": (48, F32), "oFn": (32, F32),
+    "oUs": (48, U16), "oUn": (32, U16), "qF": (16, F32), "qU": (16, U16), "aF": (16, F32), "aU": (16, U16),
+    "zw": (2 * L, BF), "cc": (L, BF), "vs": (L, BF), "rr": (L, BF), "vn": (L, BF), "fr": (L, BF), "val": (L, F32),
+    "DC": (VV // 16, F32), "DS": (VV // 16, BF), "DO": (VV // 16, BF),
+    "FC": (272, F32), "FS": (272, BF), "FO": (272, BF), "R1": (272, BF), "R2": (272, BF), "P1": (16 + L, BF), "sF": (L, F32),
+    "srn": (L, U16), "zero": (VV // 16, F32), "zerb": (L, BF), "c16": (L, F32), "yr": (544, BF),
 }
 PS = ["PK0", "PK1", "PH0", "PH1", "PN0", "PN1", "PS0", "PS1"]
 POOL = {F32: "sf", BF: "sb", I32: "si", U16: "su"}
@@ -49,8 +62,9 @@ SCRATCH = {k: ("sbuf", [128, n], d) for k, (n, d) in BIG.items()}
 SCRATCH.update({POOL[d]: ("sbuf", [128, n], d) for d, n in FILL.items()})
 SCRATCH.update({k: ("psum", [128, 512], F32) for k in PS})
 DTYPE = {k: v[2] for k, v in SCRATCH.items()}
-NDMA = 44
-SEMAPHORES = ["eV", "eA", "eP", "eG"] + ["d%d" % i for i in range(NDMA)] + ["arr%d" % i for i in range(RO)] + ["snt%d" % i for i in range(RO)]
+NDMA = 64
+SEMAPHORES = (["eV", "eA", "eP", "eG"] + ["d%d" % i for i in range(NDMA)]
+              + [s + h + str(i) for s in ("arr", "snt") for h in "ab" for i in range(RO)])
 ORDER = {}
 
 
@@ -74,7 +88,7 @@ def short(*xs):
     return 0.5 if all(DTYPE[a[1]] in (BF, U16) for a in xs if a[0] == "ap") else 1.0
 
 
-def arrange(queue, work, pre):
+def arrange(queue, work, pre, tags, fine, lap):
     n = len(queue)
     above = [0] * n
     for i in range(n):
@@ -95,36 +109,33 @@ def arrange(queue, work, pre):
     for i in range(n):
         for p, d in edges[i]:
             post[p].append((i, d))
+    ORDER["graph"] = (cost, lat, edges, cost)
+    seen, at, twin = {}, {}, []
+    for i in range(n):
+        k = seen[fine[i], lap[i]] = seen.get((fine[i], lap[i]), 0) + 1
+        at.setdefault((fine[i], k), [-1] * (RO + 1))[lap[i]] = i
+        twin.append(at[fine[i], k] if tags[i] != "set" else [])
+    extra = [[] for _ in range(n)]
+    for q in CFG["line"]:
+        chain = []
+        for r in range(RO + 1):
+            for w in CFG["line" if r else "first"][q].split():
+                nm, _, ks = w.lstrip("-").partition("#")
+                a, _, b = (ks or "1").partition(":")
+                chain += [at.get((nm, k), [-1] * (RO + 1))[r - (w[0] == "-")] for k in range(int(a), int(b or a) + 1)]
+        chain = [i for i in chain if i >= 0]
+        for a, b in zip(chain, chain[1:]):
+            extra[b].append((a, 0.0))
 
-    def place(order, ed, first):
-        t, busy = [0.0] * n, {}
-        for i in order:
-            s = first[i]
-            for p, d in ed[i]:
-                s = max(s, t[p] + cost[p] + d)
-            lst = busy.setdefault(queue[i], [])
-            lo, hi = 0, len(lst)
-            while lo < hi:
-                mid = (lo + hi) // 2
-                if lst[mid][1] <= s:
-                    lo = mid + 1
-                else:
-                    hi = mid
-            while lo < len(lst) and s + cost[i] > lst[lo][0]:
-                s = max(s, lst[lo][1])
-                lo += 1
-            lst.insert(lo, (s, s + cost[i]))
-            t[i] = s
-        return t
-
-    def topo_order(key, ed):
+    def ordered(key, ed):
         done, out = [False] * n, []
-        for i in sorted(range(n), key=lambda j: key[j]):
+        for i in sorted(range(n), key=lambda j: (key[j], j)):
             stack = [i]
             while stack:
                 j = stack[-1]
                 todo = [p for p, _ in ed[j] if not done[p]]
                 if todo and not done[j]:
+                    assert len(stack) < 20 * n, (fine[j], lap[j], [fine[p] for p in todo])
                     stack += sorted(todo, key=lambda p: -key[p])
                     continue
                 stack.pop()
@@ -133,62 +144,121 @@ def arrange(queue, work, pre):
                     out.append(j)
         return out
 
-    def length(order, plan):
-        c, la, ed, _ = plan
-        e, free, end = [0.0] * n, {}, 0.0
-        for i in order:
-            s = free.get(queue[i], 0.0)
-            for p, d in ed[i]:
-                if e[p] + d > s:
-                    s = e[p] + d
-            e[i] = free[queue[i]] = s + c[i]
-            if e[i] + la[i] > end:
-                end = e[i] + la[i]
-        return end
-
-    rest = [cost[i] + lat[i] for i in range(n)]
+    both = [edges[i] + extra[i] for i in range(n)]
+    key = [0.0] * n
+    for i in ordered(key, both):
+        key[i] = max([0.0] + [key[p] + cost[p] + d for p, d in both[i]])
+    ORDER["asap"] = max(key)
     for i in reversed(range(n)):
-        for p, d in edges[i]:
-            rest[p] = max(rest[p], cost[p] + d + rest[i])
-    best, cur, norm, seed, zero = None, None, None, 12345, [0.0] * n
-    key = [-r for r in rest]
-    for it in range(CFG["tries"]):
-        t = place(topo_order(key, edges), edges, zero)
-        order = sorted(range(n), key=lambda i: (t[i], i))
-        first = length(order, plans[0])
-        if norm is None or first * plans[0][3] / norm[0] < cur[2] * 1.03:
-            ends = [first] + [length(order, p) for p in plans[1:]]
-            norm = norm or ends
-            score = sum(e * p[3] / m for e, p, m in zip(ends, plans, norm))
-            if best is None or score < best[0]:
-                best = (score, order, ends)
-            if cur is None or score < cur[0] + CFG["heat"] * (1.0 - it / CFG["tries"]):
-                cur = (score, t, first * plans[0][3] / norm[0])
-        noise = [0.0] * n
-        if it % 4 < CFG["pull"]:
-            t, draw = cur[1], []
-            for i in range(6):
-                seed = (seed * 1103515245 + 12345) % 2147483648
-                draw.append(seed / 2147483648.0)
-            key = list(t)
-            for k in (0, 3):
-                a = int(draw[k] * n)
-                for i in range(n):
-                    if (i == a or above[a] >> i & 1) and t[i] > t[a] - draw[k + 1] * 2 * CFG["noise"]:
-                        key[i] -= draw[k + 2] ** 2 * CFG["noise"]
+        if tags[i] == "set" and post[i]:
+            key[i] = min(key[j] - d - cost[i] + (CFG["margin"] if tags[j] == "set" else 0.0) for j, d in post[i]) - CFG["margin"]
+    order = ordered(key, edges)
+
+    qn = {q: k for k, q in enumerate(sorted(set(queue)))}
+    qi = [qn[q] for q in queue]
+    flat = [(c, [c[i] + la[i] for i in range(n)], [tuple((p, c[p] + d) for p, d in ed[i]) for i in range(n)], w) for c, la, ed, w in plans]
+    up, down = [tuple(p for p, _ in edges[i]) for i in range(n)], [tuple(p for p, _ in post[i]) for i in range(n)]
+    seed, low = [CFG["seed"]], [0]
+
+    def draw():
+        seed[0] = (seed[0] * 1103515245 + 12345) % 2147483648
+        return seed[0] / 2147483648.0
+
+    def run(order, plan, a=0, old=None):
+        c, full, ed, _ = plan
+        free, who = [0.0] * len(qn), [-1] * len(qn)
+        if old is None or a < 50:
+            a, st, why, prev = 0, [0.0] * n, [-1] * n, [-1] * n
+        else:
+            why, prev, st, left = old[1][:], old[2][:], old[4][:], len(qn)
+            for k in range(a - 1, -1, -1):
+                i = order[k]
+                if who[qi[i]] < 0:
+                    who[qi[i]], free[qi[i]], left = i, st[i] + c[i], left - 1
+                    if not left:
+                        break
+        end, last = 0.0, -1
+        for i in order[a:]:
+            q = qi[i]
+            s = free[q]
+            w = prev[i] = who[q]
+            for p, d in ed[i]:
+                x = st[p] + d
+                if x > s:
+                    s, w = x, p
+            st[i] = s
+            why[i] = w
+            free[q] = s + c[i]
+            who[q] = i
+            x = s + full[i]
+            if x > end:
+                end, last = x, i
+        return end, why, prev, last, st
+
+    def arcs(res):
+        r, i = [], res[3]
+        while i >= 0:
+            w = res[1][i]
+            if w >= 0 and w == res[2][i] and not above[i] >> w & 1:
+                r.append((w, i))
+            i = w
+        return r
+
+    def move(order, mover, target, back):
+        a, b = order.index(target), order.index(mover)
+        if (a < b) != back:
+            return False
+        if not back:
+            a, b = b, a
+        part, tied, tq = order[a:b + 1], {mover}, set()
+        for x in (part[-2::-1] if back else part[1:]):
+            if qi[x] in tq or not tied.isdisjoint(down[x] if back else up[x]):
+                if qi[x] == qi[mover]:
+                    return False
+                tied.add(x)
+                tq.add(qi[x])
+        w, o = [x for x in part if x in tied], [x for x in part if x not in tied]
+        order[a:b + 1] = w + o if back else o + w
+        low[0] = min(low[0], a)
+        return True
+
+    use = [p for p in flat if p[3]]
+
+    def score(order, a=0, old=None):
+        rs = [run(order, p, min(a, n - 150), old and old[k]) for k, p in enumerate(use)]
+        return sum(r[0] * p[3] for r, p in zip(rs, use)), rs
+
+    cur, rs = score(order)
+    best, cand = (cur, order), [arcs(r) for r in rs]
+    for it in range(CFG["steps"]):
+        heat = CFG["heat"] * (CFG["cool"] / CFG["heat"]) ** (it / CFG["steps"])
+        k = int(draw() * len(use))
+        u, v = cand[k][int(draw() * len(cand[k]))]
+        prev, back, far = rs[k][2], draw() < 0.5, 1 + int(draw() ** 2 * CFG["reach"])
+        mover, target = (v, u) if back else (u, v)
+        if back:
+            for _ in range(far - 1):
+                if prev[target] >= 0 and not above[v] >> prev[target] & 1:
+                    target = prev[target]
+        elif far > 1:
+            a = order.index(v)
+            for x in [x for x in order[a:a + 60] if qi[x] == qi[v]][:far]:
+                if above[x] >> u & 1:
+                    break
+                target = x
+        new, low[0] = list(order), n
+        if not move(new, mover, target, back):
             continue
-        if it % 2:
-            t, draw = cur[1], []
-            for i in range(19):
-                seed = (seed * 1103515245 + 12345) % 2147483648
-                draw.append(seed / 2147483648.0)
-            for k in range(1 + int(draw[18] * 6)):
-                a = int(draw[3 * k] * n)
-                for i in range(a, min(n, a + 1 + int(draw[3 * k + 1] ** 2 * 60))):
-                    noise[i] += (draw[3 * k + 2] - 0.5) * CFG["noise"]
-        u = place(topo_order([-(t[i] + cost[i]) + noise[i] for i in range(n)], post), post, lat)
-        key = [-(u[i] + cost[i]) for i in range(n)]
-    ORDER["end"] = best[2]
+        if draw() < CFG["share"]:
+            for m2, t2 in zip(twin[mover], twin[target]):
+                if m2 >= 0 and t2 >= 0 and m2 != mover:
+                    move(new, m2, t2, back)
+        s, r2 = score(new, low[0], rs)
+        if s <= cur or draw() < math.exp((cur - s) / heat):
+            order, cur, rs, cand = new, s, r2, [arcs(r) for r in r2]
+            if s < best[0]:
+                best = (s, order)
+    ORDER["end"] = [run(best[1], p)[0] for p in flat]
     return best[1]
 
 
@@ -198,8 +268,21 @@ def rank_program(g, core, T, topo):
         return
     N = len(T.cores)
     B = L // N
+    NH = CFG["nh"]
+    HL = L // NH
+    CW, XS = HL // 16, HL + 512
+    own = rank * B // HL
+    halves = (("a", own), ("b", 1 - own))[:NH]
     Q = {"V": g.vector, "A": g.scalar, "P": g.tensor, "G": g, "S": g.sync}
-    ops = []
+    ops, tag, sub, lap = [], ["set"], [""], [0]
+
+    def called(a):
+        a = a[1] if a[0] == "ind" else a
+        if a[0] == "raw":
+            return "out"
+        if a[1] not in POOL.values():
+            return a[1][:2] if a[1][0] not in "SZ" else a[1][0]
+        return max((c, k) for k, (p, c) in PLACE.items() if p == a[1] and c <= a[2])[1]
 
     def real(a):
         if not isinstance(a, tuple):
@@ -225,7 +308,7 @@ def rank_program(g, core, T, topo):
             return False
         if x[3] == y[3] and (x[1] - y[1]) % x[3]:
             return False
-        return not (x[5] == y[5] and (x[4] - y[4]) % x[5])
+        return not (x[4] - y[4]) % min(x[5], y[5])
 
     def add(q, fn, out, ins, work, sem=None, cnt=1, after=None):
         w, r = [], []
@@ -239,7 +322,8 @@ def rank_program(g, core, T, topo):
                 r += [i[1], i[2]]
             else:
                 r.append(i)
-        ops.append({"q": q, "fn": fn, "w": spans(w), "r": spans(r), "sem": sem, "cnt": cnt, "work": work, "after": after, "i": len(ops)})
+        ops.append({"q": q, "fn": fn, "w": spans(w), "r": spans(r), "sem": sem, "cnt": cnt, "work": work, "after": after, "i": len(ops),
+                    "lap": lap[0], "tag": tag[0], "fine": tag[0] + q + (called(out[0]) if out and tag[0] != "set" else "") + sub[0]})
 
     def vwork(o, a, k, fix=50):
         if o[0] == "ind":
@@ -260,9 +344,6 @@ def rank_program(g, core, T, topo):
         else:
             add("V", lambda: g.vector.tensor_scalar(real(o), real(a), real(s1), real(s2), op0, op1), [o], [a, s1, s2], vwork(o, a, short(o, a)))
 
-    def rnd(o, a):
-        ts(o, a, MAGIC, OP.add, MAGIC, OP.subtract)
-
     def ms(o, c):
         add("V", lambda: g.vector.memset(real(o), c), [o], [], vwork(o, o, short(o)))
 
@@ -281,11 +362,15 @@ def rank_program(g, core, T, topo):
         w = vwork(o, a, 1, 65) if "ind" in (o[0], a[0]) else (0, 0, 64 + width(o), 0, 0, 0, 0, 0)
         add("A", lambda: g.scalar.activation(real(o), real(a), f, **{k: real(v) for k, v in kw.items()}), [o], [a] + list(kw.values()), w)
 
-    def lin(o, a, scale=None, bias=None):
-        act(o, a, AF.Identity, bias, scale)
-
-    def pick(nm, o, a):
-        (act if nm in CFG["onA"] else cp)(o, a)
+    def lin(o, a, scale=None, bias=None, nm=None):
+        if nm not in CFG["onV"]:
+            act(o, a, AF.Identity, bias, scale)
+        elif scale is None and bias is None:
+            cp(o, a)
+        elif scale is None or bias is None:
+            ts(o, a, bias if scale is None else scale, OP.add if scale is None else OP.mult)
+        else:
+            ts(o, a, scale, OP.mult, bias, OP.add)
 
     def iota(o, pat, base=0, cm=0, small=True):
         w = (130, 0, 2 * width(o), 0, 0, 0, 0, 0)
@@ -294,12 +379,15 @@ def rank_program(g, core, T, topo):
         else:
             add("G", lambda: g.iota(real(o), pat, base, cm), [o], [], w)
 
-    def gcopy(o, i):
-        add("G", lambda: g.affine_select(real(o), real(i), [[0, width(o)]], OP.is_ge, 0.0, 0, 0), [o], [i], (170, 0, 2 * width(o), 0, 0, 0, 0, 0))
+    def select(o, i, pat, op, base, cm):
+        add("G", lambda: g.affine_select(real(o), real(i), pat, op, 0.0, base, cm), [o], [i], (170, 0, 2 * width(o), 0, 0, 0, 0, 0))
 
-    def zeros(name, c1):
-        for c in range(0, c1, 1024):
-            iota(A(name, c, min(c + 1024, c1)), [[0, min(c + 1024, c1) - c]])
+    def gcopy(o, i):
+        select(o, i, [[0, width(o)]], OP.is_ge, 0, 0)
+
+    def zeros(name, c0, c1, step=512):
+        for c in range(c0, c1, step):
+            iota(A(name, c, min(c + step, c1)), [[0, min(c + step, c1) - c]])
 
     def mm(terms, start=True, stop=True):
         def fn():
@@ -314,93 +402,133 @@ def rank_program(g, core, T, topo):
 
     nd = [0]
 
-    def dma(q, o, i, nbytes=0, **kw):
+    def dma(q, o, i, nbytes=0, after=None, **kw):
         sem = "d%d" % nd[0]; nd[0] += 1
         add(q, lambda: Q[q].dma_start(real(o), real(i), **kw), [o], [i] + ([o] if kw else []),
-            (1000 if q == "G" else 100, 0, 0, 0, 0, 0, 1, nbytes), sem, 16)
+            (1000 if q == "G" else 100, 0, 0, 0, 0, 0, 1, nbytes), sem, 16, after)
+        return ops[-1]
 
-    def rows(name, r, c1):
-        return A(name, 0, c1, p0=r, ps=16)
+    def rows(name, r, c1, c0=0):
+        return A(name, c0, c1, p0=r, ps=16)
 
     col = lambda k: A("col", k, k + 1)
-    C_W, C_P, C_WR, C_A, C_TH, C_T0, C_HS, C_MX, C_CC = 0, 1, 2, 3, 4, 5, 6, 7, 8
-    pcol, rcol, gcol, kcol = A("pF", 0, 1), A("pF", 1, 2), A("pF", 2, 3), A("pF", 3, 4)
+    C_W, C_P, C_WR, C_A, C_TH, C_T0, C_HS, C_R16, C_C, C_N, C_G, C_Q, C_X, C_K, C_Y = range(15)
+    R_HI, R_LO, R_CNT, R_NEXT, R_RUN = 4, 12, 7, 8, 10
+    pcol, rcol, kcol = A("pF", 0, 1), A("pF", 1, 2), A("pF", 3, 4)
     e = lambda k: A("OH", k, k + 1)
     row = lambda k, a=0, b=16, st=1: A("row", 16 * k + a, 16 * k + b, st)
-    W = lambda nm, k=0: A(nm, 16 * k, 16 * k + 16)
-    H = lambda nm, k=0: A(nm, L * k, L * k + L)
+    W = lambda nm, k=0, n=1: A(nm, 16 * k, 16 * (k + n))
+    H = lambda nm, k=0, n=1: A(nm, L * k, L * (k + n))
+    Wh = lambda nm, h, k=0: A(nm, 16 * k + CW * h, 16 * k + CW * h + CW)
+    Hh = lambda nm, h, k=0: A(nm, L * k + HL * h, L * k + HL * h + HL)
+    CUMw = A("CUM", 16, 16 + VV)
+
+    def weights(c, pairs):
+        for k, (r, w) in enumerate(pairs):
+            lin(col(c), e(r), float(w), col(c) if k else None)
+
+    def spread(z, c0):
+        for n in (128, 256):
+            if n >= HL:
+                gcopy(A(z, c0 + n, c0 + 2 * n), A(z, c0, c0 + n))
 
     dma("S", A("tsb"), ("raw", T.ts[:]), 131072)
-    dma("A", A("X", 0, V), ("raw", T.xr[:]), 1 << 20)
-    dma("S", A("Z0"), ("raw", T.zq[:]), 65536)
+    xload = dma("A", A("X", 0, V), ("raw", T.xr[:]), 1 << 20)
+    for _, h in halves:
+        dma("S", A("Z0", 512 * h, 512 * h + HL), ("raw", T.zq[:, HL * h:HL * h + HL]), 32768)
     dma("S", A("kI", 0, 1), ("raw", T.kap[:]))
     dma("S", A("tI", 0, 1, p1=8), ("raw", T.th[:]))
     iota(A("pI", 0, 1), [[0, 1]], 0, 1, False)
     iota(A("C256"), [[1, L]])
     iota(A("PA"), [[0, 16], [1, 16]])
     iota(A("PB"), [[1, 16], [0, 16]])
-    zeros("MS", V)
+    iota(A("PM", 0, HL), [[1, 16], [0, CW]])
+    ms(A("CUM", 0, 2064), 0.0)
+    ms(A("CUM", 2064, V + 16), 0.0)
+    zeros("CUM", V + 16, VV + 16)
     cp(pcol, A("pI", 0, 1))
     ts(A("pI", 1, 2), A("pI", 0, 1), 15, OP.bitwise_and)
-    ms(A("ZB"), 0.0)
     cp(rcol, A("pI", 1, 2))
-    ts(gcol, pcol, rcol, OP.subtract, 1.0 / 16, OP.mult)
     ts(A("OH"), A("C256", 0, 16), rcol, OP.is_equal)
-    ts(A("t1"), A("PA"), e(0), OP.mult)
-    ts(A("t2"), A("PB"), e(1), OP.mult)
-    ts(A("ZB", 15, 143, 16), A("C256", 0, 8), gcol, OP.is_equal)
+    ts(A("t1"), A("PA"), -2.0, OP.add, e(14), OP.mult)
+    lin(A("t2"), A("PB"), e(0))
     ts(A("ID"), A("C256", 0, 128), pcol, OP.is_equal)
     mm([(H("PN0"), A("ID"), A("t1")), (H("PN0"), A("ID"), A("t2"))])
     act(A("PI"), H("PN0"))
+    iota(A("one"), [[0, 272]], 1)
+    select(A("t5"), A("one", 0, 128), [[-16, 8], [0, 16]], OP.is_ge, 0, 1)
+    select(A("BO"), A("t5"), [[16, 8], [0, 16]], OP.is_ge, 15, -1)
+    iota(A("ZB"), [[0, 144]])
+    gcopy(A("ZB", 15, 143, 16), A("BO", 0, 128, 16))
+    act(A("BO32"), A("BO"))
+    lin(A("IN64"), A("ID"), -64.0)
+    act(A("I32"), A("ID"))
     cp(A("tsu"), A("tsb"))
-    ts(H("tsi"), A("tsb"), 4032, OP.bitwise_and)
-    ts(H("tsi", 1), A("tsb"), 63, OP.bitwise_and)
-    cp(A("tsd"), A("tsi"))
-    dma("S", rows("MS", 0, V), H("tsd"), 65536)
-    dma("S", rows("MS", 1, V), H("tsd", 1), 65536)
-    lin(A("pay"), A("tsd"), 2.0 ** -18)
-    ts(row(0, 0, 16, 2), A("C256", 0, 8), -1.0, OP.mult, -1.0, OP.add)
-    ts(row(0, 1, 16, 2), A("C256", 0, 8), 6.0, OP.min, 7.0, OP.subtract)
-    ts(A("BO32"), A("PB", 0, 128), gcol, OP.is_equal)
+    cp(A("tsf"), A("tsb"))
+    lin(A("tsh"), A("tsf"), 1.0 / 64, UP - 63.0 / 128)
+    mm([(H("PS1"), A("I32"), A("tsf")), (H("PS1"), A("IN64"), A("tsh"))])
+    lin(H("tsd"), A("tsh"), 2.0 ** -16, -UP * 2.0 ** -16)
+    lin(H("tsd", 1), H("PS1"), 2.0 ** -16, 64 * UP * 2.0 ** -16)
+    dma("S", rows("CUM", R_HI, 16 + V, 16), H("tsd"), 65536)
+    dma("S", rows("CUM", R_LO, 16 + V, 16), H("tsd", 1), 65536)
+    iota(row(0, 0, 16, 2), [[1, 8]], 1)
+    iota(row(0, 1, 16, 2), [[-1, 8]], 7)
+    iota(row(0, 15, 16), [[0, 1]], 1)
     cp(kcol, A("kI", 0, 1))
     tt(row(1), row(0), A("OH"), OP.mult)
-    ts(W("kD", 2), A("OH"), kcol, OP.mult)
+    lin(W("kD", 2), A("OH"), kcol)
     red(col(C_W), row(1))
     mm([(W("PH1"), A("BO32"), W("kD", 2))])
-    ts(A("ZU"), A("ZB"), col(C_W), OP.mult, -1.0, OP.mult)
-    ms(col(C_A), 0.0)
-    cp(A("kR"), W("PH1"))
+    lin(A("ZU"), A("ZB"), col(C_W))
+    lin(col(C_A), pcol, 0.0, -0.375)
+    act(A("kR"), W("PH1"))
     lin(A("Z16"), A("ZB"), 16.0)
+    if "r" in "".join(CFG["st1"] + CFG["st2"]):
+        lin(A("Z32"), A("ZB"), 32.0)
+        lin(A("ZM16"), A("ZB"), -16.0)
     lin(A("IN"), A("ID"), -1.0)
     lin(A("IH"), A("ID"), 0.5)
-    lin(A("I16"), A("ID"), 16.0)
-    act(A("I32"), A("ID"))
-    act(A("BO"), A("BO32"))
+    lin(A("IBIG"), A("ID"), 8192.0)
+    lin(A("I288"), A("ID"), 288.0)
+    lin(A("I64"), A("ID"), 64.0)
+    iota(A("m128"), [[0, L]], -128)
     iota(A("zero"), [[0, VV // 16]])
-    iota(A("zerb"), [[0, L]])
-    dma("S", rows("DD", 0, VV), A("zero"), 163840)
-    zeros("FL", V + L + 16)
     for k in range(RO):
-        dma("S", rows("MK", k, V), A("zero", 0, L), 131072)
-    zeros("CUM", VV)
-    ts(A("G8", p1=8), A("PB", 0, 128, p1=8), A("pF", 0, 1, p1=8), OP.is_equal)
+        dma("S", rows("FL", k, V + L), A("zero", 0, (V + L) // 16), 139264)
+        if 0 < k < RO - 1:
+            dma("S", rows("DD", k, VV), A("zero"), 163840)
+    iota(A("G8", p1=8), [[0, 128]], 1)
+    select(A("G8", p1=8), A("G8", p1=8), [[1, 8], [0, 16]], OP.is_equal, 0, -1)
     cp(A("thF", 0, 1, p1=8), A("tI", 0, 1, p1=8))
     mm([(A("PH1", 0, 1), A("G8", p1=8), A("thF", 0, 1, p1=8))])
-    ts(col(C_TH), A("PH1", 0, 1), 1.0, OP.add, 16.0, OP.mult)
+    lin(col(C_TH), A("PH1", 0, 1), 16.0, 16.0)
     lin(col(C_T0), col(C_TH), None, 4096.0)
-    cp(W("kRi"), A("kR"))
-    ts(W("kRi", 1), W("kRi"), 4032, OP.bitwise_and)
-    ts(W("kRi", 2), W("kRi"), 63, OP.bitwise_and)
-    ts(W("kD"), W("kRi", 1), e(0), OP.mult)
-    ts(W("kD", 1), W("kRi", 2), e(1), OP.mult)
-    tt(A("KT"), W("kD"), W("kD", 1), OP.add)
-    iota(row(2), [[0, 16]])
-    for k, w in enumerate((256, 1, 16, -256, -1)):
-        iota(row(2, k, k + 1), [[0, 1]], w)
-    tt(row(3), row(2), A("OH"), OP.mult)
-    red(col(C_P), row(3))
-    lin(A("ZP"), A("ZB"), col(C_P))
-    lin(A("BP"), A("BO"), col(C_P))
+    if CFG["g1v"] or CFG["tbv"]:
+        ts(A("MSK"), A("PA"), rcol, OP.is_equal)
+        lin(A("MS4"), A("MSK"), 0.4)
+        act(A("KEEP"), A("PA"), AF.Sign)
+    if not CFG["g1v"]:
+        act(A("kB"), A("kR"))
+        lin(W("kD"), A("kR"), e(1))
+        lin(col(C_K), e(1), -1.0, e(0))
+        lin(W("kD", 1), A("kB"), col(C_K))
+        tt(A("KT"), W("kD"), W("kD", 1), OP.add)
+    weights(C_P, ((14, 32), (0, 1), (13, 16), (6, -64), (15, -1)))
+    weights(C_C, ((0, -1), (1, -1), (2, -1)))
+    weights(C_N, ((R_HI, 1 << 22), (R_LO, 1 << 16)))
+    weights(C_G, ((R_HI, 1), (R_LO, 1)))
+    weights(C_Q, ((R_NEXT, 8192), (R_CNT, -1)))
+    if CFG["early"]:
+        weights(C_X, ((R_RUN, 8192),))
+        lin(A("ZX"), A("ZB"), col(C_X))
+    if CFG["late"]:
+        weights(C_Y, ((R_RUN, 8192), (R_CNT, -1)))
+        lin(A("ZY"), A("ZB"), col(C_Y))
+    lin(A("ZC"), A("ZB"), col(C_C))
+    lin(A("ZN"), A("ZB"), col(C_N))
+    lin(A("ZQ"), A("ZB"), col(C_Q))
+    lin(A("IDG"), A("ID"), col(C_G))
+    select(A("SH"), A("BO"), [[1, 128]], OP.is_equal, -1, -1)
     ms(row(4), RATIO ** -8)
     ms(row(5), 1.0 / RATIO)
     ms(row(6), 1e29)
@@ -410,262 +538,340 @@ def rank_program(g, core, T, topo):
     tt(row(10), row(7), row(7), OP.mult)
     red(col(C_WR), row(9))
     lin(A("wW"), row(10), col(C_WR))
-    lin(A("lW"), A("C256", 0, 16), 16.0, rcol)
-    lin(A("t3"), A("PA"), e(1))
-    lin(A("t4"), A("PB"), e(2))
-    mm([(H("PN0"), A("ID"), A("t3")), (H("PN0"), A("ID"), A("t4"))])
-    act(A("P0"), H("PN0"))
-    ts(row(11, 0, 4), A("C256", 0, 4), 14.0, OP.add, e(0), OP.mult)
-    ts(row(11, 4, 8), A("C256", 0, 4), 40.0, OP.mult, e(5), OP.mult)
-    tt(row(11, 8, 12), row(11, 0, 4), row(11, 4, 8), OP.add)
-    lin(A("col", C_CC, C_CC + 4), row(11, 8, 12), None, 32.0)
-    ts(A("t5"), A("PA", 0, 128), rcol, OP.is_gt)
-    tt(A("TRI"), A("t5"), A("BO"), OP.mult)
+    for k, w in enumerate((V, V, V + L, V, V, V + 2 * L, V + 15)):
+        iota(W("ro", k), [[16, 16]], w)
+    iota(W("ro", 7), [[0, NH], [16, CW]])
+    ts(A("DM"), A("ro"), rcol, OP.add)
+    select(A("TRI"), A("BO"), [[1, 128]], OP.is_gt, 0, -1)
+    iota(A("PU"), [[0, 3 * L]], 32)
+    for k, (r, pat, base) in enumerate(((14, [[1, 3], [0, L]], 46), (0, [[0, 48], [1, 16]], 32), (13, [[0, 3], [1, 16], [0, 16]], 32))):
+        o = A("XTb", L * 3 * k, L * (3 + 3 * k), p1=8)
+        iota(o, pat, base)
+        dma("S", rows("PU", r, 3 * L), o, 24576)
+    zeros("MV", 0, RO * L)
+    iota(A("PK", p1=8), [[0, L]], MARK)
     for k in range(RO):
-        lin(H("PU", k), A("P0"), None, col(C_CC + k))
-    for nm, k, w in [("DM", k, V + (k % 3 == 1) * L * (k // 3)) for k in range(3 * RO)] + [("DN", 0, V), ("DN", 1, V + L), ("DN", 2, V + 16)]:
-        lin(W(nm, k), A("lW"), None, float(w))
+        dma("S", rows("MV", k, L * k + L, L * k), A("PK", p1=8), 8192)
+    select(A("t2", 0, 128), A("BO"), [[1, 128]], OP.is_ge, 0, -1)
+    dma("S", A("MW"), A("CUM", 0, 2048), 1 << 19, after=xload)
+    dma("S", rows("MW", R_RUN, 2048), A("t2", 0, 128), 32768)
+    lin(A("t5"), A("BO"), e(15))
+    tt(A("SD"), A("t5"), A("ID"), OP.subtract)
+    iota(A("P1", 0, 16), [[0, 16]])
+    dma("S", A("MK", 0, V), A("CUM", 0, V), 1 << 20, after=xload)
+    zeros("MK", V, V + 16 + L)
+    for c in range(0, V, 512):
+        iota(A("NUM", c, c + 512), [[1, 512]], c)
+    iota(A("zerb"), [[0, L]])
+    iota(A("c16"), [[0, L]], 16)
+    lin(col(C_R16), rcol, None, -16.0)
+    iota(A("t1", 0, 48), [[0, 48]], L)
+    dma("S", rows("CUM", 0, 16 + VV, 16 + V + L), A("t1", 0, 48), 12288)
 
-    def reorder(dst, srcw):
-        for k in range(8):
-            act(A(dst, 512 * k, 512 * k + 512), IND(srcw, A("src", 32 * k, 32 * k + 32)))
+    def reorder(dst, srcw, lst, bias=None):
+        n = CFG["reo"]
+        for c in range(0, V, n):
+            lin(A(dst, c, c + n), IND(srcw, A(lst, c // 16, (c + n) // 16)), None, bias, nm=lst + str(c // n))
 
-    turn = [0]
-
-    def stage(win, off, ref, by_a, key):
-        for k in range(8):
-            c, o = (512 * k, 512 * k + 512), A(off, 32 * k, 32 * k + 32)
-            if k in by_a:
-                j = turn[0] % 2; turn[0] += 1
-                ga, pb = A("GA", 512 * j, 512 * j + 512), A("PS%d" % j)
-                act(ga, IND(win, o))
-                mm([(pb, A("ID"), ga), (pb, A("IN"), A(ref))])
-                act(A("AB", *c), pb, AF.Abs)
+    def stage(x, h, win, off, ref, modes, key):
+        for q in range(4 // NH):
+            out, c0 = A("PK%d" % (q % 2), 0, 64), 16 * HL * h + 1024 * q
+            for k in (2 * q, 2 * q + 1):
+                sub[0] = x + str(k)
+                c = 16 * HL * h + 512 * k
+                o, ab, df = A(off, c // 16, c // 16 + 32), A("AB", c, c + 512), A("DF", c, c + 512)
+                if modes[k] == "A":
+                    ga, pb = A("GA", 512 * (k % 2), 512 * (k % 2) + 512), A("PS%d" % (k % 2 if NH == 1 else 0))
+                    act(ga, IND(win, o))
+                    mm([(pb, A("ID"), ga), (pb, A("IN"), ref)])
+                    act(ab, pb, AF.Abs)
+                else:
+                    tt(df, IND(win, o), ref, OP.subtract)
+                    if modes[k] == "r":
+                        ts(ab, df, 0.0, OP.max)
+                    else:
+                        act(ab, df, AF.Abs)
+            first = [(out, A("ID"), A("PM", 64 * q, 64 * q + 64))]
+            if modes[2 * q] == "r":
+                mm(first + wrap(out, "ZM16", "DF", c0, c0 + 1024), True, False)
+                mm(wrap(out, "Z32", "AB", c0, c0 + 1024), False, True)
             else:
-                tt(A("DF", *c), IND(win, o), A(ref), OP.subtract)
-                act(A("AB", *c), A("DF", *c), AF.Abs)
-            if k % 2:
-                q = k // 2
-                out = A("PK%d" % (q // 2), 64 * (q % 2), 64 * (q % 2) + 64)
-                mm([(out, A("ID"), A("PB", 64 * q, 64 * q + 64))] + wrap(out, "Z16", "AB", 1024 * q, 1024 * q + 1024))
-            if k == 3:
-                act(A("K1"), A("PK0", 0, 128))
-        tt(A("K2"), A("PK1", 0, 128), A("K1"), OP.min)
-        tt(A("K3", 0, 64), A("K2", 0, 64), A("K2", 64, 128), OP.min)
-        tt(A("K3", 64, 96), A("K3", 0, 32), A("K3", 32, 64), OP.min)
-        tt(W(key), W("K3", 4), W("K3", 5), OP.min)
-        ts(W(key, 1), W(key), 15, OP.bitwise_and)
+                mm(first + wrap(out, "Z16", "AB", c0, c0 + 1024))
+            if q == 0:
+                lin(A("K1"), out, nm="K1")
+            else:
+                tt(A("K1"), out, A("K1"), OP.min)
+        sub[0] = x
+        tt(A("K3", 0, 32), A("K1", 0, 32), A("K1", 32, 64), OP.min)
+        if NH == 1:
+            tt(W(key), A("K3", 0, 16), A("K3", 16, 32), OP.min)
+        else:
+            tt(A("K3", 32, 48), A("K3", 0, 16), A("K3", 16, 32), OP.min)
+            tt(Wh(key, h), A("K3", 32, 40), A("K3", 40, 48), OP.min)
+        ts(Wh(key, h, 1), Wh(key, h), 15, OP.bitwise_and)
 
-    def lowest(x, key, dm, n, bank, bank2, thr):
+    def lowest(x, key, n, dm, bank, more):
         o = 0
         for h in range(4):
             terms = []
             for c in range(4 * h, 4 * h + 4):
                 w = L - 16 * c
-                ts(A("E" + x, o, o + w), A("kU" + x, 16 * c, L), A(key, c, c + 1), OP.is_equal, A("wh", c, c + 1), OP.mult)
-                terms.append((A(bank, 16 * c, L), A("BO"), A("E" + x, o, o + w)))
+                ts(A("E", o, o + w), A("kU" + x, 16 * c, L), A("K" + x, key + c, key + c + 1), OP.is_equal, A("wh", c, c + 1), OP.mult)
+                terms.append((A("PN1", 16 * c, L), A("BO"), A("E", o, o + w)))
                 o += w
             mm(terms, h == 0, h == 3)
-        act(A("TB" + x), H(bank))
-        mm(wrap(W(bank2), "ZB", "TB" + x))
-        tt(A("win" + x), W(bank2), thr, OP.is_lt)
-        for k in range(n):
-            tt(W("o1" + x, k), W("KD" + x, k), A("win" + x), OP.mult)
-        tt(A("o2" + x, 0, 16 * n), A("o1" + x, 0, 16 * n), dm, OP.add)
-        cp(A("oU" + x, 0, 16 * n), A("o2" + x, 0, 16 * n))
+        if CFG["tbv"]:
+            tt(A("TB" + x), H("PN1"), A("MS4"), OP.mult)
+            scan(A("TS"), A("KEEP"), A("TB" + x), 0.0, OP.mult, OP.add)
+            tt(A("lo" + x), A("TS", 15, L, 16), A("wh"), OP.is_ge)
+        else:
+            lin(A("TB" + x), H("PN1"), 1.0 / 40, nm="TB" + x)
+            mm(wrap(W("PN1"), "ZB", "TB" + x))
+            tt(A("lo" + x), W("PN1"), A("wh"), OP.is_ge)
+        mm([(W(bank, 0, n), A("I32"), W("K" + x, 0, n))] + more, True, False)
+        mm([(W(bank, k), A("IBIG"), A("lo" + x)) for k in range(n)], False, True)
+        tt(W("oF" + x, 0, n), W(bank, 0, n), dm, OP.min)
+        cp(W("oU" + x, 0, n), W("oF" + x, 0, n))
 
-    peers = [r for r in range(N) if r != rank]
+    def mates(r, x):
+        return [s for s in range(N) if s != r and (s * B // HL == r * B // HL) == (x == "a")]
 
-    def engines_for(sender, dst):
+    def engines_for(sender, dst, x):
         sc = T.cores[sender]
-        fr = [r for r in range(N) if topo.chip(T.cores[r]) != topo.chip(sc)]
-        nr = [r for r in range(N) if r != sender and r not in fr]
+        fr = [r for r in mates(sender, x) if topo.chip(T.cores[r]) != topo.chip(sc)]
+        nr = [r for r in mates(sender, x) if r not in fr]
         used = topo.engines(sc, T.cores[fr[0]]) if fr else []
-        pool, lst = (used, fr) if dst in fr else ([x for x in topo.engines(sc, T.cores[dst]) if x not in used], nr)
+        pool, lst = (used, fr) if dst in fr else ([k for k in topo.engines(sc, T.cores[dst]) if k not in used], nr)
         n = 1
         while 2 * n * len(lst) <= len(pool):
             n *= 2
         k = lst.index(dst)
         return pool[k * n:(k + 1) * n]
 
-    def send(rho):
-        s, z = "S%d" % rho, "Z%d" % (rho + 1)
+    def send(rho, x):
+        s, z, peers = "S%d" % rho, "Z%d" % (rho + 1), mates(rank, x)
+        spot = lambda r: r * B if rho == RO - 1 else 512 * (r * B // HL) + r * B % HL
 
         def fn():
             trs = []
             for r in peers:
                 rid, pid, _ = topo.addr(T.cores[r])
-                trs.append(RemoteDMATransfer(dst_ids=[DstId(rid=rid, pnc=pid)], dma_engine_mask=sum(1 << x for x in engines_for(rank, r)),
-                                             remote_sem=T.sem["arr%d" % rho], src=T[s][:, r * B:r * B + B], dst=T[z][:, rank * B:rank * B + B]))
-            g.remote_dma_fused(trs, local_sem=T.sem["snt%d" % rho])
+                trs.append(RemoteDMATransfer(dst_ids=[DstId(rid=rid, pnc=pid)], dma_engine_mask=sum(1 << k for k in engines_for(rank, r, x)),
+                                             remote_sem=T.sem["arr%s%d" % (x, rho)], src=T[s][:, r * B:r * B + B],
+                                             dst=T[z][:, spot(rank):spot(rank) + B]))
+            g.remote_dma_fused(trs, local_sem=T.sem["snt%s%d" % (x, rho)])
             return None
-        add("G", fn, [], [A(s)], (1000, 0, 0, 0, 0, 0, 0, 0), "snt%d" % rho, sum(len(engines_for(rank, r)) for r in peers))
-        add("R", None, [A(z, r * B, r * B + B) for r in peers], [], (0, 0, 0, 0, 0, 0, 2, 0), "arr%d" % rho,
-            sum(len(engines_for(r, rank)) for r in peers), ops[-1])
-        gcopy(A(z, rank * B, rank * B + B), A(s, rank * B, rank * B + B))
+        add("G", fn, [], [A(s, r * B, r * B + B) for r in peers], (1000, 0, 0, 0, 0, 0, 0, 0), "snt%s%d" % (x, rho),
+            sum(len(engines_for(rank, r, x)) for r in peers))
+        add("R", None, [A(z, spot(r), spot(r) + B) for r in peers], [], (0, 0, 0, 0, 0, 0, 2, 0), "arr%s%d" % (x, rho),
+            sum(len(engines_for(r, rank, x)) for r in peers), ops[-1])
+        if x == "a":
+            gcopy(A(z, spot(rank), spot(rank) + B), A(s, rank * B, rank * B + B))
 
-    xt, xt2, xs = "XTa", "XTb", H("XR")
+    xt, xt2 = "XTa", "XTb"
     for rho in range(RO):
         z, last_round = "Z%d" % rho, rho == RO - 1
-        Xw, XTw, PU, new = A("X", 0, V), A(xt, 0, V), H("PU", rho), 525.0 + 41 * rho
-        mm(wrap(W("PH0"), "ZU", z))
-        gcopy(H("ZR"), A(z))
-        gcopy(H("ZR", 1), A(z))
-        cp(A("uF"), W("PH0"))
-        tt(W("uI"), W("PH0"), A("uF"), OP.mult)
-        ts(W("uI", 1), W("uI"), 5, OP.arith_shift_right)
-        ts(A("bF"), W("uI", 1), col(C_A), OP.add)
-        for c in range(16):
-            ts(A("hI", c, L, 16), A("kR"), A("uF", c, c + 1), OP.mult, A("bF", c, c + 1), OP.add)
-        ts(H("hI", 1), H("hI"), V - 1, OP.bitwise_and)
-        cp(A("off"), H("hI", 1))
+        by_place = rho == 0 or last_round
+        Xw, XTw = A("X", 0, V), A(xt, 0, V)
+        zh = lambda h, n=HL: A(z, 512 * h, 512 * h + n)
+        xs = lambda h, n=HL: A("XR", XS * h + HL, XS * h + HL + n)
+        kv = 1 if rho == 0 else 2
+        lap[0] = rho
+        for (x, h), bank in zip(halves, CFG["bank"]):
+            tag[0], sub[0] = "u", x
+            mm(wrap(A(bank, 0, CW), "ZU", z, 512 * h, 512 * h + HL))
+            spread(z, 512 * h)
+            cp(Wh("uF", h), A(bank, 0, CW))
+            if "sq" in CFG["onV"]:
+                tt(Wh("sq", h), A(bank, 0, CW), Wh("uF", h), OP.mult)
+            else:
+                act(Wh("sq", h), Wh("uF", h), AF.Square)
+            ts(Wh("uI", h), Wh("sq", h), 1.0 / 32, OP.mult, col(C_A), OP.add)
+            cp(Wh("bF", h), Wh("uI", h))
+            for c in range(CW * h, CW * h + CW):
+                ts(A("hI", HL * h + c % CW, HL * h + HL, CW), A("kR"), A("uF", c, c + 1), OP.mult, A("bF", c, c + 1), OP.add)
+            ts(Hh("hI", h, 1), Hh("hI", h), V - 1, OP.bitwise_and)
+            cp(Hh("off", h), Hh("hI", h, 1))
+        sub[0] = ""
         if rho == 0:
-            mm(wrap(H("PN1"), "ZB", "MS", 0, V))
+            tag[0] = "src0"
+            mm(wrap(H("PN1"), "ZN", "CUM", 16, 16 + V))
             cp(A("src"), H("PN1"))
-            dma("S", rows("MS", 1, V), A("zerb"), 65536)
+            tag[0] = "pos0"
             for k in range(16):
-                ts(IND(A("POS", 0, V), W("tsu", k)), A("PI"), 1.0, OP.mult, float(k), OP.add)
-            reorder(xt, Xw)
-            dma("G", rows(xt, 0, V), H("pay"), 262144, accum_op=OP.add, max_dma_last_dim=8192)
-            dma("G", rows(xt, 1, V), H("pay", 1), 262144, accum_op=OP.add, max_dma_last_dim=8192)
-        stage(Xw, "off", "ZR", CFG["na1"][rho], "KI")
-        cp(A("mU"), W("KI", 1))
-        pick("g1", A("g1"), IND(A("KT"), A("mU")))
-        mm(wrap(W("PH0"), "ZB", "g1"))
-        tt(W("w1"), W("PH0"), A("uF"), OP.mult)
-        tt(W("sI"), W("w1"), A("bF"), OP.add)
-        ts(W("sI", 1), W("sI"), V - 1, OP.bitwise_and)
-        cp(A("sU"), W("sI", 1))
-        pick("g2", A("g2"), IND(A("POS", 0, V), A("sU")))
-        pick("xs", xs, IND(Xw, A("sU")))
-        mm(wrap(W("PH1"), "ZP", "g2"))
-        mm(wrap(W("PH0"), "ZU", "XR"))
-        gcopy(H("XR", 1), xs)
-        if rho > 0:
-            cp(A("vU"), W("PH1"))
-            pick("g3", A("g3"), IND(A("CUM"), A("vU")))
-        cp(A("vF"), W("PH1"))
-        if rho > 0:
-            mm(wrap(W("PH1"), "ZB", "g3"))
-        cp(W("dI"), W("PH0"))
-        ts(W("dI", 1), W("dI"), 15, OP.bitwise_and)
-        ts(A("nd"), W("dI", 1), -1.0, OP.mult, -1.0, OP.add)
-        if rho > 0:
-            lin(W("w1", 1), A("vF"), None, -1.0)
-            tt(A("pm"), W("w1", 1), W("PH1"), OP.subtract)
+                ts(IND(A("POS", 0, V), W("tsu", k)), A("PI"), 1.0, OP.mult, 32.0 + k, OP.add)
+            tag[0] = "reo0"
+            reorder(xt, Xw, "src", UP)
+            for c in (0, V // 2):
+                dma("G", A(xt, c, c + V // 2, p0=R_HI, ps=8), A("CUM", 16 + c, 16 + c + V // 2, p0=R_HI, ps=8), 131072,
+                    accum_op=OP.add, max_dma_last_dim=8192)
+        for x, h in halves:
+            tag[0] = "st1" if rho else "st10"
+            stage(x, h, Xw, "off", zh(h, 512), CFG["st1"][rho], "k1")
+        for (x, h), bank in zip(halves, CFG["bank"]):
+            tag[0], sub[0] = "s", x
+            p8 = lambda k=0: A(bank, CW * k, CW * k + CW)
+            cp(Wh("mU", h), Wh("k1", h, 1))
+            if CFG["g1v"]:
+                tt(Hh("g1f", h), IND(A("kR"), Wh("mU", h)), A("MSK", 0, HL), OP.mult)
+                scan(Hh("g1s", h), A("KEEP", 0, HL), Hh("g1f", h), 0.0, OP.mult, OP.add)
+                tt(Wh("w1", h), A("g1s", HL * h + 15, HL * h + HL, 16), Wh("uF", h), OP.mult)
+            else:
+                lin(Hh("g1", h), IND(A("KT"), Wh("mU", h)), nm="g1")
+                mm(wrap(p8(), "ZB", "g1", HL * h, HL * h + HL))
+                tt(Wh("w1", h), p8(), Wh("uF", h), OP.mult)
+            tt(Wh("sI", h), Wh("w1", h), Wh("uI", h), OP.add)
+            ts(Wh("sI", h, 1), Wh("sI", h), V - 1, OP.bitwise_and)
+            cp(Wh("sU", h), Wh("sI", h, 1))
+            lin(A("XR", XS * h, XS * h + HL), IND(A("POS", 0, V), Wh("sU", h)), col(C_P), nm="g2")
+            lin(xs(h), IND(Xw, Wh("sU", h)), None, UP, nm="xs")
+            mm(wrap(A(bank, 0, 2 * CW), "ZU", "XR", XS * h, XS * h + 2 * HL))
+            spread("XR", XS * h + HL)
+            cp(Wh("vU", h), p8())
+            lin(Wh("Ks", h, kv), p8(), nm="vF")
+            cp(Wh("dI", h), p8(1))
+            lin(Hh("g3", h), IND(CUMw, Wh("vU", h)), nm="g3")
+            ts(Wh("dI", h, 1), Wh("dI", h), 15, OP.bitwise_and)
+            ts(Wh("nd", h), Wh("dI", h, 1), -1.0, OP.mult, -1.0, OP.add)
+            if rho > 0:
+                mm(wrap(p8(), "ZC", "g3", HL * h, HL * h + HL))
+                tt(Wh("Ks", h, 1), p8(), Wh("Ks", h, kv), OP.add)
+            ts(Wh("pm", h), Wh("Ks", h, 1), -1.0, OP.add)
+            for c in range(CW * h, CW * h + CW):
+                ts(A("of2", HL * h + c % CW, HL * h + HL, CW), A("C256", 0, 16), A("nd", c, c + 1), OP.mult, A("pm", c, c + 1), OP.add)
+            tag[0] = "hit"
+            ts(Wh("hit", h), Wh("k1", h), col(C_TH), OP.is_lt, float(HL), OP.mult)
+            tt(Wh("w1", h, 1), Wh("hit", h), Wh("DM", h, 7), OP.add)
+            cp(Wh("hU", h), Wh("w1", h, 1))
+        sub[0] = ""
+        if not last_round:
+            tag[0] = "cnt"
+            dma("S", A("CUM", 16 + V + L * rho, 16 + V + L * rho + L, p0=R_HI, ps=8), A("g3", p0=R_HI, ps=8), 8192)
+            mm([(W("PN0"), A("BO"), A("hit"))])
+            red(col(C_HS), W("PN0"))
+            lin(col(C_A), col(C_HS), -1.0 / HL, L - 0.375)
+            lin(col(C_TH), col(C_HS), -16.0 / HL, col(C_T0))
+        tag[0] = "vals"
+        mm([(Hh("PN0", h, k), A(m), r) for _, h in halves for k, m, r in ((0, "ID", zh(h)), (0, "IN", xs(h)), (1, "IH", zh(h)), (1, "IH", xs(h)))])
+        lin(A("vs"), H("PN0", 1), None, 128.0 - UP / 2 - 0.25)
+        ts(A("cc"), H("PN0"), -2.0 - UP, OP.max, 2.0 - UP, OP.min)
+        mm([(H("PN0"), A("ID"), A("vs")), (H("PN0"), A("IDG"), A("g3"))])
+        lin(A(xt, V, V + L), H("PN0"), None, UP - 128.0, nm="app")
+        tag[0] = "lows"
+        tt(A("wh"), A("wW"), A("hit"), OP.mult)
+        cp(W("Ks"), W("sI", 1))
+        cp(A("kUs"), IND(A("NUM"), A("sU")))
+        ns = 2 if by_place else 3
+        lowest("s", 0, ns, W("DM", 3 if rho == 2 else 0, ns), "PH1", [])
+        if CFG["early"]:
+            tag[0] = "xs"
+            tt(IND(A("X"), W("oUs")), A("vs"), A("m128"), OP.add)
+        tag[0] = "fold"
+        E = (V + L) // 16
+        act(IND(A("FL"), W("oUs", 1)), H("MV", rho), AF.Silu)
+        dma("S", A("FC"), rows("FL", rho, V + L), 139264)
+        scan(A("FS"), A("FC"), A("FC"), 0.0, OP.add, OP.max)
+        scan(A("R1"), A("one", 0, E), A("FC"), 0.0, OP.add, OP.min)
+        mm([(A("PH1", 0, 1), A("TRI"), A("FS", E - 1, E)), (A("PH1", 1, 2), A("SH"), A("R1", E - 1, E))])
+        ts(A("FO"), A("FS"), A("PH1", 0, 1), OP.add, 1.0 / MARK, OP.mult)
+        scan(A("R2"), A("one", 0, E), A("FC"), A("PH1", 1, 2), OP.add, OP.min)
+        dma("S", rows("CUM", R_CNT, 16 + V + L, 16), A("FO"), 69632)
+        dma("S", rows("CUM", R_RUN, 16 + V + L, 16), A("R2"), 69632)
+        dma("S", rows("CUM", R_NEXT, 15 + V + L, 15), A("R2"), 69632)
+        if rho == 0:
+            dma("S", rows("CUM", 0, 16 + V + L, 16), A("FO"), 69632)
+        if not last_round:
+            tag[0] = "posw"
+            act(IND(A("POS"), W("oUs")), H("PU", rho), AF.Silu)
         else:
-            ts(A("pm"), A("vF"), -1.0, OP.add)
-        for c in range(16):
-            ts(A("of2", c, L, 16), A("C256", 0, 16), A("nd", c, c + 1), OP.mult, A("pm", c, c + 1), OP.add)
-        ts(A("hit"), W("KI"), col(C_TH), OP.is_lt)
-        lin(W("w2", 5), A("hit"), float(L))
-        tt(W("w2", 6), W("w2", 5), A("lW"), OP.add)
-        cp(A("hU"), W("w2", 6))
-        tt(W("wh"), A("wW"), A("hit"), OP.mult)
-        lin(W("wh", 1), W("wh"), 40.0)
-        mm([(H("PN0"), A("BP"), A("g2"))])
-        cp(A("kUs"), H("PN0"))
-        tt(W("KDs"), W("sI", 1), W("DM", 3 * rho), OP.subtract)
-        tt(W("KDs", 1), A("vF"), W("DM", 3 * rho + 1), OP.subtract)
-        lin(W("w1", 2), A("pm"), None, 1.0)
-        ts(A("pU"), A("pm"), 1.0, OP.add)
-        tt(W("KDs", 2), W("w1", 2), W("DM", 3 * rho + 2), OP.subtract)
-        mm([(H("PN0"), A("ID"), A(z)), (H("PN0"), A("IN"), xs)])
-        lin(A("v2"), H("PN0"), 0.5, -0.25)
-        ts(A("cc"), H("PN0"), -2.0, OP.max, 2.0, OP.min)
-        rnd(A("vs"), A("v2"))
-        lowest("s", "vF", A("DM", 48 * rho, 48 * rho + 48), 3, "PN1", "PH0", W("wh", 1))
-        ts(W("oUs", 3), W("o2s", 2), 1.0, OP.add)
-        act(IND(A("DD"), W("oUs", 1)), PU, AF.Silu)
-        dma("S", A("DC"), rows("DD", 0, VV), 163840)
-        act(IND(A("FL", 0, V + L), W("oUs", 2)), PU, AF.Silu)
-        pick("g5", H("g4", 1), IND(A("FL"), W("oUs", 3)))
-        tt(IND(A("X"), W("oUs")), xs, A("vs"), OP.add)
-        act(A("DB"), A("DC"), AF.Relu, -91.0 - 2 * rho, 2.0)
-        scan(A("DS"), A("DB"), A("DB"), 0.0, OP.add, OP.max)
-        mm([(A("PH1", 0, 1), A("TRI"), A("DS", VV // 16 - 1, VV // 16))])
-        ts(A("DO"), A("DS"), A("PH1", 0, 1), OP.add)
-        dma("S", rows("CUM", rho, VV), A("DO"), 81920)
+            tag[0] = "fin"
+            dma("S", A("PU", 0, 272), rows(xt, R_HI, V + L), 139264)
+            dma("S", A("PU", 272, 544), rows(xt, R_LO, V + L), 139264)
+            lin(A("yr"), A("PU", 0, 544), nm="yr")
+            o = A(CFG["bank"][0], 0, 272)
+            mm([(o, A("I64"), A("PU", 0, 272)), (o, A("IN64"), A("yr", 0, 272)), (o, A("I32"), A("PU", 272, 544)), (o, A("IN"), A("yr", 272, 544))])
+            lin(A("DC", 0, 272), o, 2.0 ** 16, nm="yo")
+            dma("S", rows(xt2, 0, V + L), A("DC", 0, 272), 139264)
+        for x, h in halves:
+            tag[0] = "st2"
+            stage(x, h, XTw, "of2", xs(h, 512), CFG["st2"][rho], "k2")
+            tag[0] = "n"
+            tt(Wh("w1", h, 2), Wh("k2", h, 1), Wh("nd", h), OP.mult)
+            tt(Wh("aF", h), Wh("w1", h, 2), Wh("pm", h), OP.add)
+            cp(Wh("aU", h), Wh("aF", h))
+            lin(Hh("rr", h), IND(XTw, Wh("aU", h)), nm="rr")
+            o0, o1, zw = A("PN0", 0, HL), A("PN0", HL, 2 * HL), A("zw", 2 * HL * h, 2 * HL * h + 2 * HL)
+            mm([(o0, A("ID"), zh(h)), (o0, A("I288"), A("one", 0, HL)), (o1, A("IH"), zh(h))], True, False)
+            mm([(o0, A("IN"), Hh("rr", h)), (o1, A("IH"), Hh("rr", h))], False, True)
+            lin(zw, A("PN0", 0, 2 * HL), None, UP / 2 - 0.25, nm="zw")
+            act(Hh("S%d" % rho, h), IND(zw, Wh("hU", h)), AF.Abs, -UP)
+            send(rho, x)
+        sub[0] = ""
+        late = CFG["late"] and not last_round
+        if CFG["early"] or late:
+            tag[0] = "lown"
+            lin(A("g6"), IND(CUMw, A("aU")), nm="g6")
+        tag[0] = "mark"
+        lin(A("g4"), IND(CUMw, W("oUs", 1)), nm="g4")
+        mm([(W("PH1"), A("I32"), W("oFs", 1))], True, False)
+        mm(wrap(W("PH1"), "ZQ", "g4"), False, True)
+        tt(A("qF"), W("PH1"), W("DM", 6), OP.min)
+        ts(A("qU"), A("qF"), 1.0, OP.add)
+        cp(IND(A("MK"), A("qU")), A("g4"))
+        n = CFG["mk"]
+        for c in range(0, L, n):
+            o = A("PH1", 0, n)
+            for k in range(0, 16, 4):
+                mm([(o, A("MW", 128 * j, 128 * j + 128), A("MK", 16 * c + j, 16 * (c + n), 16)) for j in range(k, k + 4)], k == 0, k == 12)
+            lin(A("P1", 16 + c, 16 + c + n), o, nm="P1")
+            mm([(o, A("SD"), A("P1", 15 + c, 15 + c + n)), (o, A("ID"), A("P1", 16 + c, 16 + c + n))])
+            scan(A("sF", c, c + n), o, A("c16", 0, n), A("sF", c - 1, c) if c else col(C_R16), OP.add, OP.add)
+            cp(A("srn", c, c + n), A("sF", c, c + n))
         if not last_round:
-            act(IND(A("POS"), W("oUs")), PU, AF.Silu)
-            act(A("xsf"), IND(XTw, A("pU")))
-            mm([(H("PN1"), A("I32"), A("xsf")), (H("PN1"), A("ID"), A("vs"))])
-            act(A(xt, V, V + L), H("PN1"))
-            mm([(W("PH0"), A("BO"), A("hit"))])
-            red(col(C_HS), W("PH0"))
-            lin(col(C_A), col(C_HS), -1.0, float(L))
-            lin(col(C_TH), col(C_HS), -16.0, col(C_T0))
-        else:
-            act(A(xt, V, V + L), IND(XTw, A("pU")))
-            dma("S", A("ya", 0, 272), rows(xt, 0, V + L), 139264)
-            dma("S", A("ya", 272, 544), rows(xt, 1, V + L), 139264)
-            rnd(A("yr"), A("ya"))
-            o = A("PN1", 0, 272)
-            mm([(o, A("I32"), A("ya", 0, 272)), (o, A("IN"), A("yr", 0, 272)), (o, A("I32"), A("ya", 272, 544)), (o, A("IN"), A("yr", 272, 544))])
-            lin(A("yo"), o, 2.0 ** 18)
-            dma("S", rows(xt2, 0, V + L), A("yo"), 139264)
-        stage(XTw, "of2", "XR", CFG["na2"][rho], "KJ")
-        tt(W("w1", 3), W("KJ", 1), A("nd"), OP.mult)
-        tt(W("aF"), W("w1", 3), A("pm"), OP.add)
-        cp(A("aU"), W("aF"))
-        rnd(A("rr"), IND(XTw, A("aU")))
-        mm([(H("PN0"), A("ID"), A(z)), (H("PN0"), A("IN"), A("rr"))])
-        mm([(H("PN0", 1), A("IH"), A(z)), (H("PN0", 1), A("IH"), A("rr"))])
-        lin(H("zw"), H("PN0"), None, 128.0)
-        lin(H("zw", 1), H("PN0", 1), None, 127.75)
-        act(A("S%d" % rho), IND(A("zw"), A("hU")), AF.Abs, -128.0)
-        send(rho)
-        pick("g4", H("g4"), IND(A("CUM"), W("oUs", 1)))
-        mm(wrap(A("PH1", 0, 32), "ZB", "g4", 0, 2 * L))
-        lin(W("w2"), W("o2s", 1), None, 1.0)
-        tt(W("w2", 1), W("w2"), W("DN", 2), OP.subtract)
-        tt(W("w2", 2), W("w2", 1), W("PH1"), OP.subtract)
-        ts(W("w2", 3), W("PH1", 1), new, OP.is_lt)
-        tt(W("w2", 4), W("w2", 2), W("w2", 3), OP.mult)
-        tt(W("w2"), W("w2", 4), W("DN", 2), OP.add)
-        cp(A("qU"), W("w2"))
-        lin(A("g4f"), H("g4"), None, 32.0)
-        act(IND(A("MK"), A("qU")), A("g4f"), AF.Silu)
-        dma("S", A("MC"), rows("MK", rho, V), 131072)
-        lin(A("MB"), A("MC"), None, -32.0)
-        scan(A("MX"), A("MB"), A("MB"), 0.0, OP.max, OP.max)
-        ts(A("MR"), A("OH"), A("MX", L - 1, L), OP.mult)
-        mm([(W("PH1"), A("TRI"), A("MR"))])
-        red(col(C_MX), W("PH1"), OP.max)
-        ts(A("MO"), A("MX"), col(C_MX), OP.max)
-        dma("S", rows("MS", 0, V), A("MO"), 65536)
-        pick("g6", H("fr", 1), IND(A("FL"), A("aU")))
-        tt(H("fr"), IND(XTw, A("aU")), A("rr"), OP.subtract)
-        mm([(H("PS0"), A("ID"), A("rr")), (H("PS0"), A("ID"), A("cc"))])
-        mm([(H("PS1"), A("BO"), H("fr"))])
-        mm(wrap(A("PH0", 0, 32), "ZB", "fr", 0, 2 * L))
-        ts(W("wh", 3), W("PH0", 1), new, OP.is_lt)
-        tt(W("wh", 2), W("wh", 3), W("wh", 1), OP.mult)
-        ts(A("kUn"), H("PS1"), 2.0 ** 18, OP.mult)
-        lin(A("nF"), W("PH0"), 2.0 ** 18)
-        ts(A("vn"), H("PS0"), 0.0, OP.max, 63.0, OP.min)
-        tt(W("KDn"), A("nF"), W("DN"), OP.subtract)
+            dma("S", rows("MK", R_RUN, V), A("zerb"), 65536)
+        tag[0] = "dd"
+        if not by_place:
+            act(IND(A("DD"), W("oUs", 2)), H("MV", rho), AF.Silu)
+            dma("S", A("DC"), rows("DD", rho, VV), 163840)
+            scan(A("DS"), A("DC"), A("DC"), 0.0, OP.add, OP.max)
+            mm([(A("PH1", 0, 1), A("TRI"), A("DS", VV // 16 - 1, VV // 16))])
+            ts(A("DO"), A("DS"), A("PH1", 0, 1), OP.add, 1.0 / MARK, OP.mult)
+            dma("S", rows("CUM", rho, 16 + VV, 16), A("DO"), 81920)
+        tag[0] = "lown"
+        tt(A("fr"), IND(XTw, A("aU")), A("rr"), OP.subtract)
+        mm([(H("PN0"), A("ID"), A("rr")), (H("PN0"), A("ID"), A("cc"))])
+        ts(A("vn"), H("PN0"), 0.0, OP.max, 63.0, OP.min)
+        cp(A("kUn"), IND(A("NUM"), A("aU")))
+        mm(wrap(W("PK0"), "ZN", "fr"))
+        lin(W("Kn"), W("PK0"), nm="nF")
+        act(W("Kn", 1), A("aF"), AF.Relu)
         if not last_round:
-            act(W("aF", 1), W("aF"), AF.Relu)
-            tt(W("KDn", 1), W("aF", 1), W("DN", 1), OP.subtract)
-            mm([(H("PS0"), A("ID"), H("fr")), (H("PS0"), A("ID"), A("vn"))])
-            act(A("val"), H("PS0"))
-        lowest("n", "nF", A("DN", 0, 16 if last_round else 32), 1 if last_round else 2, "PS1", "PH0", W("wh", 2))
-        if not last_round:
-            cp(IND(A(xt), W("oUn", 1)), A("val"))
+            mm([(H("PN0"), A("ID"), A("fr")), (H("PN0"), A("ID"), A("vn"))])
+            lin(A("val"), H("PN0"), None, UP, nm="val")
+        nn = 1 if last_round else 2
+        lowest("n", 16, 1 if late else nn, W("DM", 1, 1 if late else nn), "PK1", wrap(W("PK1"), "ZX", "g6") if CFG["early"] else [])
+        tag[0] = "xw"
         cp(IND(A("X"), W("oUn")), A("vn"))
-        for h in range(4):
-            o = A(("PN1", "PN0")[h % 2], 0, 64)
-            mm([(o, A("I16"), A("C256", 64 * h, 64 * h + 64))] + wrap(o, "ZB", "MS", 1024 * h, 1024 * h + 1024))
-            ts(A("src", 64 * h, 64 * h + 64), o, rcol, OP.add)
+        if not CFG["early"]:
+            tt(IND(A("X"), W("oUs")), A("vs"), A("m128"), OP.add)
+        if not last_round and not late:
+            tag[0] = "xtn"
+            cp(IND(A(xt), W("oUn", 1)), A("val"))
+        tag[0] = "reo"
         if not last_round:
             xt, xt2 = xt2, xt
-            reorder(xt, A(xt2, 0, V + L))
+            reorder(xt, A(xt2, 0, V + L), "srn")
+            if late:
+                tag[0] = "xtn"
+                mm([(W("PH1"), A("I32"), W("Kn", 1)), (W("PH1"), A("IBIG"), A("lon"))] + wrap(W("PH1"), "ZY", "g6"))
+                tt(W("oFn", 1), W("PH1"), W("DM", 2), OP.min)
+                cp(W("oUn", 1), W("oFn", 1))
+                cp(IND(A(xt), W("oUn", 1)), A("val"))
         else:
             dma("S", ("raw", T.yx[:]), A("X", 0, V), 1 << 20)
             dma("S", ("raw", T.yz[:]), A("Z4"), 65536)
             for h in range(4):
-                (cp if h % 2 else act)(A("POS", 1024 * h, 1024 * h + 1024), IND(A(xt2, 0, V + L), A("src", 64 * h, 64 * h + 64)))
+                (cp if h % 2 else act)(A("POS", 1024 * h, 1024 * h + 1024), IND(A(xt2, 0, V + L), A("srn", 64 * h, 64 * h + 64)))
             dma("S", ("raw", T.yt[:]), rows("POS", 0, V), 131072)
 
     hist = {}
@@ -681,7 +887,7 @@ def rank_program(g, core, T, topo):
                     if (p["i"], free) not in seen:
                         seen.add((p["i"], free)); o["pre"].append((p, 0 if free else 1 if same else 2))
         if o["after"]:
-            o["pre"].append((o["after"], 0))
+            o["pre"].append((o["after"], 0 if o["q"] == "R" else 2))
         for kind in ("r", "w"):
             for x in o[kind]:
                 h = hist.setdefault(x[0], [])
@@ -689,9 +895,12 @@ def rank_program(g, core, T, topo):
                     h[:] = [y for y in h if not (x[1] <= y[2][1] and y[2][2] <= x[2])]
                 if not any(y[0] is o and y[1] == kind and y[2] == x for y in h[-3:]):
                     h.append((o, kind, x))
+        o["pre"].sort(key=lambda y: (y[0]["i"], y[1]))
     shape = tuple((o["q"], tuple(p["i"] for p, _ in o["pre"])) for o in ops)
+    ORDER["ops"] = ops
     if shape not in ORDER:
-        ORDER[shape] = arrange([o["q"] for o in ops], [o["work"] for o in ops], [[(p["i"], d) for p, d in o["pre"]] for o in ops])
+        ORDER[shape] = arrange([o["q"] for o in ops], [o["work"] for o in ops], [[(p["i"], d) for p, d in o["pre"]] for o in ops],
+                               [o["tag"] for o in ops], [o["fine"] for o in ops], [o["lap"] for o in ops])
     count, known = {}, {q: {} for q in Q}
     for o in [ops[i] for i in ORDER[shape]]:
         q = o["q"]

@@ -7,33 +7,33 @@ VV = V + RO * L
 RATIO = 1.875
 MARK = 512
 UP = 192.0
-ST_V = "%sVDFa0 %sVDFa1 %sVABa0 {} %sVABa1 %sVDFa4 {} %sVDFa5 %sVDFa6 %sVDFa7 "
-ST_A = "%sAGAa2 %sAGAa3 {} %sAABa2 %sAABa4 %sAABa3 {} %sAABa5 %sAABa6 %sAABa7 "
-TAIL_V = ("lowsVkUs lowsVE#1:16 " + (ST_V % (("st2",) * 8)).format("lowsVoFs lowsVoUs", "") + "xsVX foldVFS foldVR1 foldVFO foldVR2 "
-          "nVaUa lownVkUn lownVE#1:16 lownVfr lownVvn markVMK")
-TAIL_A = "valsAvs " + (ST_A % (("st2",) * 8)).format("foldAFL", "") + "valsAXT nArra nAzwa nASa markAg4 lownAg6 ddADD poswAPO"
-CFG = {"war": True, "nh": 1, "late": True, "st1": ["AAAAAAbb"] + ["rrAAbbbb"] * 3, "st2": ["rrAAbbbb"] * 4, "early": True, "g1v": True, "tbv": True,
-       "reo": 512, "mk": 128, "onV": ["sq"], "bank": ("PH0", "PS1"),
-       "line": {"V": "-xwVX uVuFa " + (ST_V % (("st1",) * 8)).format("-ddVDS", "-ddVDO") + "sVmUa -xtnVXT " + TAIL_V,
-                "A": "-reoAXT#1:4 " + (ST_A % (("st1",) * 8)).format("-reoAXT#5", "-reoAXT#6") + "-reoAXT#7:8 sAXRa#1:2 sAg3a " + TAIL_A},
-       "first": {"V": "pos0VPO#1:8 st10VDFa6 st10VDFa7 pos0VPO#9:16 " + TAIL_V,
-                 "A": "st10AGAa0 st10AGAa1 st10AABa0 st10AABa6 reo0AXT#1:4 st10AGAa2 st10AABa1 st10AABa7 st10AGAa3 st10AABa2 st10AGAa4 "
-                      "st10AABa3 st10AGAa5 st10AABa4 st10AABa5 reo0AXT#5:8 sAXRa#1:2 sAg3a " + TAIL_A},
-       "seed": 1, "steps": 190000, "reach": 5, "heat": 400.0, "cool": 30.0, "share": 0.6, "margin": 4000.0,
-       "plans": [(0.88, 1.56, 3.8, 0.6, 130.0, 70.0, 1300.0, 3200.0, 1.0)]}
+TAIL_V = ("lowsVkUs lowsVE#1:4 st2VDFa0 lowsVoFs lowsVoUs st2VDFa1 st2VABa0 st2VDFa5 st2VDFa6 st2VDFa7 foldVFS foldVR1 foldVFO "
+          "foldVR2 xsVX nVaUa lownVkUn lownVE#1:2 markVMK lownVE#3:4 lownVfr lownVvn")
+TAIL_A = ("sAXRa#1:2 sAg3a valsAvs st2AGAa2 foldAFL st2AGAa3 st2AABa2 st2AGAa4 st2AABa3 st2AABa5 st2AABa4 st2AABa6 st2AABa7 valsAXT markAg4 "
+          "nArra nAzwa nASa lownAg6 ddADD poswAPO")
+CFG = {"war": True, "nh": 1, "st1": ["A2A2 A2A2 A2A2 A2A2"] + ["r2r2 A2A2 r2r2 A2b2"] * 3, "st2": ["r2r2 A2A2 A2b2 b2b2"] * 4,
+       "g1v": True, "tbv": True, "bys": True, "byn": True, "tbn": True, "zw2": True, "pe2": False, "posA": [], "gfold": False, "gdd": False,
+       "cut": [64], "reo": 512, "mk": 256, "onV": ["pl", "sF"], "bank": ("PH0", "PS1"),
+       "line": {"V": "-xwVX uVuFa st1VDFa0 st1VDFa1 st1VABa0 st1VDFa4 -ddVDS st1VDFa5 st1VABa4 st1VDFa7 -ddVDO sVmUa -xtnVXT " + TAIL_V,
+                "A": "-reoAXT#1:4 st1AGAa2 st1AGAa3 st1AABa2 -reoAXT#5 st1AGAa6 st1AABa3 -reoAXT#6 st1AABa7 st1AABa6 -reoAXT#7:8 " + TAIL_A},
+       "first": {"V": "pos0VPO#1:16 " + TAIL_V,
+                 "A": "st10AGAa0 st10AGAa1 st10AABa0 st10AGAa2 reo0AXT#1:4 st10AABa1 st10AGAa3 st10AABa2 st10AGAa4 st10AABa3 st10AGAa5 "
+                      "st10AABa4 st10AGAa6 st10AABa5 st10AGAa7 st10AABa6 st10AABa7 reo0AXT#5:8 " + TAIL_A},
+       "fix": 10, "gdma": 2000, "more": 0, "again": 120.0, "seed": 1, "steps": 170000, "reach": 5, "heat": 800.0, "cool": 20.0, "share": 0.6, "margin": 4000.0,
+       "plans": [(0.9, 1.56, 3.8, 0.5, 180.0, 150.0, 1400.0, 3500.0, 0.6), (0.96, 1.56, 3.8, 0.55, 120.0, 60.0, 1800.0, 4000.0, 0.4)]}
 
-F32, BF, I32, U16 = "float32", "bfloat16", "int32", "uint16"
+F32, BF, I32, U16, F16 = "float32", "bfloat16", "int32", "uint16", "float16"
 BIG = {
     "X": (V + L, BF), "XTa": (V + 2 * L, F32), "XTb": (V + 2 * L, F32), "POS": (V + L, F32), "FL": (V + L, F32),
-    "DD": (VV, F32), "CUM": (16 + VV, BF), "MK": (V + 16 + L, BF), "MW": (2048, BF), "DF": (V, BF), "AB": (V, BF),
-    "E": (2176, BF), "NUM": (V, F32), "GA": (1024, BF), "XR": (5 * L, BF), "PU": (3 * L, F32), "MV": (RO * L, F32),
+    "DD": (VV, F32), "CUM": (16 + VV, BF), "MK": (V + 2 * L, BF), "DF": (V, BF), "AB": (V, BF),
+    "E": (2176, BF), "NUM": (V, F32), "GA": (1024, BF), "XR": (5 * L, BF), "PU": (4 * L, F32), "KI": (1920, BF), "MV": (RO * L, F32),
     "Z0": (4 * L, BF), "Z1": (4 * L, BF), "Z2": (4 * L, BF), "Z3": (4 * L, BF), "Z4": (L, BF),
     "S0": (L, BF), "S1": (L, BF), "S2": (L, BF), "S3": (L, BF),
 }
 SMALL = {
     "tsb": (L, I32), "tsf": (L, F32), "tsh": (L, BF), "tsu": (L, U16), "tsd": (2 * L, BF), "src": (L, U16),
     "C256": (L, BF), "PA": (L, BF), "PB": (L, BF), "PM": (L, BF), "pI": (2, I32), "pF": (4, F32), "kI": (2, I32), "tI": (2, I32),
-    "OH": (16, F32), "ZB": (144, BF), "Z16": (144, BF), "Z32": (144, BF), "ZM16": (144, BF), "ZU": (144, BF), "ZC": (144, BF),
+    "OH": (16, F32), "ZB": (144, BF), "Z256": (144, BF), "Z512": (144, BF), "ZM256": (144, BF), "Z16": (144, BF), "Z32": (144, BF), "ZM16": (144, BF), "ZU": (144, BF), "ZC": (144, BF),
     "ZN": (144, BF), "ZQ": (144, BF), "ZX": (144, BF), "ZY": (144, BF), "BO": (128, BF), "ID": (128, BF), "IN": (128, BF), "IH": (128, BF),
     "IBIG": (128, BF), "IDG": (128, BF), "IN64": (128, BF), "I288": (128, BF), "I32": (128, F32), "I64": (128, F32),
     "BO32": (128, F32), "TRI": (128, BF), "SH": (128, BF), "SD": (128, BF), "one": (272, BF), "m128": (L, BF),
@@ -43,17 +43,17 @@ SMALL = {
     "wW": (16, F32), "DM": (128, F32), "uF": (16, F32), "sq": (16, F32), "uI": (16, I32), "bF": (16, F32), "hI": (2 * L, I32),
     "off": (L, U16), "of2": (L, U16), "K1": (64, F32), "K3": (48, F32), "k1": (32, I32), "k2": (32, I32),
     "mU": (16, U16), "hit": (16, BF), "hU": (16, U16), "g1": (L, BF), "g1f": (L, F32), "g1s": (L, F32), "g3": (L, BF), "g4": (L, BF),
-    "g6": (L, BF), "w1": (64, F32), "sI": (32, I32), "sU": (16, U16), "vU": (16, U16), "pm": (16, F32),
-    "dI": (32, I32), "nd": (16, F32), "wh": (16, F32), "kUs": (L, U16), "kUn": (L, U16), "TBs": (L, BF), "TBn": (L, BF), "TS": (L, BF),
-    "los": (16, BF), "lon": (16, BF), "Ks": (48, F32), "Kn": (32, F32), "oFs": (48, F32), "oFn": (32, F32),
-    "oUs": (48, U16), "oUn": (32, U16), "qF": (16, F32), "qU": (16, U16), "aF": (16, F32), "aU": (16, U16),
+    "g6": (L, BF), "w1": (64, F32), "sI": (32, I32), "sU": (16, U16), "vU": (16, U16), "pm": (16, F16 if CFG["pe2"] else F32),
+    "dI": (32, I32), "nd": (16, BF if CFG["pe2"] else F32), "wh": (16, F32), "kUs": (L, U16), "kUn": (L, U16), "TBs": (L, BF), "TBn": (L, BF), "TS": (L, BF),
+    "los": (16, BF), "lon": (16, BF), "Ks": (48, F32), "Kn": (32, F32), "oFs": (48, F32), "oFn": (48, F32),
+    "oUs": (48, U16), "oUn": (32, U16), "qF": (48, F32), "qU": (16, U16), "aF": (16, F32), "aU": (16, U16),
     "zw": (2 * L, BF), "cc": (L, BF), "vs": (L, BF), "rr": (L, BF), "vn": (L, BF), "fr": (L, BF), "val": (L, F32),
     "DC": (VV // 16, F32), "DS": (VV // 16, BF), "DO": (VV // 16, BF),
-    "FC": (272, F32), "FS": (272, BF), "FO": (272, BF), "R1": (272, BF), "R2": (272, BF), "P1": (16 + L, BF), "sF": (L, F32),
-    "srn": (L, U16), "zero": (VV // 16, F32), "zerb": (L, BF), "c16": (L, F32), "yr": (544, BF),
+    "FB": (272, BF), "DB": (VV // 16, BF), "gone": (16, BF), "BW": (128, BF), "BN": (128, BF), "IDh": (128, F16), "FC": (272, F32), "FS": (272, BF), "FO": (272, BF), "R1": (272, BF), "R2": (272, BF), "P1": (16 + 272, BF), "TI": (128, BF), "TX": (128, BF), "I272": (128, F32), "qI": (16, I32), "sF": (L, F32),
+    "srn": (L, U16), "zero": (VV // 16, F32), "zerb": (272, BF), "c16": (L, F32), "yr": (544, BF),
 }
 PS = ["PK0", "PK1", "PH0", "PH1", "PN0", "PN1", "PS0", "PS1"]
-POOL = {F32: "sf", BF: "sb", I32: "si", U16: "su"}
+POOL = {F32: "sf", BF: "sb", I32: "si", U16: "su", F16: "sh"}
 PLACE, FILL = {}, {d: 0 for d in POOL}
 for _k, (_n, _d) in SMALL.items():
     PLACE[_k] = (POOL[_d], FILL[_d])
@@ -85,7 +85,7 @@ def width(a):
 
 
 def short(*xs):
-    return 0.5 if all(DTYPE[a[1]] in (BF, U16) for a in xs if a[0] == "ap") else 1.0
+    return 0.5 if all(DTYPE[a[1]] in (BF, U16, F16) for a in xs if a[0] == "ap") else 1.0
 
 
 def arrange(queue, work, pre, tags, fine, lap):
@@ -101,7 +101,7 @@ def arrange(queue, work, pre, tags, fine, lap):
         pre[i] = keep
     plans = []
     for cy, gg, ss, pe, x, own, dm, rem, weight in CFG["plans"]:
-        cost = [1.0 + w[0] + cy * (max(64, w[1]) * (w[1] > 0) + w[2] + gg * w[3] + ss * w[4]) + pe * w[5] for w in work]
+        cost = [1.0 + w[0] + cy * (max(64, w[1] + CFG["fix"]) * (w[1] > 0) + w[2] + gg * w[3] + ss * w[4]) + pe * w[5] for w in work]
         lat = [(0.0, dm + w[7] / 200.0, rem - 1000.0)[w[6]] for w in work]
         plans.append((cost, lat, [[(p, lat[p] + (0.0, own, x)[d]) for p, d in pre[i]] for i in range(n)], weight))
     cost, lat, edges, _ = plans[0]
@@ -230,8 +230,14 @@ def arrange(queue, work, pre, tags, fine, lap):
 
     cur, rs = score(order)
     best, cand = (cur, order), [arcs(r) for r in rs]
-    for it in range(CFG["steps"]):
+    for it in range(CFG["steps"] + CFG["more"]):
         heat = CFG["heat"] * (CFG["cool"] / CFG["heat"]) ** (it / CFG["steps"])
+        if it >= CFG["steps"]:
+            if it == CFG["steps"]:
+                order = best[1]
+                cur, rs = score(order)
+                cand = [arcs(r) for r in rs]
+            heat = CFG["again"] * (CFG["cool"] / CFG["again"]) ** ((it - CFG["steps"]) / CFG["more"])
         k = int(draw() * len(use))
         u, v = cand[k][int(draw() * len(cand[k]))]
         prev, back, far = rs[k][2], draw() < 0.5, 1 + int(draw() ** 2 * CFG["reach"])
@@ -325,6 +331,11 @@ def rank_program(g, core, T, topo):
         ops.append({"q": q, "fn": fn, "w": spans(w), "r": spans(r), "sem": sem, "cnt": cnt, "work": work, "after": after, "i": len(ops),
                     "lap": lap[0], "tag": tag[0], "fine": tag[0] + q + (called(out[0]) if out and tag[0] != "set" else "") + sub[0]})
 
+    def glue(n):
+        part = [ops.pop() for _ in range(n)][::-1]
+        ops.append(dict(part[0], fn=[p["fn"] for p in part], w=[x for p in part for x in p["w"]], r=[x for p in part for x in p["r"]], cnt=n,
+                        work=(0, 0, sum(max(64, p["work"][1] + CFG["fix"]) + p["work"][2] for p in part), 0, 0, 0, 0, 0)))
+
     def vwork(o, a, k, fix=50):
         if o[0] == "ind":
             return (fix, 0, 0, 0, width(o), 0, 0, 0)
@@ -405,7 +416,7 @@ def rank_program(g, core, T, topo):
     def dma(q, o, i, nbytes=0, after=None, **kw):
         sem = "d%d" % nd[0]; nd[0] += 1
         add(q, lambda: Q[q].dma_start(real(o), real(i), **kw), [o], [i] + ([o] if kw else []),
-            (1000 if q == "G" else 100, 0, 0, 0, 0, 0, 1, nbytes), sem, 16, after)
+            (CFG["gdma"] if q == "G" else 100, 0, 0, 0, 0, 0, 1, nbytes), sem, 16, after)
         return ops[-1]
 
     def rows(name, r, c1, c0=0):
@@ -428,9 +439,8 @@ def rank_program(g, core, T, topo):
             lin(col(c), e(r), float(w), col(c) if k else None)
 
     def spread(z, c0):
-        for n in (128, 256):
-            if n >= HL:
-                gcopy(A(z, c0 + n, c0 + 2 * n), A(z, c0, c0 + n))
+        for n in (256, 512)[:1 + ("4" in "".join(CFG["st1"] + CFG["st2"]))]:
+            gcopy(A(z, c0 + n, c0 + 2 * n), A(z, c0, c0 + n))
 
     dma("S", A("tsb"), ("raw", T.ts[:]), 131072)
     xload = dma("A", A("X", 0, V), ("raw", T.xr[:]), 1 << 20)
@@ -482,15 +492,15 @@ def rank_program(g, core, T, topo):
     lin(A("ZU"), A("ZB"), col(C_W))
     lin(col(C_A), pcol, 0.0, -0.375)
     act(A("kR"), W("PH1"))
-    lin(A("Z16"), A("ZB"), 16.0)
-    if "r" in "".join(CFG["st1"] + CFG["st2"]):
-        lin(A("Z32"), A("ZB"), 32.0)
-        lin(A("ZM16"), A("ZB"), -16.0)
+    for nm, w in (("Z16", 16), ("Z32", 32), ("ZM16", -16), ("Z256", 256), ("Z512", 512), ("ZM256", -256)):
+        lin(A(nm), A("ZB"), float(w))
     lin(A("IN"), A("ID"), -1.0)
-    lin(A("IH"), A("ID"), 0.5)
-    lin(A("IBIG"), A("ID"), 8192.0)
-    lin(A("I288"), A("ID"), 288.0)
-    lin(A("I64"), A("ID"), 64.0)
+    iota(A("t5"), [[0, 128]])
+    for nm, w in (("IH", 0.5), ("IBIG", 8192.0), ("I64", 64.0), ("I272", 272.0)):
+        add("G", lambda nm=nm, w=w: g.affine_select(real(A(nm)), real(A("t5")), [[-1, 128]], OP.not_equal, w, 0, 1), [A(nm)], [A("t5")],
+            (170, 0, 256, 0, 0, 0, 0, 0))
+    if not CFG["zw2"]:
+        lin(A("I288"), A("ID"), 288.0)
     iota(A("m128"), [[0, L]], -128)
     iota(A("zero"), [[0, VV // 16]])
     for k in range(RO):
@@ -501,8 +511,8 @@ def rank_program(g, core, T, topo):
     select(A("G8", p1=8), A("G8", p1=8), [[1, 8], [0, 16]], OP.is_equal, 0, -1)
     cp(A("thF", 0, 1, p1=8), A("tI", 0, 1, p1=8))
     mm([(A("PH1", 0, 1), A("G8", p1=8), A("thF", 0, 1, p1=8))])
-    lin(col(C_TH), A("PH1", 0, 1), 16.0, 16.0)
-    lin(col(C_T0), col(C_TH), None, 4096.0)
+    lin(col(C_TH), A("PH1", 0, 1), 256.0, 256.0)
+    lin(col(C_T0), col(C_TH), None, 256.0 * L)
     if CFG["g1v"] or CFG["tbv"]:
         ts(A("MSK"), A("PA"), rcol, OP.is_equal)
         lin(A("MS4"), A("MSK"), 0.4)
@@ -517,13 +527,14 @@ def rank_program(g, core, T, topo):
     weights(C_C, ((0, -1), (1, -1), (2, -1)))
     weights(C_N, ((R_HI, 1 << 22), (R_LO, 1 << 16)))
     weights(C_G, ((R_HI, 1), (R_LO, 1)))
-    weights(C_Q, ((R_NEXT, 8192), (R_CNT, -1)))
-    if CFG["early"]:
-        weights(C_X, ((R_RUN, 8192),))
-        lin(A("ZX"), A("ZB"), col(C_X))
-    if CFG["late"]:
-        weights(C_Y, ((R_RUN, 8192), (R_CNT, -1)))
-        lin(A("ZY"), A("ZB"), col(C_Y))
+    weights(C_Q, ((R_NEXT, 272 << 17), (R_CNT, -272)))
+    weights(C_Y, ((R_RUN, 8192), (R_CNT, -1)))
+    lin(A("ZY"), A("ZB"), col(C_Y))
+    if CFG["pe2"]:
+        cp(A("IDh"), A("ID"))
+        for k in range(0, 15, 3):
+            iota(A("KI", 128 * k, 128 * k + 384), [[1, 3], [0, 128]], k + 1)
+            select(A("KI", 128 * k, 128 * k + 384), A("KI", 128 * k, 128 * k + 384), [[0, 3], [-1, 128]], OP.is_equal, 0, 1)
     lin(A("ZC"), A("ZB"), col(C_C))
     lin(A("ZN"), A("ZB"), col(C_N))
     lin(A("ZQ"), A("ZB"), col(C_Q))
@@ -538,12 +549,12 @@ def rank_program(g, core, T, topo):
     tt(row(10), row(7), row(7), OP.mult)
     red(col(C_WR), row(9))
     lin(A("wW"), row(10), col(C_WR))
-    for k, w in enumerate((V, V, V + L, V, V, V + 2 * L, V + 15)):
+    for k, w in enumerate((V, V, V + L, V, V, V + 2 * L, V + L - 272)):
         iota(W("ro", k), [[16, 16]], w)
     iota(W("ro", 7), [[0, NH], [16, CW]])
     ts(A("DM"), A("ro"), rcol, OP.add)
     select(A("TRI"), A("BO"), [[1, 128]], OP.is_gt, 0, -1)
-    iota(A("PU"), [[0, 3 * L]], 32)
+    iota(H("PU", 0, 3), [[0, 3 * L]], 32)
     for k, (r, pat, base) in enumerate(((14, [[1, 3], [0, L]], 46), (0, [[0, 48], [1, 16]], 32), (13, [[0, 3], [1, 16], [0, 16]], 32))):
         o = A("XTb", L * 3 * k, L * (3 + 3 * k), p1=8)
         iota(o, pat, base)
@@ -552,17 +563,17 @@ def rank_program(g, core, T, topo):
     iota(A("PK", p1=8), [[0, L]], MARK)
     for k in range(RO):
         dma("S", rows("MV", k, L * k + L, L * k), A("PK", p1=8), 8192)
-    select(A("t2", 0, 128), A("BO"), [[1, 128]], OP.is_ge, 0, -1)
-    dma("S", A("MW"), A("CUM", 0, 2048), 1 << 19, after=xload)
-    dma("S", rows("MW", R_RUN, 2048), A("t2", 0, 128), 32768)
-    lin(A("t5"), A("BO"), e(15))
-    tt(A("SD"), A("t5"), A("ID"), OP.subtract)
+    select(A("TI"), A("BO"), [[1, 128]], OP.is_ge, 0, -1)
+    select(A("TX"), A("BO"), [[-1, 128]], OP.is_gt, 0, 1)
     iota(A("P1", 0, 16), [[0, 16]])
-    dma("S", A("MK", 0, V), A("CUM", 0, V), 1 << 20, after=xload)
-    zeros("MK", V, V + 16 + L)
-    for c in range(0, V, 512):
+    for c in range(0, V, 512) if CFG["bys"] or CFG["byn"] else ():
         iota(A("NUM", c, c + 512), [[1, 512]], c)
-    iota(A("zerb"), [[0, L]])
+    if not CFG["bys"]:
+        lin(A("BW"), A("BO"), col(C_W))
+    if not CFG["byn"]:
+        lin(A("BN"), A("BO"), col(C_N))
+    iota(A("zerb"), [[0, 272]])
+    dma("S", rows("MK", R_RUN, V + L), A("zerb"), 69632)
     iota(A("c16"), [[0, L]], 16)
     lin(col(C_R16), rcol, None, -16.0)
     iota(A("t1", 0, 48), [[0, 48]], L)
@@ -573,42 +584,46 @@ def rank_program(g, core, T, topo):
         for c in range(0, V, n):
             lin(A(dst, c, c + n), IND(srcw, A(lst, c // 16, (c + n) // 16)), None, bias, nm=lst + str(c // n))
 
-    def stage(x, h, win, off, ref, modes, key):
-        for q in range(4 // NH):
-            out, c0 = A("PK%d" % (q % 2), 0, 64), 16 * HL * h + 1024 * q
-            for k in (2 * q, 2 * q + 1):
+    def stage(x, h, win, off, ref, modes, key, w):
+        c, k, turn, blocks = 0, 0, 0, modes.split()
+        for q, block in enumerate(blocks):
+            c0 = c
+            for mode, n in zip(block[::2], [L * int(d) for d in block[1::2]]):
                 sub[0] = x + str(k)
-                c = 16 * HL * h + 512 * k
-                o, ab, df = A(off, c // 16, c // 16 + 32), A("AB", c, c + 512), A("DF", c, c + 512)
-                if modes[k] == "A":
-                    ga, pb = A("GA", 512 * (k % 2), 512 * (k % 2) + 512), A("PS%d" % (k % 2 if NH == 1 else 0))
+                o, ab, df = A(off, c // 16, (c + n) // 16), A("AB", c, c + n), A("DF", c, c + n)
+                if mode == "A":
+                    ga, pb = A("GA", 512 * turn, 512 * turn + n), A("PS%d" % turn, 0, n)
+                    turn = 1 - turn
                     act(ga, IND(win, o))
-                    mm([(pb, A("ID"), ga), (pb, A("IN"), ref)])
+                    mm([(pb, A("ID"), ga), (pb, A("IN"), ref(h, n))])
                     act(ab, pb, AF.Abs)
                 else:
-                    tt(df, IND(win, o), ref, OP.subtract)
-                    if modes[k] == "r":
+                    tt(df, IND(win, o), ref(h, n), OP.subtract)
+                    if mode == "r":
                         ts(ab, df, 0.0, OP.max)
                     else:
                         act(ab, df, AF.Abs)
-            first = [(out, A("ID"), A("PM", 64 * q, 64 * q + 64))]
-            if modes[2 * q] == "r":
-                mm(first + wrap(out, "ZM16", "DF", c0, c0 + 1024), True, False)
-                mm(wrap(out, "Z32", "AB", c0, c0 + 1024), False, True)
+                c, k = c + n, k + 1
+            n = (c - c0) // 16
+            out = A("PK%d" % (q % 2), 0, n)
+            first = [(out, A("ID"), A("PM" if w == 16 else "C256", c0 // 16, c // 16))]
+            if mode == "r":
+                mm(first + wrap(out, "ZM%d" % w, "DF", c0, c), True, False)
+                mm(wrap(out, "Z%d" % (2 * w), "AB", c0, c), False, True)
             else:
-                mm(first + wrap(out, "Z16", "AB", c0, c0 + 1024))
+                mm(first + wrap(out, "Z%d" % w, "AB", c0, c))
             if q == 0:
                 lin(A("K1"), out, nm="K1")
-            else:
-                tt(A("K1"), out, A("K1"), OP.min)
+            elif n > 16:
+                tt(A("K1", 0, n), out, A("K1", 0, n), OP.min)
         sub[0] = x
         tt(A("K3", 0, 32), A("K1", 0, 32), A("K1", 32, 64), OP.min)
-        if NH == 1:
+        if n > 16:
             tt(W(key), A("K3", 0, 16), A("K3", 16, 32), OP.min)
         else:
             tt(A("K3", 32, 48), A("K3", 0, 16), A("K3", 16, 32), OP.min)
-            tt(Wh(key, h), A("K3", 32, 40), A("K3", 40, 48), OP.min)
-        ts(Wh(key, h, 1), Wh(key, h), 15, OP.bitwise_and)
+            tt(W(key), out, A("K3", 32, 48), OP.min)
+        ts(W(key, 1), W(key), w - 1, OP.bitwise_and)
 
     def lowest(x, key, n, dm, bank, more):
         o = 0
@@ -619,8 +634,9 @@ def rank_program(g, core, T, topo):
                 ts(A("E", o, o + w), A("kU" + x, 16 * c, L), A("K" + x, key + c, key + c + 1), OP.is_equal, A("wh", c, c + 1), OP.mult)
                 terms.append((A("PN1", 16 * c, L), A("BO"), A("E", o, o + w)))
                 o += w
+            glue(4)
             mm(terms, h == 0, h == 3)
-        if CFG["tbv"]:
+        if CFG["tbv" if x == "s" else "tbn"]:
             tt(A("TB" + x), H("PN1"), A("MS4"), OP.mult)
             scan(A("TS"), A("KEEP"), A("TB" + x), 0.0, OP.mult, OP.add)
             tt(A("lo" + x), A("TS", 15, L, 16), A("wh"), OP.is_ge)
@@ -643,7 +659,7 @@ def rank_program(g, core, T, topo):
         used = topo.engines(sc, T.cores[fr[0]]) if fr else []
         pool, lst = (used, fr) if dst in fr else ([k for k in topo.engines(sc, T.cores[dst]) if k not in used], nr)
         n = 1
-        while 2 * n * len(lst) <= len(pool):
+        while 2 * n * max(len(lst), len(fr)) <= len(pool):
             n *= 2
         k = lst.index(dst)
         return pool[k * n:(k + 1) * n]
@@ -676,22 +692,27 @@ def rank_program(g, core, T, topo):
         zh = lambda h, n=HL: A(z, 512 * h, 512 * h + n)
         xs = lambda h, n=HL: A("XR", XS * h + HL, XS * h + HL + n)
         kv = 1 if rho == 0 else 2
+        mid = 2047.0 if CFG["pe2"] else 0.0
         lap[0] = rho
         for (x, h), bank in zip(halves, CFG["bank"]):
             tag[0], sub[0] = "u", x
             mm(wrap(A(bank, 0, CW), "ZU", z, 512 * h, 512 * h + HL))
             spread(z, 512 * h)
-            cp(Wh("uF", h), A(bank, 0, CW))
             if "sq" in CFG["onV"]:
+                cp(Wh("uF", h), A(bank, 0, CW))
                 tt(Wh("sq", h), A(bank, 0, CW), Wh("uF", h), OP.mult)
             else:
-                act(Wh("sq", h), Wh("uF", h), AF.Square)
+                act(Wh("sq", h), A(bank, 0, CW), AF.Square)
+                cp(Wh("uF", h), A(bank, 0, CW))
             ts(Wh("uI", h), Wh("sq", h), 1.0 / 32, OP.mult, col(C_A), OP.add)
             cp(Wh("bF", h), Wh("uI", h))
             for c in range(CW * h, CW * h + CW):
                 ts(A("hI", HL * h + c % CW, HL * h + HL, CW), A("kR"), A("uF", c, c + 1), OP.mult, A("bF", c, c + 1), OP.add)
-            ts(Hh("hI", h, 1), Hh("hI", h), V - 1, OP.bitwise_and)
-            cp(Hh("off", h), Hh("hI", h, 1))
+                if c % 4 == 3:
+                    glue(4)
+            for c0, c1 in zip([0] + CFG["cut"], CFG["cut"] + [HL]):
+                ts(A("hI", L + HL * h + c0, L + HL * h + c1), A("hI", HL * h + c0, HL * h + c1), V - 1, OP.bitwise_and)
+                cp(A("off", HL * h + c0, HL * h + c1), A("hI", L + HL * h + c0, L + HL * h + c1))
         sub[0] = ""
         if rho == 0:
             tag[0] = "src0"
@@ -699,7 +720,11 @@ def rank_program(g, core, T, topo):
             cp(A("src"), H("PN1"))
             tag[0] = "pos0"
             for k in range(16):
-                ts(IND(A("POS", 0, V), W("tsu", k)), A("PI"), 1.0, OP.mult, 32.0 + k, OP.add)
+                if k in CFG["posA"]:
+                    lin(H("PU", 3), A("PI"), None, 32.0 + k)
+                    act(IND(A("POS", 0, V), W("tsu", k)), H("PU", 3), AF.Silu)
+                else:
+                    ts(IND(A("POS", 0, V), W("tsu", k)), A("PI"), 1.0, OP.mult, 32.0 + k, OP.add)
             tag[0] = "reo0"
             reorder(xt, Xw, "src", UP)
             for c in (0, V // 2):
@@ -707,22 +732,14 @@ def rank_program(g, core, T, topo):
                     accum_op=OP.add, max_dma_last_dim=8192)
         for x, h in halves:
             tag[0] = "st1" if rho else "st10"
-            stage(x, h, Xw, "off", zh(h, 512), CFG["st1"][rho], "k1")
+            stage(x, h, Xw, "off", zh, CFG["st1"][rho], "k1", 256)
         for (x, h), bank in zip(halves, CFG["bank"]):
             tag[0], sub[0] = "s", x
             p8 = lambda k=0: A(bank, CW * k, CW * k + CW)
             cp(Wh("mU", h), Wh("k1", h, 1))
-            if CFG["g1v"]:
-                tt(Hh("g1f", h), IND(A("kR"), Wh("mU", h)), A("MSK", 0, HL), OP.mult)
-                scan(Hh("g1s", h), A("KEEP", 0, HL), Hh("g1f", h), 0.0, OP.mult, OP.add)
-                tt(Wh("w1", h), A("g1s", HL * h + 15, HL * h + HL, 16), Wh("uF", h), OP.mult)
-            else:
-                lin(Hh("g1", h), IND(A("KT"), Wh("mU", h)), nm="g1")
-                mm(wrap(p8(), "ZB", "g1", HL * h, HL * h + HL))
-                tt(Wh("w1", h), p8(), Wh("uF", h), OP.mult)
-            tt(Wh("sI", h), Wh("w1", h), Wh("uI", h), OP.add)
-            ts(Wh("sI", h, 1), Wh("sI", h), V - 1, OP.bitwise_and)
-            cp(Wh("sU", h), Wh("sI", h, 1))
+            tt(A("g1f"), IND(H("hI", 1), A("mU")), A("MSK"), OP.mult)
+            scan(A("g1s"), A("KEEP"), A("g1f"), 0.0, OP.mult, OP.add)
+            cp(A("sU"), A("g1s", 15, L, 16))
             lin(A("XR", XS * h, XS * h + HL), IND(A("POS", 0, V), Wh("sU", h)), col(C_P), nm="g2")
             lin(xs(h), IND(Xw, Wh("sU", h)), None, UP, nm="xs")
             mm(wrap(A(bank, 0, 2 * CW), "ZU", "XR", XS * h, XS * h + 2 * HL))
@@ -734,11 +751,21 @@ def rank_program(g, core, T, topo):
             ts(Wh("dI", h, 1), Wh("dI", h), 15, OP.bitwise_and)
             ts(Wh("nd", h), Wh("dI", h, 1), -1.0, OP.mult, -1.0, OP.add)
             if rho > 0:
+                lin(W("w1"), W("Ks", kv), None, -1.0 - mid)
                 mm(wrap(p8(), "ZC", "g3", HL * h, HL * h + HL))
-                tt(Wh("Ks", h, 1), p8(), Wh("Ks", h, kv), OP.add)
-            ts(Wh("pm", h), Wh("Ks", h, 1), -1.0, OP.add)
-            for c in range(CW * h, CW * h + CW):
+                tt(A("pm"), p8(), W("w1"), OP.add)
+                lin(W("Ks", 1), A("pm"), None, 1.0 + mid, nm="pl")
+            else:
+                ts(Wh("pm", h), Wh("Ks", h, 1), -1.0 - mid, OP.add)
+            if CFG["pe2"]:
+                for pb, k0, n in ((bank, 0, 4), ("PK1", 4, 4), ("PK0", 8, 8)):
+                    mm([(W(pb, k), A("KI", 128 * k - 128, 128 * k), A("nd")) for k in range(max(k0, 1), k0 + n)], True, False)
+                    mm([(W(pb, k), A("IDh"), A("pm")) for k in range(k0, k0 + n)], False, True)
+                    ts(W("of2", k0, n), W(pb, k0, n), mid, OP.add)
+            for c in range(CW * h, CW * h + CW) if not CFG["pe2"] else ():
                 ts(A("of2", HL * h + c % CW, HL * h + HL, CW), A("C256", 0, 16), A("nd", c, c + 1), OP.mult, A("pm", c, c + 1), OP.add)
+                if c % 4 == 3:
+                    glue(4)
             tag[0] = "hit"
             ts(Wh("hit", h), Wh("k1", h), col(C_TH), OP.is_lt, float(HL), OP.mult)
             tt(Wh("w1", h, 1), Wh("hit", h), Wh("DM", h, 7), OP.add)
@@ -750,7 +777,7 @@ def rank_program(g, core, T, topo):
             mm([(W("PN0"), A("BO"), A("hit"))])
             red(col(C_HS), W("PN0"))
             lin(col(C_A), col(C_HS), -1.0 / HL, L - 0.375)
-            lin(col(C_TH), col(C_HS), -16.0 / HL, col(C_T0))
+            lin(col(C_TH), col(C_HS), -256.0 / HL, col(C_T0))
         tag[0] = "vals"
         mm([(Hh("PN0", h, k), A(m), r) for _, h in halves for k, m, r in ((0, "ID", zh(h)), (0, "IN", xs(h)), (1, "IH", zh(h)), (1, "IH", xs(h)))])
         lin(A("vs"), H("PN0", 1), None, 128.0 - UP / 2 - 0.25)
@@ -759,22 +786,26 @@ def rank_program(g, core, T, topo):
         lin(A(xt, V, V + L), H("PN0"), None, UP - 128.0, nm="app")
         tag[0] = "lows"
         tt(A("wh"), A("wW"), A("hit"), OP.mult)
-        cp(W("Ks"), W("sI", 1))
-        cp(A("kUs"), IND(A("NUM"), A("sU")))
+        lin(W("Ks"), A("g1s", 15, L, 16), nm="sF")
+        if CFG["bys"]:
+            cp(A("kUs"), IND(A("NUM"), A("sU")))
+        else:
+            mm([(H("PN1"), A("BW"), H("XR"))])
+            cp(A("kUs"), H("PN1"))
         ns = 2 if by_place else 3
-        lowest("s", 0, ns, W("DM", 3 if rho == 2 else 0, ns), "PH1", [])
-        if CFG["early"]:
-            tag[0] = "xs"
-            tt(IND(A("X"), W("oUs")), A("vs"), A("m128"), OP.add)
+        lowest("s", 0 if CFG["bys"] else 16 * kv, ns, W("DM", 3 if rho == 2 else 0, ns), "PH1", [])
+        tag[0] = "xs"
+        tt(IND(A("X"), W("oUs")), A("vs"), A("m128"), OP.add)
         tag[0] = "fold"
         E = (V + L) // 16
         act(IND(A("FL"), W("oUs", 1)), H("MV", rho), AF.Silu)
-        dma("S", A("FC"), rows("FL", rho, V + L), 139264)
-        scan(A("FS"), A("FC"), A("FC"), 0.0, OP.add, OP.max)
-        scan(A("R1"), A("one", 0, E), A("FC"), 0.0, OP.add, OP.min)
+        FC = A("FB" if CFG["gfold"] else "FC")
+        dma("G" if CFG["gfold"] else "S", FC, rows("FL", rho, V + L), 69632 if CFG["gfold"] else 139264)
+        scan(A("FS"), FC, FC, 0.0, OP.add, OP.max)
+        scan(A("R1"), A("one", 0, E), FC, 0.0, OP.add, OP.min)
         mm([(A("PH1", 0, 1), A("TRI"), A("FS", E - 1, E)), (A("PH1", 1, 2), A("SH"), A("R1", E - 1, E))])
         ts(A("FO"), A("FS"), A("PH1", 0, 1), OP.add, 1.0 / MARK, OP.mult)
-        scan(A("R2"), A("one", 0, E), A("FC"), A("PH1", 1, 2), OP.add, OP.min)
+        scan(A("R2"), A("one", 0, E), FC, A("PH1", 1, 2), OP.add, OP.min)
         dma("S", rows("CUM", R_CNT, 16 + V + L, 16), A("FO"), 69632)
         dma("S", rows("CUM", R_RUN, 16 + V + L, 16), A("R2"), 69632)
         dma("S", rows("CUM", R_NEXT, 15 + V + L, 15), A("R2"), 69632)
@@ -794,46 +825,55 @@ def rank_program(g, core, T, topo):
             dma("S", rows(xt2, 0, V + L), A("DC", 0, 272), 139264)
         for x, h in halves:
             tag[0] = "st2"
-            stage(x, h, XTw, "of2", xs(h, 512), CFG["st2"][rho], "k2")
+            stage(x, h, XTw, "of2", xs, CFG["st2"][rho], "k2", 16)
             tag[0] = "n"
             tt(Wh("w1", h, 2), Wh("k2", h, 1), Wh("nd", h), OP.mult)
             tt(Wh("aF", h), Wh("w1", h, 2), Wh("pm", h), OP.add)
-            cp(Wh("aU", h), Wh("aF", h))
+            ts(Wh("aU", h), Wh("aF", h), mid, OP.add)
             lin(Hh("rr", h), IND(XTw, Wh("aU", h)), nm="rr")
             o0, o1, zw = A("PN0", 0, HL), A("PN0", HL, 2 * HL), A("zw", 2 * HL * h, 2 * HL * h + 2 * HL)
-            mm([(o0, A("ID"), zh(h)), (o0, A("I288"), A("one", 0, HL)), (o1, A("IH"), zh(h))], True, False)
-            mm([(o0, A("IN"), Hh("rr", h)), (o1, A("IH"), Hh("rr", h))], False, True)
-            lin(zw, A("PN0", 0, 2 * HL), None, UP / 2 - 0.25, nm="zw")
+            if CFG["zw2"]:
+                o1 = H("PH0")
+                mm([(o0, A("ID"), zh(h))], True, False)
+                mm([(o1, A("IH"), zh(h))], True, False)
+                mm([(o0, A("IN"), Hh("rr", h))], False, True)
+                mm([(o1, A("IH"), Hh("rr", h))], False, True)
+                lin(H("zw"), o0, None, 2 * UP)
+                ts(H("zw", 1), o1, UP / 2 - 0.25, OP.add)
+            else:
+                mm([(o0, A("ID"), zh(h)), (o0, A("I288"), A("one", 0, HL)), (o1, A("IH"), zh(h))], True, False)
+                mm([(o0, A("IN"), Hh("rr", h)), (o1, A("IH"), Hh("rr", h))], False, True)
+                lin(zw, A("PN0", 0, 2 * HL), None, UP / 2 - 0.25, nm="zw")
             act(Hh("S%d" % rho, h), IND(zw, Wh("hU", h)), AF.Abs, -UP)
             send(rho, x)
         sub[0] = ""
-        late = CFG["late"] and not last_round
-        if CFG["early"] or late:
-            tag[0] = "lown"
-            lin(A("g6"), IND(CUMw, A("aU")), nm="g6")
+        tag[0] = "lown"
+        lin(A("g6"), IND(CUMw, A("aU")), nm="g6")
         tag[0] = "mark"
         lin(A("g4"), IND(CUMw, W("oUs", 1)), nm="g4")
-        mm([(W("PH1"), A("I32"), W("oFs", 1))], True, False)
+        mm([(W("PH1"), A("I272"), W("oFs", 1))], True, False)
         mm(wrap(W("PH1"), "ZQ", "g4"), False, True)
-        tt(A("qF"), W("PH1"), W("DM", 6), OP.min)
-        ts(A("qU"), A("qF"), 1.0, OP.add)
+        ts(A("qI"), W("PH1"), 1.0 / (16 * E), OP.mult, -13.0 / 32, OP.add)
+        ts(W("qF"), A("qI"), 1.0 - 16 * E, OP.mult)
+        tt(W("qF", 1), W("PH1"), W("qF"), OP.add)
+        tt(W("qF", 2), W("qF", 1), W("DM", 6), OP.min)
+        ts(A("qU"), W("qF", 2), float(E), OP.add)
         cp(IND(A("MK"), A("qU")), A("g4"))
+        dma("S", A("P1", 16, 16 + E), rows("MK", R_RUN, 16 * E), 69632)
         n = CFG["mk"]
         for c in range(0, L, n):
             o = A("PH1", 0, n)
-            for k in range(0, 16, 4):
-                mm([(o, A("MW", 128 * j, 128 * j + 128), A("MK", 16 * c + j, 16 * (c + n), 16)) for j in range(k, k + 4)], k == 0, k == 12)
-            lin(A("P1", 16 + c, 16 + c + n), o, nm="P1")
-            mm([(o, A("SD"), A("P1", 15 + c, 15 + c + n)), (o, A("ID"), A("P1", 16 + c, 16 + c + n))])
+            mm([(o, A("TI"), A("P1", 16 + c, 16 + c + n)), (o, A("TX"), A("P1", 15 + c, 15 + c + n))])
             scan(A("sF", c, c + n), o, A("c16", 0, n), A("sF", c - 1, c) if c else col(C_R16), OP.add, OP.add)
             cp(A("srn", c, c + n), A("sF", c, c + n))
         if not last_round:
-            dma("S", rows("MK", R_RUN, V), A("zerb"), 65536)
+            dma("S", rows("MK", R_RUN, 16 * E), A("zerb"), 69632)
         tag[0] = "dd"
         if not by_place:
             act(IND(A("DD"), W("oUs", 2)), H("MV", rho), AF.Silu)
-            dma("S", A("DC"), rows("DD", rho, VV), 163840)
-            scan(A("DS"), A("DC"), A("DC"), 0.0, OP.add, OP.max)
+            DC = A("DB" if CFG["gdd"] else "DC")
+            dma("G" if CFG["gdd"] else "S", DC, rows("DD", rho, VV), 81920 if CFG["gdd"] else 163840)
+            scan(A("DS"), DC, DC, 0.0, OP.add, OP.max)
             mm([(A("PH1", 0, 1), A("TRI"), A("DS", VV // 16 - 1, VV // 16))])
             ts(A("DO"), A("DS"), A("PH1", 0, 1), OP.add, 1.0 / MARK, OP.mult)
             dma("S", rows("CUM", rho, 16 + VV, 16), A("DO"), 81920)
@@ -841,32 +881,32 @@ def rank_program(g, core, T, topo):
         tt(A("fr"), IND(XTw, A("aU")), A("rr"), OP.subtract)
         mm([(H("PN0"), A("ID"), A("rr")), (H("PN0"), A("ID"), A("cc"))])
         ts(A("vn"), H("PN0"), 0.0, OP.max, 63.0, OP.min)
-        cp(A("kUn"), IND(A("NUM"), A("aU")))
+        if CFG["byn"]:
+            cp(A("kUn"), IND(A("NUM"), A("aU")))
+        else:
+            mm([(H("PN1"), A("BN"), A("fr"))])
+            cp(A("kUn"), H("PN1"))
         mm(wrap(W("PK0"), "ZN", "fr"))
         lin(W("Kn"), W("PK0"), nm="nF")
-        act(W("Kn", 1), A("aF"), AF.Relu)
+        act(W("Kn", 1), A("aF"), AF.Relu, mid)
         if not last_round:
             mm([(H("PN0"), A("ID"), A("fr")), (H("PN0"), A("ID"), A("vn"))])
             lin(A("val"), H("PN0"), None, UP, nm="val")
-        nn = 1 if last_round else 2
-        lowest("n", 16, 1 if late else nn, W("DM", 1, 1 if late else nn), "PK1", wrap(W("PK1"), "ZX", "g6") if CFG["early"] else [])
+        mm([(W("PS0"), A("I32"), W("Kn", 1))] + wrap(W("PS0"), "ZY", "g6"))
+        tt(W("w1", 3), W("PS0"), W("DM", 2), OP.min)
+        ts(A("gone"), W("w1", 3), float(V), OP.is_ge)
+        lowest("n", 16 if CFG["byn"] else 0, 1, W("DM", 1), "PK1", [(W("PK1"), A("IBIG"), A("gone"))])
         tag[0] = "xw"
         cp(IND(A("X"), W("oUn")), A("vn"))
-        if not CFG["early"]:
-            tt(IND(A("X"), W("oUs")), A("vs"), A("m128"), OP.add)
-        if not last_round and not late:
-            tag[0] = "xtn"
-            cp(IND(A(xt), W("oUn", 1)), A("val"))
         tag[0] = "reo"
         if not last_round:
             xt, xt2 = xt2, xt
             reorder(xt, A(xt2, 0, V + L), "srn")
-            if late:
-                tag[0] = "xtn"
-                mm([(W("PH1"), A("I32"), W("Kn", 1)), (W("PH1"), A("IBIG"), A("lon"))] + wrap(W("PH1"), "ZY", "g6"))
-                tt(W("oFn", 1), W("PH1"), W("DM", 2), OP.min)
-                cp(W("oUn", 1), W("oFn", 1))
-                cp(IND(A(xt), W("oUn", 1)), A("val"))
+            tag[0] = "xtn"
+            tt(W("oFn", 1), A("lon"), W("DM", 2), OP.mult)
+            tt(W("oFn", 2), W("oFn", 1), W("w1", 3), OP.max)
+            cp(W("oUn", 1), W("oFn", 2))
+            cp(IND(A(xt), W("oUn", 1)), A("val"))
         else:
             dma("S", ("raw", T.yx[:]), A("X", 0, V), 1 << 20)
             dma("S", ("raw", T.yz[:]), A("Z4"), 65536)
@@ -927,8 +967,9 @@ def rank_program(g, core, T, topo):
             for s, c in list(p["kn"].items()) + [p["tok"]]:
                 kn[s] = max(kn.get(s, 0), c)
         o["kn"] = dict(kn)
-        ins = o["fn"]()
-        if ins is not None:
-            ins.then_inc(T.sem[sem], o["cnt"])
+        for fn in o["fn"] if isinstance(o["fn"], list) else [o["fn"]]:
+            ins = fn()
+            if ins is not None:
+                ins.then_inc(T.sem[sem], 1 if isinstance(o["fn"], list) else o["cnt"])
     for s, c in count.items():
         g.wait_ge(T.sem[s], c)

import math
from concourse.bass import DstId, RemoteDMATransfer
from concourse.mybir import AluOpType as OP, AxisListType, ActivationFunctionType as AF

V, L, RO = 4096, 256, 4
VV = V + RO * L
RATIO = 1.875
MARK = 512
UP = 192.0
TAIL_V = ("lowsVkUs lowsVE#1:4 st2VDFa0 lowsVoFs lowsVoUs st2VDFa1 st2VABa0 st2VDFa5 st2VDFa6 st2VDFa7 foldVFS foldVR1 foldVFO "
          "foldVR2 xsVX nVaUa lownVkUn lownVE#1:2 markVMK lownVE#3:4 lownVfr lownVvn")
TAIL_A = ("sAXRa#1:2 sAg3a valsAvs st2AGAa2 foldAFL st2AGAa3 st2AABa2 st2AGAa4 st2AABa3 st2AABa5 st2AABa4 st2AABa6 st2AABa7 valsAXT markAg4 "
          "nArra nAzwa nASa lownAg6 ddADD poswAPO")
CFG = {"war": True, "nh": 1, "st1": ["A2A2 A2A2 A2A2 A2A2"] + ["r2r2 A2A2 r2r2 A2b2"] * 3, "st2": ["r2r2 A2A2 A2b2 b2b2"] * 4,
       "g1v": True, "tbv": True, "bys": True, "byn": True, "tbn": True, "zw2": True, "pe2": False, "posA": [], "gfold": False, "gdd": False,
       "cut": [64], "reo": 512, "mk": 256, "onV": ["pl", "sF"], "bank": ("PH0", "PS1"),
       "line": {"V": "-xwVX uVuFa st1VDFa0 st1VDFa1 st1VABa0 st1VDFa4 -ddVDS st1VDFa5 st1VABa4 st1VDFa7 -ddVDO sVmUa -xtnVXT " + TAIL_V,
                "A": "-reoAXT#1:4 st1AGAa2 st1AGAa3 st1AABa2 -reoAXT#5 st1AGAa6 st1AABa3 -reoAXT#6 st1AABa7 st1AABa6 -reoAXT#7:8 " + TAIL_A},
       "first": {"V": "pos0VPO#1:16 " + TAIL_V,
                 "A": "st10AGAa0 st10AGAa1 st10AABa0 st10AGAa2 reo0AXT#1:4 st10AABa1 st10AGAa3 st10AABa2 st10AGAa4 st10AABa3 st10AGAa5 "
                      "st10AABa4 st10AGAa6 st10AABa5 st10AGAa7 st10AABa6 st10AABa7 reo0AXT#5:8 " + TAIL_A},
       "fix": 10, "gdma": 2000, "more": 0, "again": 120.0, "seed": 1, "steps": 170000, "reach": 5, "heat": 800.0, "cool": 20.0, "share": 0.6, "margin": 4000.0,
       "plans": [(0.9, 1.56, 3.8, 0.5, 180.0, 150.0, 1400.0, 3500.0, 0.6), (0.96, 1.56, 3.8, 0.55, 120.0, 60.0, 1800.0, 4000.0, 0.4)]}

F32, BF, I32, U16, F16 = "float32", "bfloat16", "int32", "uint16", "float16"
BIG = {
    "X": (V + L, BF), "XTa": (V + 2 * L, F32), "XTb": (V + 2 * L, F32), "POS": (V + L, F32), "FL": (V + L, F32),
    "DD": (VV, F32), "CUM": (16 + VV, BF), "MK": (V + 2 * L, BF), "DF": (V, BF), "AB": (V, BF),
    "E": (2176, BF), "NUM": (V, F32), "GA": (1024, BF), "XR": (5 * L, BF), "PU": (4 * L, F32), "KI": (1920, BF), "MV": (RO * L, F32),
    "Z0": (4 * L, BF), "Z1": (4 * L, BF), "Z2": (4 * L, BF), "Z3": (4 * L, BF), "Z4": (L, BF),
    "S0": (L, BF), "S1": (L, BF), "S2": (L, BF), "S3": (L, BF),
}
SMALL = {
    "tsb": (L, I32), "tsf": (L, F32), "tsh": (L, BF), "tsu": (L, U16), "tsd": (2 * L, BF), "src": (L, U16),
    "C256": (L, BF), "PA": (L, BF), "PB": (L, BF), "PM": (L, BF), "pI": (2, I32), "pF": (4, F32), "kI": (2, I32), "tI": (2, I32),
    "OH": (16, F32), "ZB": (144, BF), "Z256": (144, BF), "Z512": (144, BF), "ZM256": (144, BF), "Z16": (144, BF), "Z32": (144, BF), "ZM16": (144, BF), "ZU": (144, BF), "ZC": (144, BF),
    "ZN": (144, BF), "ZQ": (144, BF), "ZX": (144, BF), "ZY": (144, BF), "BO": (128, BF), "ID": (128, BF), "IN": (128, BF), "IH": (128, BF),
    "IBIG": (128, BF), "IDG": (128, BF), "IN64": (128, BF), "I288": (128, BF), "I32": (128, F32), "I64": (128, F32),
    "BO32": (128, F32), "TRI": (128, BF), "SH": (128, BF), "SD": (128, BF), "one": (272, BF), "m128": (L, BF),
    "MSK": (L, BF), "MS4": (L, BF), "KEEP": (L, BF),
    "G8": (128, F32), "row": (176, F32), "col": (32, F32), "ro": (128, F32), "kR": (16, F32), "kB": (16, BF), "thF": (2, F32),
    "kD": (48, F32), "KT": (16, BF), "PI": (L, F32), "PK": (L, F32), "t1": (L, BF), "t2": (L, BF), "t5": (128, BF),
    "wW": (16, F32), "DM": (128, F32), "uF": (16, F32), "sq": (16, F32), "uI": (16, I32), "bF": (16, F32), "hI": (2 * L, I32),
    "off": (L, U16), "of2": (L, U16), "K1": (64, F32), "K3": (48, F32), "k1": (32, I32), "k2": (32, I32),
    "mU": (16, U16), "hit": (16, BF), "hU": (16, U16), "g1": (L, BF), "g1f": (L, F32), "g1s": (L, F32), "g3": (L, BF), "g4": (L, BF),
    "g6": (L, BF), "w1": (64, F32), "sI": (32, I32), "sU": (16, U16), "vU": (16, U16), "pm": (16, F16 if CFG["pe2"] else F32),
    "dI": (32, I32), "nd": (16, BF if CFG["pe2"] else F32), "wh": (16, F32), "kUs": (L, U16), "kUn": (L, U16), "TBs": (L, BF), "TBn": (L, BF), "TS": (L, BF),
    "los": (16, BF), "lon": (16, BF), "Ks": (48, F32), "Kn": (32, F32), "oFs": (48, F32), "oFn": (48, F32),
    "oUs": (48, U16), "oUn": (32, U16), "qF": (48, F32), "qU": (16, U16), "aF": (16, F32), "aU": (16, U16),
    "zw": (2 * L, BF), "cc": (L, BF), "vs": (L, BF), "rr": (L, BF), "vn": (L, BF), "fr": (L, BF), "val": (L, F32),
    "DC": (VV // 16, F32), "DS": (VV // 16, BF), "DO": (VV // 16, BF),
    "FB": (272, BF), "DB": (VV // 16, BF), "gone": (16, BF), "BW": (128, BF), "BN": (128, BF), "IDh": (128, F16), "FC": (272, F32), "FS": (272, BF), "FO": (272, BF), "R1": (272, BF), "R2": (272, BF), "P1": (16 + 272, BF), "TI": (128, BF), "TX": (128, BF), "I272": (128, F32), "qI": (16, I32), "sF": (L, F32),
    "srn": (L, U16), "zero": (VV // 16, F32), "zerb": (272, BF), "c16": (L, F32), "yr": (544, BF),
}
PS = ["PK0", "PK1", "PH0", "PH1", "PN0", "PN1", "PS0", "PS1"]
POOL = {F32: "sf", BF: "sb", I32: "si", U16: "su", F16: "sh"}
PLACE, FILL = {}, {d: 0 for d in POOL}
for _k, (_n, _d) in SMALL.items():
    PLACE[_k] = (POOL[_d], FILL[_d])
    FILL[_d] += (_n + 15) // 16 * 16
SCRATCH = {k: ("sbuf", [128, n], d) for k, (n, d) in BIG.items()}
SCRATCH.update({POOL[d]: ("sbuf", [128, n], d) for d, n in FILL.items()})
SCRATCH.update({k: ("psum", [128, 512], F32) for k in PS})
DTYPE = {k: v[2] for k, v in SCRATCH.items()}
NDMA = 64
SEMAPHORES = (["eV", "eA", "eP", "eG"] + ["d%d" % i for i in range(NDMA)]
              + [s + h + str(i) for s in ("arr", "snt") for h in "ab" for i in range(RO)])
ORDER = {}


def A(name, c0=0, c1=None, st=1, p0=0, p1=128, ps=1):
    if c1 is None:
        c1 = BIG[name][0] if name in BIG else SMALL[name][0] if name in SMALL else 512
    if name in PLACE:
        name, c0, c1 = PLACE[name][0], c0 + PLACE[name][1], c1 + PLACE[name][1]
    return ("ap", name, c0, c1, st, p0, p1, ps)


def IND(win, off):
    return ("ind", win, off)


def width(a):
    return 16 * (a[2][3] - a[2][2]) if a[0] == "ind" else (a[3] - a[2] + a[4] - 1) // a[4]


def short(*xs):
    return 0.5 if all(DTYPE[a[1]] in (BF, U16, F16) for a in xs if a[0] == "ap") else 1.0


def arrange(queue, work, pre, tags, fine, lap):
    n = len(queue)
    above = [0] * n
    for i in range(n):
        far = 0
        for p, _ in pre[i]:
            far |= above[p]
        keep = [(p, d) for p, d in pre[i] if not far >> p & 1 or work[p][6]]
        for p, _ in pre[i]:
            above[i] |= above[p] | 1 << p
        pre[i] = keep
    plans = []
    for cy, gg, ss, pe, x, own, dm, rem, weight in CFG["plans"]:
        cost = [1.0 + w[0] + cy * (max(64, w[1] + CFG["fix"]) * (w[1] > 0) + w[2] + gg * w[3] + ss * w[4]) + pe * w[5] for w in work]
        lat = [(0.0, dm + w[7] / 200.0, rem - 1000.0)[w[6]] for w in work]
        plans.append((cost, lat, [[(p, lat[p] + (0.0, own, x)[d]) for p, d in pre[i]] for i in range(n)], weight))
    cost, lat, edges, _ = plans[0]
    post = [[] for _ in range(n)]
    for i in range(n):
        for p, d in edges[i]:
            post[p].append((i, d))
    ORDER["graph"] = (cost, lat, edges, cost)
    seen, at, twin = {}, {}, []
    for i in range(n):
        k = seen[fine[i], lap[i]] = seen.get((fine[i], lap[i]), 0) + 1
        at.setdefault((fine[i], k), [-1] * (RO + 1))[lap[i]] = i
        twin.append(at[fine[i], k] if tags[i] != "set" else [])
    extra = [[] for _ in range(n)]
    for q in CFG["line"]:
        chain = []
        for r in range(RO + 1):
            for w in CFG["line" if r else "first"][q].split():
                nm, _, ks = w.lstrip("-").partition("#")
                a, _, b = (ks or "1").partition(":")
                chain += [at.get((nm, k), [-1] * (RO + 1))[r - (w[0] == "-")] for k in range(int(a), int(b or a) + 1)]
        chain = [i for i in chain if i >= 0]
        for a, b in zip(chain, chain[1:]):
            extra[b].append((a, 0.0))

    def ordered(key, ed):
        done, out = [False] * n, []
        for i in sorted(range(n), key=lambda j: (key[j], j)):
            stack = [i]
            while stack:
                j = stack[-1]
                todo = [p for p, _ in ed[j] if not done[p]]
                if todo and not done[j]:
                    assert len(stack) < 20 * n, (fine[j], lap[j], [fine[p] for p in todo])
                    stack += sorted(todo, key=lambda p: -key[p])
                    continue
                stack.pop()
                if not done[j]:
                    done[j] = True
                    out.append(j)
        return out

    both = [edges[i] + extra[i] for i in range(n)]
    key = [0.0] * n
    for i in ordered(key, both):
        key[i] = max([0.0] + [key[p] + cost[p] + d for p, d in both[i]])
    ORDER["asap"] = max(key)
    for i in reversed(range(n)):
        if tags[i] == "set" and post[i]:
            key[i] = min(key[j] - d - cost[i] + (CFG["margin"] if tags[j] == "set" else 0.0) for j, d in post[i]) - CFG["margin"]
    order = ordered(key, edges)

    qn = {q: k for k, q in enumerate(sorted(set(queue)))}
    qi = [qn[q] for q in queue]
    flat = [(c, [c[i] + la[i] for i in range(n)], [tuple((p, c[p] + d) for p, d in ed[i]) for i in range(n)], w) for c, la, ed, w in plans]
    up, down = [tuple(p for p, _ in edges[i]) for i in range(n)], [tuple(p for p, _ in post[i]) for i in range(n)]
    seed, low = [CFG["seed"]], [0]

    def draw():
        seed[0] = (seed[0] * 1103515245 + 12345) % 2147483648
        return seed[0] / 2147483648.0

    def run(order, plan, a=0, old=None):
        c, full, ed, _ = plan
        free, who = [0.0] * len(qn), [-1] * len(qn)
        if old is None or a < 50:
            a, st, why, prev = 0, [0.0] * n, [-1] * n, [-1] * n
        else:
            why, prev, st, left = old[1][:], old[2][:], old[4][:], len(qn)
            for k in range(a - 1, -1, -1):
                i = order[k]
                if who[qi[i]] < 0:
                    who[qi[i]], free[qi[i]], left = i, st[i] + c[i], left - 1
                    if not left:
                        break
        end, last = 0.0, -1
        for i in order[a:]:
            q = qi[i]
            s = free[q]
            w = prev[i] = who[q]
            for p, d in ed[i]:
                x = st[p] + d
                if x > s:
                    s, w = x, p
            st[i] = s
            why[i] = w
            free[q] = s + c[i]
            who[q] = i
            x = s + full[i]
            if x > end:
                end, last = x, i
        return end, why, prev, last, st

    def arcs(res):
        r, i = [], res[3]
        while i >= 0:
            w = res[1][i]
            if w >= 0 and w == res[2][i] and not above[i] >> w & 1:
                r.append((w, i))
            i = w
        return r

    def move(order, mover, target, back):
        a, b = order.index(target), order.index(mover)
        if (a < b) != back:
            return False
        if not back:
            a, b = b, a
        part, tied, tq = order[a:b + 1], {mover}, set()
        for x in (part[-2::-1] if back else part[1:]):
            if qi[x] in tq or not tied.isdisjoint(down[x] if back else up[x]):
                if qi[x] == qi[mover]:
                    return False
                tied.add(x)
                tq.add(qi[x])
        w, o = [x for x in part if x in tied], [x for x in part if x not in tied]
        order[a:b + 1] = w + o if back else o + w
        low[0] = min(low[0], a)
        return True

    use = [p for p in flat if p[3]]

    def score(order, a=0, old=None):
        rs = [run(order, p, min(a, n - 150), old and old[k]) for k, p in enumerate(use)]
        return sum(r[0] * p[3] for r, p in zip(rs, use)), rs

    cur, rs = score(order)
    best, cand = (cur, order), [arcs(r) for r in rs]
    for it in range(CFG["steps"] + CFG["more"]):
        heat = CFG["heat"] * (CFG["cool"] / CFG["heat"]) ** (it / CFG["steps"])
        if it >= CFG["steps"]:
            if it == CFG["steps"]:
                order = best[1]
                cur, rs = score(order)
                cand = [arcs(r) for r in rs]
            heat = CFG["again"] * (CFG["cool"] / CFG["again"]) ** ((it - CFG["steps"]) / CFG["more"])
        k = int(draw() * len(use))
        u, v = cand[k][int(draw() * len(cand[k]))]
        prev, back, far = rs[k][2], draw() < 0.5, 1 + int(draw() ** 2 * CFG["reach"])
        mover, target = (v, u) if back else (u, v)
        if back:
            for _ in range(far - 1):
                if prev[target] >= 0 and not above[v] >> prev[target] & 1:
                    target = prev[target]
        elif far > 1:
            a = order.index(v)
            for x in [x for x in order[a:a + 60] if qi[x] == qi[v]][:far]:
                if above[x] >> u & 1:
                    break
                target = x
        new, low[0] = list(order), n
        if not move(new, mover, target, back):
            continue
        if draw() < CFG["share"]:
            for m2, t2 in zip(twin[mover], twin[target]):
                if m2 >= 0 and t2 >= 0 and m2 != mover:
                    move(new, m2, t2, back)
        s, r2 = score(new, low[0], rs)
        if s <= cur or draw() < math.exp((cur - s) / heat):
            order, cur, rs, cand = new, s, r2, [arcs(r) for r in r2]
            if s < best[0]:
                best = (s, order)
    ORDER["end"] = [run(best[1], p)[0] for p in flat]
    return best[1]


def rank_program(g, core, T, topo):
    rank = T.rank_of(core)
    if rank is None:
        return
    N = len(T.cores)
    B = L // N
    NH = CFG["nh"]
    HL = L // NH
    CW, XS = HL // 16, HL + 512
    own = rank * B // HL
    halves = (("a", own), ("b", 1 - own))[:NH]
    Q = {"V": g.vector, "A": g.scalar, "P": g.tensor, "G": g, "S": g.sync}
    ops, tag, sub, lap = [], ["set"], [""], [0]

    def called(a):
        a = a[1] if a[0] == "ind" else a
        if a[0] == "raw":
            return "out"
        if a[1] not in POOL.values():
            return a[1][:2] if a[1][0] not in "SZ" else a[1][0]
        return max((c, k) for k, (p, c) in PLACE.items() if p == a[1] and c <= a[2])[1]

    def real(a):
        if not isinstance(a, tuple):
            return a
        if a[0] == "ind":
            return real(a[1]).indirect(real(a[2]))
        if a[0] == "raw":
            return a[1]
        _, n, c0, c1, st, p0, p1, ps = a
        rows = slice(p0, p1) if ps == 1 else slice(p0, p1, ps)
        cols = slice(c0, c1) if st == 1 else slice(c0, c1, st)
        return T[n][rows, cols]

    def spans(xs):
        r = []
        for a in xs:
            if isinstance(a, tuple) and a[0] == "ap":
                r.append((a[1], 0, 512, 1, 0, 1) if a[1] in PS else (a[1], a[2], a[3], a[4], a[5], a[7]))
        return r

    def meet(x, y):
        if x[1] >= y[2] or y[1] >= x[2]:
            return False
        if x[3] == y[3] and (x[1] - y[1]) % x[3]:
            return False
        return not (x[4] - y[4]) % min(x[5], y[5])

    def add(q, fn, out, ins, work, sem=None, cnt=1, after=None):
        w, r = [], []
        for o in out:
            if o[0] == "ind":
                w.append(o[1]); r.append(o[2])
            else:
                w.append(o)
        for i in ins:
            if isinstance(i, tuple) and i[0] == "ind":
                r += [i[1], i[2]]
            else:
                r.append(i)
        ops.append({"q": q, "fn": fn, "w": spans(w), "r": spans(r), "sem": sem, "cnt": cnt, "work": work, "after": after, "i": len(ops),
                    "lap": lap[0], "tag": tag[0], "fine": tag[0] + q + (called(out[0]) if out and tag[0] != "set" else "") + sub[0]})

    def glue(n):
        part = [ops.pop() for _ in range(n)][::-1]
        ops.append(dict(part[0], fn=[p["fn"] for p in part], w=[x for p in part for x in p["w"]], r=[x for p in part for x in p["r"]], cnt=n,
                        work=(0, 0, sum(max(64, p["work"][1] + CFG["fix"]) + p["work"][2] for p in part), 0, 0, 0, 0, 0)))

    def vwork(o, a, k, fix=50):
        if o[0] == "ind":
            return (fix, 0, 0, 0, width(o), 0, 0, 0)
        if a[0] == "ind":
            return (fix, 0, 0, width(o), 0, 0, 0, 0)
        return (0, width(o) * k, 0, 0, 0, 0, 0, 0)

    def cp(o, i):
        add("V", lambda: g.vector.tensor_copy(real(o), real(i)), [o], [i], vwork(o, i, short(o, i)))

    def tt(o, a, b, op):
        add("V", lambda: g.vector.tensor_tensor(real(o), real(a), real(b), op), [o], [a, b], vwork(o, a, 1 if a[1] in PS or b[1] in PS else 2))

    def ts(o, a, s1, op0, s2=None, op1=None):
        if op1 is None:
            add("V", lambda: g.vector.tensor_scalar(real(o), real(a), real(s1), None, op0), [o], [a, s1], vwork(o, a, short(o, a)))
        else:
            add("V", lambda: g.vector.tensor_scalar(real(o), real(a), real(s1), real(s2), op0, op1), [o], [a, s1, s2], vwork(o, a, short(o, a)))

    def ms(o, c):
        add("V", lambda: g.vector.memset(real(o), c), [o], [], vwork(o, o, short(o)))

    def red(o, a, op=OP.add):
        add("V", lambda: g.vector.tensor_reduce(real(o), real(a), AxisListType.X, op), [o], [a], vwork(a, a, 1))

    def scan(o, a, b, ini, op0, op1):
        add("V", lambda: g.vector.tensor_tensor_scan(real(o), real(a), real(b), real(ini), op0, op1), [o], [a, b, ini], vwork(o, a, short(o, a, b)))

    def act(o, a, f=AF.Copy, bias=None, scale=None):
        kw = {}
        if bias is not None:
            kw["bias"] = bias
        if scale is not None:
            kw["scale"] = scale
        w = vwork(o, a, 1, 65) if "ind" in (o[0], a[0]) else (0, 0, 64 + width(o), 0, 0, 0, 0, 0)
        add("A", lambda: g.scalar.activation(real(o), real(a), f, **{k: real(v) for k, v in kw.items()}), [o], [a] + list(kw.values()), w)

    def lin(o, a, scale=None, bias=None, nm=None):
        if nm not in CFG["onV"]:
            act(o, a, AF.Identity, bias, scale)
        elif scale is None and bias is None:
            cp(o, a)
        elif scale is None or bias is None:
            ts(o, a, bias if scale is None else scale, OP.add if scale is None else OP.mult)
        else:
            ts(o, a, scale, OP.mult, bias, OP.add)

    def iota(o, pat, base=0, cm=0, small=True):
        w = (130, 0, 2 * width(o), 0, 0, 0, 0, 0)
        if small:
            add("G", lambda: g.iota(real(o), pat, base, cm, allow_small_or_imprecise_dtypes=True), [o], [], w)
        else:
            add("G", lambda: g.iota(real(o), pat, base, cm), [o], [], w)

    def select(o, i, pat, op, base, cm):
        add("G", lambda: g.affine_select(real(o), real(i), pat, op, 0.0, base, cm), [o], [i], (170, 0, 2 * width(o), 0, 0, 0, 0, 0))

    def gcopy(o, i):
        select(o, i, [[0, width(o)]], OP.is_ge, 0, 0)

    def zeros(name, c0, c1, step=512):
        for c in range(c0, c1, step):
            iota(A(name, c, min(c + step, c1)), [[0, min(c + step, c1) - c]])

    def mm(terms, start=True, stop=True):
        def fn():
            for k, (o, l, r) in enumerate(terms):
                ins = g.tensor.matmul(real(o), real(l), real(r), start and k == 0, stop and k == len(terms) - 1)
            return ins
        c = sum(max(64, width(r)) * (4 if DTYPE[l[1]] == F32 else 1) for _, l, r in terms)
        add("P", fn, [t[0] for t in terms], [t[1] for t in terms] + [t[2] for t in terms], (0, 0, 0, 0, 0, c, 0, 0))

    def wrap(out, band, name, c0=0, c1=L):
        return [(out, A(band, 15 - r, 143 - r), A(name, c0 + r, c1, 16)) for r in range(16)]

    nd = [0]

    def dma(q, o, i, nbytes=0, after=None, **kw):
        sem = "d%d" % nd[0]; nd[0] += 1
        add(q, lambda: Q[q].dma_start(real(o), real(i), **kw), [o], [i] + ([o] if kw else []),
            (CFG["gdma"] if q == "G" else 100, 0, 0, 0, 0, 0, 1, nbytes), sem, 16, after)
        return ops[-1]

    def rows(name, r, c1, c0=0):
        return A(name, c0, c1, p0=r, ps=16)

    col = lambda k: A("col", k, k + 1)
    C_W, C_P, C_WR, C_A, C_TH, C_T0, C_HS, C_R16, C_C, C_N, C_G, C_Q, C_X, C_K, C_Y = range(15)
    R_HI, R_LO, R_CNT, R_NEXT, R_RUN = 4, 12, 7, 8, 10
    pcol, rcol, kcol = A("pF", 0, 1), A("pF", 1, 2), A("pF", 3, 4)
    e = lambda k: A("OH", k, k + 1)
    row = lambda k, a=0, b=16, st=1: A("row", 16 * k + a, 16 * k + b, st)
    W = lambda nm, k=0, n=1: A(nm, 16 * k, 16 * (k + n))
    H = lambda nm, k=0, n=1: A(nm, L * k, L * (k + n))
    Wh = lambda nm, h, k=0: A(nm, 16 * k + CW * h, 16 * k + CW * h + CW)
    Hh = lambda nm, h, k=0: A(nm, L * k + HL * h, L * k + HL * h + HL)
    CUMw = A("CUM", 16, 16 + VV)

    def weights(c, pairs):
        for k, (r, w) in enumerate(pairs):
            lin(col(c), e(r), float(w), col(c) if k else None)

    def spread(z, c0):
        for n in (256, 512)[:1 + ("4" in "".join(CFG["st1"] + CFG["st2"]))]:
            gcopy(A(z, c0 + n, c0 + 2 * n), A(z, c0, c0 + n))

    dma("S", A("tsb"), ("raw", T.ts[:]), 131072)
    xload = dma("A", A("X", 0, V), ("raw", T.xr[:]), 1 << 20)
    for _, h in halves:
        dma("S", A("Z0", 512 * h, 512 * h + HL), ("raw", T.zq[:, HL * h:HL * h + HL]), 32768)
    dma("S", A("kI", 0, 1), ("raw", T.kap[:]))
    dma("S", A("tI", 0, 1, p1=8), ("raw", T.th[:]))
    iota(A("pI", 0, 1), [[0, 1]], 0, 1, False)
    iota(A("C256"), [[1, L]])
    iota(A("PA"), [[0, 16], [1, 16]])
    iota(A("PB"), [[1, 16], [0, 16]])
    iota(A("PM", 0, HL), [[1, 16], [0, CW]])
    ms(A("CUM", 0, 2064), 0.0)
    ms(A("CUM", 2064, V + 16), 0.0)
    zeros("CUM", V + 16, VV + 16)
    cp(pcol, A("pI", 0, 1))
    ts(A("pI", 1, 2), A("pI", 0, 1), 15, OP.bitwise_and)
    cp(rcol, A("pI", 1, 2))
    ts(A("OH"), A("C256", 0, 16), rcol, OP.is_equal)
    ts(A("t1"), A("PA"), -2.0, OP.add, e(14), OP.mult)
    lin(A("t2"), A("PB"), e(0))
    ts(A("ID"), A("C256", 0, 128), pcol, OP.is_equal)
    mm([(H("PN0"), A("ID"), A("t1")), (H("PN0"), A("ID"), A("t2"))])
    act(A("PI"), H("PN0"))
    iota(A("one"), [[0, 272]], 1)
    select(A("t5"), A("one", 0, 128), [[-16, 8], [0, 16]], OP.is_ge, 0, 1)
    select(A("BO"), A("t5"), [[16, 8], [0, 16]], OP.is_ge, 15, -1)
    iota(A("ZB"), [[0, 144]])
    gcopy(A("ZB", 15, 143, 16), A("BO", 0, 128, 16))
    act(A("BO32"), A("BO"))
    lin(A("IN64"), A("ID"), -64.0)
    act(A("I32"), A("ID"))
    cp(A("tsu"), A("tsb"))
    cp(A("tsf"), A("tsb"))
    lin(A("tsh"), A("tsf"), 1.0 / 64, UP - 63.0 / 128)
    mm([(H("PS1"), A("I32"), A("tsf")), (H("PS1"), A("IN64"), A("tsh"))])
    lin(H("tsd"), A("tsh"), 2.0 ** -16, -UP * 2.0 ** -16)
    lin(H("tsd", 1), H("PS1"), 2.0 ** -16, 64 * UP * 2.0 ** -16)
    dma("S", rows("CUM", R_HI, 16 + V, 16), H("tsd"), 65536)
    dma("S", rows("CUM", R_LO, 16 + V, 16), H("tsd", 1), 65536)
    iota(row(0, 0, 16, 2), [[1, 8]], 1)
    iota(row(0, 1, 16, 2), [[-1, 8]], 7)
    iota(row(0, 15, 16), [[0, 1]], 1)
    cp(kcol, A("kI", 0, 1))
    tt(row(1), row(0), A("OH"), OP.mult)
    lin(W("kD", 2), A("OH"), kcol)
    red(col(C_W), row(1))
    mm([(W("PH1"), A("BO32"), W("kD", 2))])
    lin(A("ZU"), A("ZB"), col(C_W))
    lin(col(C_A), pcol, 0.0, -0.375)
    act(A("kR"), W("PH1"))
    for nm, w in (("Z16", 16), ("Z32", 32), ("ZM16", -16), ("Z256", 256), ("Z512", 512), ("ZM256", -256)):
        lin(A(nm), A("ZB"), float(w))
    lin(A("IN"), A("ID"), -1.0)
    iota(A("t5"), [[0, 128]])
    for nm, w in (("IH", 0.5), ("IBIG", 8192.0), ("I64", 64.0), ("I272", 272.0)):
        add("G", lambda nm=nm, w=w: g.affine_select(real(A(nm)), real(A("t5")), [[-1, 128]], OP.not_equal, w, 0, 1), [A(nm)], [A("t5")],
            (170, 0, 256, 0, 0, 0, 0, 0))
    if not CFG["zw2"]:
        lin(A("I288"), A("ID"), 288.0)
    iota(A("m128"), [[0, L]], -128)
    iota(A("zero"), [[0, VV // 16]])
    for k in range(RO):
        dma("S", rows("FL", k, V + L), A("zero", 0, (V + L) // 16), 139264)
        if 0 < k < RO - 1:
            dma("S", rows("DD", k, VV), A("zero"), 163840)
    iota(A("G8", p1=8), [[0, 128]], 1)
    select(A("G8", p1=8), A("G8", p1=8), [[1, 8], [0, 16]], OP.is_equal, 0, -1)
    cp(A("thF", 0, 1, p1=8), A("tI", 0, 1, p1=8))
    mm([(A("PH1", 0, 1), A("G8", p1=8), A("thF", 0, 1, p1=8))])
    lin(col(C_TH), A("PH1", 0, 1), 256.0, 256.0)
    lin(col(C_T0), col(C_TH), None, 256.0 * L)
    if CFG["g1v"] or CFG["tbv"]:
        ts(A("MSK"), A("PA"), rcol, OP.is_equal)
        lin(A("MS4"), A("MSK"), 0.4)
        act(A("KEEP"), A("PA"), AF.Sign)
    if not CFG["g1v"]:
        act(A("kB"), A("kR"))
        lin(W("kD"), A("kR"), e(1))
        lin(col(C_K), e(1), -1.0, e(0))
        lin(W("kD", 1), A("kB"), col(C_K))
        tt(A("KT"), W("kD"), W("kD", 1), OP.add)
    weights(C_P, ((14, 32), (0, 1), (13, 16), (6, -64), (15, -1)))
    weights(C_C, ((0, -1), (1, -1), (2, -1)))
    weights(C_N, ((R_HI, 1 << 22), (R_LO, 1 << 16)))
    weights(C_G, ((R_HI, 1), (R_LO, 1)))
    weights(C_Q, ((R_NEXT, 272 << 17), (R_CNT, -272)))
    weights(C_Y, ((R_RUN, 8192), (R_CNT, -1)))
    lin(A("ZY"), A("ZB"), col(C_Y))
    if CFG["pe2"]:
        cp(A("IDh"), A("ID"))
        for k in range(0, 15, 3):
            iota(A("KI", 128 * k, 128 * k + 384), [[1, 3], [0, 128]], k + 1)
            select(A("KI", 128 * k, 128 * k + 384), A("KI", 128 * k, 128 * k + 384), [[0, 3], [-1, 128]], OP.is_equal, 0, 1)
    lin(A("ZC"), A("ZB"), col(C_C))
    lin(A("ZN"), A("ZB"), col(C_N))
    lin(A("ZQ"), A("ZB"), col(C_Q))
    lin(A("IDG"), A("ID"), col(C_G))
    select(A("SH"), A("BO"), [[1, 128]], OP.is_equal, -1, -1)
    ms(row(4), RATIO ** -8)
    ms(row(5), 1.0 / RATIO)
    ms(row(6), 1e29)
    scan(row(7), row(4), row(6), RATIO ** 68, OP.mult, OP.min)
    scan(row(8), row(5), row(6), RATIO ** 8, OP.mult, OP.min)
    tt(row(9), row(8), A("OH"), OP.mult)
    tt(row(10), row(7), row(7), OP.mult)
    red(col(C_WR), row(9))
    lin(A("wW"), row(10), col(C_WR))
    for k, w in enumerate((V, V, V + L, V, V, V + 2 * L, V + L - 272)):
        iota(W("ro", k), [[16, 16]], w)
    iota(W("ro", 7), [[0, NH], [16, CW]])
    ts(A("DM"), A("ro"), rcol, OP.add)
    select(A("TRI"), A("BO"), [[1, 128]], OP.is_gt, 0, -1)
    iota(H("PU", 0, 3), [[0, 3 * L]], 32)
    for k, (r, pat, base) in enumerate(((14, [[1, 3], [0, L]], 46), (0, [[0, 48], [1, 16]], 32), (13, [[0, 3], [1, 16], [0, 16]], 32))):
        o = A("XTb", L * 3 * k, L * (3 + 3 * k), p1=8)
        iota(o, pat, base)
        dma("S", rows("PU", r, 3 * L), o, 24576)
    zeros("MV", 0, RO * L)
    iota(A("PK", p1=8), [[0, L]], MARK)
    for k in range(RO):
        dma("S", rows("MV", k, L * k + L, L * k), A("PK", p1=8), 8192)
    select(A("TI"), A("BO"), [[1, 128]], OP.is_ge, 0, -1)
    select(A("TX"), A("BO"), [[-1, 128]], OP.is_gt, 0, 1)
    iota(A("P1", 0, 16), [[0, 16]])
    for c in range(0, V, 512) if CFG["bys"] or CFG["byn"] else ():
        iota(A("NUM", c, c + 512), [[1, 512]], c)
    if not CFG["bys"]:
        lin(A("BW"), A("BO"), col(C_W))
    if not CFG["byn"]:
        lin(A("BN"), A("BO"), col(C_N))
    iota(A("zerb"), [[0, 272]])
    dma("S", rows("MK", R_RUN, V + L), A("zerb"), 69632)
    iota(A("c16"), [[0, L]], 16)
    lin(col(C_R16), rcol, None, -16.0)
    iota(A("t1", 0, 48), [[0, 48]], L)
    dma("S", rows("CUM", 0, 16 + VV, 16 + V + L), A("t1", 0, 48), 12288)

    def reorder(dst, srcw, lst, bias=None):
        n = CFG["reo"]
        for c in range(0, V, n):
            lin(A(dst, c, c + n), IND(srcw, A(lst, c // 16, (c + n) // 16)), None, bias, nm=lst + str(c // n))

    def stage(x, h, win, off, ref, modes, key, w):
        c, k, turn, blocks = 0, 0, 0, modes.split()
        for q, block in enumerate(blocks):
            c0 = c
            for mode, n in zip(block[::2], [L * int(d) for d in block[1::2]]):
                sub[0] = x + str(k)
                o, ab, df = A(off, c // 16, (c + n) // 16), A("AB", c, c + n), A("DF", c, c + n)
                if mode == "A":
                    ga, pb = A("GA", 512 * turn, 512 * turn + n), A("PS%d" % turn, 0, n)
                    turn = 1 - turn
                    act(ga, IND(win, o))
                    mm([(pb, A("ID"), ga), (pb, A("IN"), ref(h, n))])
                    act(ab, pb, AF.Abs)
                else:
                    tt(df, IND(win, o), ref(h, n), OP.subtract)
                    if mode == "r":
                        ts(ab, df, 0.0, OP.max)
                    else:
                        act(ab, df, AF.Abs)
                c, k = c + n, k + 1
            n = (c - c0) // 16
            out = A("PK%d" % (q % 2), 0, n)
            first = [(out, A("ID"), A("PM" if w == 16 else "C256", c0 // 16, c // 16))]
            if mode == "r":
                mm(first + wrap(out, "ZM%d" % w, "DF", c0, c), True, False)
                mm(wrap(out, "Z%d" % (2 * w), "AB", c0, c), False, True)
            else:
                mm(first + wrap(out, "Z%d" % w, "AB", c0, c))
            if q == 0:
                lin(A("K1"), out, nm="K1")
            elif n > 16:
                tt(A("K1", 0, n), out, A("K1", 0, n), OP.min)
        sub[0] = x
        tt(A("K3", 0, 32), A("K1", 0, 32), A("K1", 32, 64), OP.min)
        if n > 16:
            tt(W(key), A("K3", 0, 16), A("K3", 16, 32), OP.min)
        else:
            tt(A("K3", 32, 48), A("K3", 0, 16), A("K3", 16, 32), OP.min)
            tt(W(key), out, A("K3", 32, 48), OP.min)
        ts(W(key, 1), W(key), w - 1, OP.bitwise_and)

    def lowest(x, key, n, dm, bank, more):
        o = 0
        for h in range(4):
            terms = []
            for c in range(4 * h, 4 * h + 4):
                w = L - 16 * c
                ts(A("E", o, o + w), A("kU" + x, 16 * c, L), A("K" + x, key + c, key + c + 1), OP.is_equal, A("wh", c, c + 1), OP.mult)
                terms.append((A("PN1", 16 * c, L), A("BO"), A("E", o, o + w)))
                o += w
            glue(4)
            mm(terms, h == 0, h == 3)
        if CFG["tbv" if x == "s" else "tbn"]:
            tt(A("TB" + x), H("PN1"), A("MS4"), OP.mult)
            scan(A("TS"), A("KEEP"), A("TB" + x), 0.0, OP.mult, OP.add)
            tt(A("lo" + x), A("TS", 15, L, 16), A("wh"), OP.is_ge)
        else:
            lin(A("TB" + x), H("PN1"), 1.0 / 40, nm="TB" + x)
            mm(wrap(W("PN1"), "ZB", "TB" + x))
            tt(A("lo" + x), W("PN1"), A("wh"), OP.is_ge)
        mm([(W(bank, 0, n), A("I32"), W("K" + x, 0, n))] + more, True, False)
        mm([(W(bank, k), A("IBIG"), A("lo" + x)) for k in range(n)], False, True)
        tt(W("oF" + x, 0, n), W(bank, 0, n), dm, OP.min)
        cp(W("oU" + x, 0, n), W("oF" + x, 0, n))

    def mates(r, x):
        return [s for s in range(N) if s != r and (s * B // HL == r * B // HL) == (x == "a")]

    def engines_for(sender, dst, x):
        sc = T.cores[sender]
        fr = [r for r in mates(sender, x) if topo.chip(T.cores[r]) != topo.chip(sc)]
        nr = [r for r in mates(sender, x) if r not in fr]
        used = topo.engines(sc, T.cores[fr[0]]) if fr else []
        pool, lst = (used, fr) if dst in fr else ([k for k in topo.engines(sc, T.cores[dst]) if k not in used], nr)
        n = 1
        while 2 * n * max(len(lst), len(fr)) <= len(pool):
            n *= 2
        k = lst.index(dst)
        return pool[k * n:(k + 1) * n]

    def send(rho, x):
        s, z, peers = "S%d" % rho, "Z%d" % (rho + 1), mates(rank, x)
        spot = lambda r: r * B if rho == RO - 1 else 512 * (r * B // HL) + r * B % HL

        def fn():
            trs = []
            for r in peers:
                rid, pid, _ = topo.addr(T.cores[r])
                trs.append(RemoteDMATransfer(dst_ids=[DstId(rid=rid, pnc=pid)], dma_engine_mask=sum(1 << k for k in engines_for(rank, r, x)),
                                             remote_sem=T.sem["arr%s%d" % (x, rho)], src=T[s][:, r * B:r * B + B],
                                             dst=T[z][:, spot(rank):spot(rank) + B]))
            g.remote_dma_fused(trs, local_sem=T.sem["snt%s%d" % (x, rho)])
            return None
        add("G", fn, [], [A(s, r * B, r * B + B) for r in peers], (1000, 0, 0, 0, 0, 0, 0, 0), "snt%s%d" % (x, rho),
            sum(len(engines_for(rank, r, x)) for r in peers))
        add("R", None, [A(z, spot(r), spot(r) + B) for r in peers], [], (0, 0, 0, 0, 0, 0, 2, 0), "arr%s%d" % (x, rho),
            sum(len(engines_for(r, rank, x)) for r in peers), ops[-1])
        if x == "a":
            gcopy(A(z, spot(rank), spot(rank) + B), A(s, rank * B, rank * B + B))

    xt, xt2 = "XTa", "XTb"
    for rho in range(RO):
        z, last_round = "Z%d" % rho, rho == RO - 1
        by_place = rho == 0 or last_round
        Xw, XTw = A("X", 0, V), A(xt, 0, V)
        zh = lambda h, n=HL: A(z, 512 * h, 512 * h + n)
        xs = lambda h, n=HL: A("XR", XS * h + HL, XS * h + HL + n)
        kv = 1 if rho == 0 else 2
        mid = 2047.0 if CFG["pe2"] else 0.0
        lap[0] = rho
        for (x, h), bank in zip(halves, CFG["bank"]):
            tag[0], sub[0] = "u", x
            mm(wrap(A(bank, 0, CW), "ZU", z, 512 * h, 512 * h + HL))
            spread(z, 512 * h)
            if "sq" in CFG["onV"]:
                cp(Wh("uF", h), A(bank, 0, CW))
                tt(Wh("sq", h), A(bank, 0, CW), Wh("uF", h), OP.mult)
            else:
                act(Wh("sq", h), A(bank, 0, CW), AF.Square)
                cp(Wh("uF", h), A(bank, 0, CW))
            ts(Wh("uI", h), Wh("sq", h), 1.0 / 32, OP.mult, col(C_A), OP.add)
            cp(Wh("bF", h), Wh("uI", h))
            for c in range(CW * h, CW * h + CW):
                ts(A("hI", HL * h + c % CW, HL * h + HL, CW), A("kR"), A("uF", c, c + 1), OP.mult, A("bF", c, c + 1), OP.add)
                if c % 4 == 3:
                    glue(4)
            for c0, c1 in zip([0] + CFG["cut"], CFG["cut"] + [HL]):
                ts(A("hI", L + HL * h + c0, L + HL * h + c1), A("hI", HL * h + c0, HL * h + c1), V - 1, OP.bitwise_and)
                cp(A("off", HL * h + c0, HL * h + c1), A("hI", L + HL * h + c0, L + HL * h + c1))
        sub[0] = ""
        if rho == 0:
            tag[0] = "src0"
            mm(wrap(H("PN1"), "ZN", "CUM", 16, 16 + V))
            cp(A("src"), H("PN1"))
            tag[0] = "pos0"
            for k in range(16):
                if k in CFG["posA"]:
                    lin(H("PU", 3), A("PI"), None, 32.0 + k)
                    act(IND(A("POS", 0, V), W("tsu", k)), H("PU", 3), AF.Silu)
                else:
                    ts(IND(A("POS", 0, V), W("tsu", k)), A("PI"), 1.0, OP.mult, 32.0 + k, OP.add)
            tag[0] = "reo0"
            reorder(xt, Xw, "src", UP)
            for c in (0, V // 2):
                dma("G", A(xt, c, c + V // 2, p0=R_HI, ps=8), A("CUM", 16 + c, 16 + c + V // 2, p0=R_HI, ps=8), 131072,
                    accum_op=OP.add, max_dma_last_dim=8192)
        for x, h in halves:
            tag[0] = "st1" if rho else "st10"
            stage(x, h, Xw, "off", zh, CFG["st1"][rho], "k1", 256)
        for (x, h), bank in zip(halves, CFG["bank"]):
            tag[0], sub[0] = "s", x
            p8 = lambda k=0: A(bank, CW * k, CW * k + CW)
            cp(Wh("mU", h), Wh("k1", h, 1))
            tt(A("g1f"), IND(H("hI", 1), A("mU")), A("MSK"), OP.mult)
            scan(A("g1s"), A("KEEP"), A("g1f"), 0.0, OP.mult, OP.add)
            cp(A("sU"), A("g1s", 15, L, 16))
            lin(A("XR", XS * h, XS * h + HL), IND(A("POS", 0, V), Wh("sU", h)), col(C_P), nm="g2")
            lin(xs(h), IND(Xw, Wh("sU", h)), None, UP, nm="xs")
            mm(wrap(A(bank, 0, 2 * CW), "ZU", "XR", XS * h, XS * h + 2 * HL))
            spread("XR", XS * h + HL)
            cp(Wh("vU", h), p8())
            lin(Wh("Ks", h, kv), p8(), nm="vF")
            cp(Wh("dI", h), p8(1))
            lin(Hh("g3", h), IND(CUMw, Wh("vU", h)), nm="g3")
            ts(Wh("dI", h, 1), Wh("dI", h), 15, OP.bitwise_and)
            ts(Wh("nd", h), Wh("dI", h, 1), -1.0, OP.mult, -1.0, OP.add)
            if rho > 0:
                lin(W("w1"), W("Ks", kv), None, -1.0 - mid)
                mm(wrap(p8(), "ZC", "g3", HL * h, HL * h + HL))
                tt(A("pm"), p8(), W("w1"), OP.add)
                lin(W("Ks", 1), A("pm"), None, 1.0 + mid, nm="pl")
            else:
                ts(Wh("pm", h), Wh("Ks", h, 1), -1.0 - mid, OP.add)
            if CFG["pe2"]:
                for pb, k0, n in ((bank, 0, 4), ("PK1", 4, 4), ("PK0", 8, 8)):
                    mm([(W(pb, k), A("KI", 128 * k - 128, 128 * k), A("nd")) for k in range(max(k0, 1), k0 + n)], True, False)
                    mm([(W(pb, k), A("IDh"), A("pm")) for k in range(k0, k0 + n)], False, True)
                    ts(W("of2", k0, n), W(pb, k0, n), mid, OP.add)
            for c in range(CW * h, CW * h + CW) if not CFG["pe2"] else ():
                ts(A("of2", HL * h + c % CW, HL * h + HL, CW), A("C256", 0, 16), A("nd", c, c + 1), OP.mult, A("pm", c, c + 1), OP.add)
                if c % 4 == 3:
                    glue(4)
            tag[0] = "hit"
            ts(Wh("hit", h), Wh("k1", h), col(C_TH), OP.is_lt, float(HL), OP.mult)
            tt(Wh("w1", h, 1), Wh("hit", h), Wh("DM", h, 7), OP.add)
            cp(Wh("hU", h), Wh("w1", h, 1))
        sub[0] = ""
        if not last_round:
            tag[0] = "cnt"
            dma("S", A("CUM", 16 + V + L * rho, 16 + V + L * rho + L, p0=R_HI, ps=8), A("g3", p0=R_HI, ps=8), 8192)
            mm([(W("PN0"), A("BO"), A("hit"))])
            red(col(C_HS), W("PN0"))
            lin(col(C_A), col(C_HS), -1.0 / HL, L - 0.375)
            lin(col(C_TH), col(C_HS), -256.0 / HL, col(C_T0))
        tag[0] = "vals"
        mm([(Hh("PN0", h, k), A(m), r) for _, h in halves for k, m, r in ((0, "ID", zh(h)), (0, "IN", xs(h)), (1, "IH", zh(h)), (1, "IH", xs(h)))])
        lin(A("vs"), H("PN0", 1), None, 128.0 - UP / 2 - 0.25)
        ts(A("cc"), H("PN0"), -2.0 - UP, OP.max, 2.0 - UP, OP.min)
        mm([(H("PN0"), A("ID"), A("vs")), (H("PN0"), A("IDG"), A("g3"))])
        lin(A(xt, V, V + L), H("PN0"), None, UP - 128.0, nm="app")
        tag[0] = "lows"
        tt(A("wh"), A("wW"), A("hit"), OP.mult)
        lin(W("Ks"), A("g1s", 15, L, 16), nm="sF")
        if CFG["bys"]:
            cp(A("kUs"), IND(A("NUM"), A("sU")))
        else:
            mm([(H("PN1"), A("BW"), H("XR"))])
            cp(A("kUs"), H("PN1"))
        ns = 2 if by_place else 3
        lowest("s", 0 if CFG["bys"] else 16 * kv, ns, W("DM", 3 if rho == 2 else 0, ns), "PH1", [])
        tag[0] = "xs"
        tt(IND(A("X"), W("oUs")), A("vs"), A("m128"), OP.add)
        tag[0] = "fold"
        E = (V + L) // 16
        act(IND(A("FL"), W("oUs", 1)), H("MV", rho), AF.Silu)
        FC = A("FB" if CFG["gfold"] else "FC")
        dma("G" if CFG["gfold"] else "S", FC, rows("FL", rho, V + L), 69632 if CFG["gfold"] else 139264)
        scan(A("FS"), FC, FC, 0.0, OP.add, OP.max)
        scan(A("R1"), A("one", 0, E), FC, 0.0, OP.add, OP.min)
        mm([(A("PH1", 0, 1), A("TRI"), A("FS", E - 1, E)), (A("PH1", 1, 2), A("SH"), A("R1", E - 1, E))])
        ts(A("FO"), A("FS"), A("PH1", 0, 1), OP.add, 1.0 / MARK, OP.mult)
        scan(A("R2"), A("one", 0, E), FC, A("PH1", 1, 2), OP.add, OP.min)
        dma("S", rows("CUM", R_CNT, 16 + V + L, 16), A("FO"), 69632)
        dma("S", rows("CUM", R_RUN, 16 + V + L, 16), A("R2"), 69632)
        dma("S", rows("CUM", R_NEXT, 15 + V + L, 15), A("R2"), 69632)
        if rho == 0:
            dma("S", rows("CUM", 0, 16 + V + L, 16), A("FO"), 69632)
        if not last_round:
            tag[0] = "posw"
            act(IND(A("POS"), W("oUs")), H("PU", rho), AF.Silu)
        else:
            tag[0] = "fin"
            dma("S", A("PU", 0, 272), rows(xt, R_HI, V + L), 139264)
            dma("S", A("PU", 272, 544), rows(xt, R_LO, V + L), 139264)
            lin(A("yr"), A("PU", 0, 544), nm="yr")
            o = A(CFG["bank"][0], 0, 272)
            mm([(o, A("I64"), A("PU", 0, 272)), (o, A("IN64"), A("yr", 0, 272)), (o, A("I32"), A("PU", 272, 544)), (o, A("IN"), A("yr", 272, 544))])
            lin(A("DC", 0, 272), o, 2.0 ** 16, nm="yo")
            dma("S", rows(xt2, 0, V + L), A("DC", 0, 272), 139264)
        for x, h in halves:
            tag[0] = "st2"
            stage(x, h, XTw, "of2", xs, CFG["st2"][rho], "k2", 16)
            tag[0] = "n"
            tt(Wh("w1", h, 2), Wh("k2", h, 1), Wh("nd", h), OP.mult)
            tt(Wh("aF", h), Wh("w1", h, 2), Wh("pm", h), OP.add)
            ts(Wh("aU", h), Wh("aF", h), mid, OP.add)
            lin(Hh("rr", h), IND(XTw, Wh("aU", h)), nm="rr")
            o0, o1, zw = A("PN0", 0, HL), A("PN0", HL, 2 * HL), A("zw", 2 * HL * h, 2 * HL * h + 2 * HL)
            if CFG["zw2"]:
                o1 = H("PH0")
                mm([(o0, A("ID"), zh(h))], True, False)
                mm([(o1, A("IH"), zh(h))], True, False)
                mm([(o0, A("IN"), Hh("rr", h))], False, True)
                mm([(o1, A("IH"), Hh("rr", h))], False, True)
                lin(H("zw"), o0, None, 2 * UP)
                ts(H("zw", 1), o1, UP / 2 - 0.25, OP.add)
            else:
                mm([(o0, A("ID"), zh(h)), (o0, A("I288"), A("one", 0, HL)), (o1, A("IH"), zh(h))], True, False)
                mm([(o0, A("IN"), Hh("rr", h)), (o1, A("IH"), Hh("rr", h))], False, True)
                lin(zw, A("PN0", 0, 2 * HL), None, UP / 2 - 0.25, nm="zw")
            act(Hh("S%d" % rho, h), IND(zw, Wh("hU", h)), AF.Abs, -UP)
            send(rho, x)
        sub[0] = ""
        tag[0] = "lown"
        lin(A("g6"), IND(CUMw, A("aU")), nm="g6")
        tag[0] = "mark"
        lin(A("g4"), IND(CUMw, W("oUs", 1)), nm="g4")
        mm([(W("PH1"), A("I272"), W("oFs", 1))], True, False)
        mm(wrap(W("PH1"), "ZQ", "g4"), False, True)
        ts(A("qI"), W("PH1"), 1.0 / (16 * E), OP.mult, -13.0 / 32, OP.add)
        ts(W("qF"), A("qI"), 1.0 - 16 * E, OP.mult)
        tt(W("qF", 1), W("PH1"), W("qF"), OP.add)
        tt(W("qF", 2), W("qF", 1), W("DM", 6), OP.min)
        ts(A("qU"), W("qF", 2), float(E), OP.add)
        cp(IND(A("MK"), A("qU")), A("g4"))
        dma("S", A("P1", 16, 16 + E), rows("MK", R_RUN, 16 * E), 69632)
        n = CFG["mk"]
        for c in range(0, L, n):
            o = A("PH1", 0, n)
            mm([(o, A("TI"), A("P1", 16 + c, 16 + c + n)), (o, A("TX"), A("P1", 15 + c, 15 + c + n))])
            scan(A("sF", c, c + n), o, A("c16", 0, n), A("sF", c - 1, c) if c else col(C_R16), OP.add, OP.add)
            cp(A("srn", c, c + n), A("sF", c, c + n))
        if not last_round:
            dma("S", rows("MK", R_RUN, 16 * E), A("zerb"), 69632)
        tag[0] = "dd"
        if not by_place:
            act(IND(A("DD"), W("oUs", 2)), H("MV", rho), AF.Silu)
            DC = A("DB" if CFG["gdd"] else "DC")
            dma("G" if CFG["gdd"] else "S", DC, rows("DD", rho, VV), 81920 if CFG["gdd"] else 163840)
            scan(A("DS"), DC, DC, 0.0, OP.add, OP.max)
            mm([(A("PH1", 0, 1), A("TRI"), A("DS", VV // 16 - 1, VV // 16))])
            ts(A("DO"), A("DS"), A("PH1", 0, 1), OP.add, 1.0 / MARK, OP.mult)
            dma("S", rows("CUM", rho, 16 + VV, 16), A("DO"), 81920)
        tag[0] = "lown"
        tt(A("fr"), IND(XTw, A("aU")), A("rr"), OP.subtract)
        mm([(H("PN0"), A("ID"), A("rr")), (H("PN0"), A("ID"), A("cc"))])
        ts(A("vn"), H("PN0"), 0.0, OP.max, 63.0, OP.min)
        if CFG["byn"]:
            cp(A("kUn"), IND(A("NUM"), A("aU")))
        else:
            mm([(H("PN1"), A("BN"), A("fr"))])
            cp(A("kUn"), H("PN1"))
        mm(wrap(W("PK0"), "ZN", "fr"))
        lin(W("Kn"), W("PK0"), nm="nF")
        act(W("Kn", 1), A("aF"), AF.Relu, mid)
        if not last_round:
            mm([(H("PN0"), A("ID"), A("fr")), (H("PN0"), A("ID"), A("vn"))])
            lin(A("val"), H("PN0"), None, UP, nm="val")
        mm([(W("PS0"), A("I32"), W("Kn", 1))] + wrap(W("PS0"), "ZY", "g6"))
        tt(W("w1", 3), W("PS0"), W("DM", 2), OP.min)
        ts(A("gone"), W("w1", 3), float(V), OP.is_ge)
        lowest("n", 16 if CFG["byn"] else 0, 1, W("DM", 1), "PK1", [(W("PK1"), A("IBIG"), A("gone"))])
        tag[0] = "xw"
        cp(IND(A("X"), W("oUn")), A("vn"))
        tag[0] = "reo"
        if not last_round:
            xt, xt2 = xt2, xt
            reorder(xt, A(xt2, 0, V + L), "srn")
            tag[0] = "xtn"
            tt(W("oFn", 1), A("lon"), W("DM", 2), OP.mult)
            tt(W("oFn", 2), W("oFn", 1), W("w1", 3), OP.max)
            cp(W("oUn", 1), W("oFn", 2))
            cp(IND(A(xt), W("oUn", 1)), A("val"))
        else:
            dma("S", ("raw", T.yx[:]), A("X", 0, V), 1 << 20)
            dma("S", ("raw", T.yz[:]), A("Z4"), 65536)
            for h in range(4):
                (cp if h % 2 else act)(A("POS", 1024 * h, 1024 * h + 1024), IND(A(xt2, 0, V + L), A("srn", 64 * h, 64 * h + 64)))
            dma("S", ("raw", T.yt[:]), rows("POS", 0, V), 131072)

    hist = {}
    for o in ops:
        o["pre"], seen = [], set()
        for kind in ("r", "w"):
            for x in o[kind]:
                for p, k2, y in hist.get(x[0], []):
                    same = p["q"] == o["q"] and p["sem"] is None
                    if not meet(x, y) or (kind == "r" and k2 == "r" and (x[0] not in PS or same)):
                        continue
                    free = same and (o["q"] == "P" or (not CFG["war"] and not (kind == "r" and k2 == "w")))
                    if (p["i"], free) not in seen:
                        seen.add((p["i"], free)); o["pre"].append((p, 0 if free else 1 if same else 2))
        if o["after"]:
            o["pre"].append((o["after"], 0 if o["q"] == "R" else 2))
        for kind in ("r", "w"):
            for x in o[kind]:
                h = hist.setdefault(x[0], [])
                if kind == "w" and x[3] == 1 and x[5] == 1 and x[4] == 0:
                    h[:] = [y for y in h if not (x[1] <= y[2][1] and y[2][2] <= x[2])]
                if not any(y[0] is o and y[1] == kind and y[2] == x for y in h[-3:]):
                    h.append((o, kind, x))
        o["pre"].sort(key=lambda y: (y[0]["i"], y[1]))
    shape = tuple((o["q"], tuple(p["i"] for p, _ in o["pre"])) for o in ops)
    ORDER["ops"] = ops
    if shape not in ORDER:
        ORDER[shape] = arrange([o["q"] for o in ops], [o["work"] for o in ops], [[(p["i"], d) for p, d in o["pre"]] for o in ops],
                               [o["tag"] for o in ops], [o["fine"] for o in ops], [o["lap"] for o in ops])
    count, known = {}, {q: {} for q in Q}
    for o in [ops[i] for i in ORDER[shape]]:
        q = o["q"]
        sem = o["sem"] or "e" + q
        count[sem] = count.get(sem, 0) + o["cnt"]
        o["tok"] = (sem, count[sem])
        if q == "R":
            o["kn"] = {}
            continue
        kn, want = known[q], {}
        need = [p for p, d in o["pre"] if d]
        for p in need:
            s, c = p["tok"]
            if kn.get(s, 0) < c:
                want[s] = max(want.get(s, 0), c)
        for p in need:
            for s, c in p["kn"].items():
                if want.get(s, 0) and want[s] <= c:
                    want[s] = 0
        for s, c in want.items():
            if c:
                Q[q].wait_ge(T.sem[s], c)
        for p in need:
            for s, c in list(p["kn"].items()) + [p["tok"]]:
                kn[s] = max(kn.get(s, 0), c)
        o["kn"] = dict(kn)
        for fn in o["fn"] if isinstance(o["fn"], list) else [o["fn"]]:
            ins = fn()
            if ins is not None:
                ins.then_inc(T.sem[sem], 1 if isinstance(o["fn"], list) else o["cnt"])
    for s, c in count.items():
        g.wait_ge(T.sem[s], c)
